import numpy as np, ml_dtypes
CORES = [48,51,52,55]
N = 4
BF = ml_dtypes.bfloat16
E, V, L, ST, OF, BL, RO, M = 4096, 768, 256, 16, 5, 4, 3, 8
NONE = E - 1; B = L // BL; KM = 31 * 16 * (63 + M)
def ring(rng, pm, n, dl, dense):
    x = np.repeat(np.arange(n), 8); z = (x + np.tile(dl, n)) % n
    first = (x < dense * n) & (rng.random(8 * n) < 0.97)
    o = rng.permutation(np.argsort(rng.random(8 * n) - first)[:E - 1])
    return pm[x[o]], pm[z[o]]
def fill_rows(rng, a, b):
    h = np.concatenate([a, b]); ids = np.concatenate([np.arange(E - 1), np.arange(E - 1)])
    o = rng.permutation(2 * (E - 1)); h = h[o]; ids = ids[o]
    o = np.argsort(h, kind="stable"); h = h[o]; ids = ids[o]
    place = np.arange(2 * (E - 1)) - np.searchsorted(h, h)
    k = np.argsort(rng.random((V, 16)), axis=1)[h, place]
    out = np.full((16, V), NONE); out[k, h] = ids
    return out
def pack(rng, y, a, b, th):
    en = np.zeros((N, 8, E), np.int32); en[:, :, :E - 1] = 1024 * np.minimum(a, b) + np.maximum(a, b)
    ne = np.stack([np.concatenate([fill_rows(rng, a[r, g], b[r, g]) for g in range(8)]) for r in range(N)]).astype(np.int32)
    return {"y0": y.reshape(N, 128, E).astype(np.float32).astype(BF), "ends0": en, "ne0": ne, "th": np.ascontiguousarray(np.reshape(th, (N, 8, 1))).astype(np.int32)}
def levels(rng):
    return np.clip(rng.integers(0, 64, (N, 8, 1, E)) + rng.integers(-12, 13, (N, 8, 16, E)), 0, 63)
def blank():
    return np.zeros((N, 8, E - 1), np.int64), np.zeros((N, 8, E - 1), np.int64)
def numbers(rng, at, forced):
    num = np.full(E - 1, -1); num[at] = forced
    num[num < 0] = rng.permutation(np.setdiff1d(np.arange(E - 1), forced))
    return num
def setup_inputs(rng):
    a, b = blank()
    for g in range(8):
        pm = rng.permutation(V)
        for r in range(N): a[r, g], b[r, g] = ring(rng, np.roll(pm, rng.integers(0, V)), V, rng.integers(1, 10, 8), 0.2)
    return pack(rng, levels(rng), a, b, rng.integers(300, 1801, (N, 8)))
def setup_inputs_spread(rng):
    a, b = blank()
    for g in range(8):
        pm = rng.permutation(V)
        for r in range(N): a[r, g], b[r, g] = ring(rng, pm, int(rng.integers((E + 6) // 8 + 8, V + 1)), rng.integers(1, int(rng.integers(4, 16)), 8), 0.5 * rng.random())
    y = np.minimum((np.exp2(6 * rng.random((N, 8, 1, E))) * rng.random((N, 8, 16, E))).astype(np.int64), 63)
    return pack(rng, y, a, b, np.minimum(np.exp2(15.2 * rng.random((N, 8))).astype(np.int64) - 1, KM))
def setup_inputs_corners(rng):
    a, b = blank(); sh = int(rng.integers(0, 4)); flat = rng.permutation(8)[:3]
    y = levels(rng); y = np.where(rng.random((N, 8, 1, E)) < 0.4, 63 * rng.integers(0, 2, (N, 8, 1, E)), y)
    th = rng.choice(np.array([0, 1, 16 * M, 640, 1280, KM]), (N, 8))
    for g in range(8):
        pm = rng.permutation(V); one = int(rng.choice(np.array([0, 63, 20])))
        if g == flat[0]: one = 63
        for r in range(N):
            k = (g + r + sh) % 4; n = V; dl = rng.permutation(8) + 1; dense = 0.3
            if k == 0: n = min(V, (E + 6) // 8 + int(rng.choice(np.array([0, 2, 6]))))
            if k == 1: dl = np.array([1, 1, 1, 1, 2, 2, 2, 2])
            if k == 3: dl = np.array([1, 1, 1, 1, 1, 1, 1, 1]); dense = 0.1
            a[r, g], b[r, g] = ring(rng, pm, n, dl, dense)
            if g in flat: y[r, g] = one; th[r, g] = 16 * M * int(rng.integers(0, 12))
    return pack(rng, y, a, b, th)
def setup_inputs_crowd(rng):
    a, b = blank(); sh = int(rng.integers(0, 4)); y = rng.integers(1, 64, (N, 8, 16, E)); th = rng.choice(np.array([0, 1, 300]), (N, 8))
    off = np.arange(E - 1); off = off[(off % ST > 0) & (off % ST != OF)]
    for g in range(8):
        kind = (g + sh) % 4; c0 = np.arange(g % 2, V, 2); c1 = np.arange(1 - g % 2, V, 2)
        tri = rng.permutation(c0[B:])[:3]; lo = int(rng.integers(0, 11)); came = (B, B - 1, 1, 2)[kind] & (B - 1)
        for r in range(N):
            u = rng.permutation(c0[:B]); p = rng.permutation(np.setdiff1d(c0[B:], tri))[:B]; v = rng.permutation(c1[V // 2 - B:])
            o = rng.permutation(c1[:V // 2 - B])
            if g % 2 == 1: o = np.concatenate([np.zeros(1, np.int64), o[o != 0]])
            s = np.array(o[:B]); w = o[B:2 * B]; j = int(rng.integers(1, B))
            if kind == 1: s[j] = s[j - 1]
            if kind >= 2:
                lu, ls = int(u[B - 1]), int(s[B - 1]); u = u[np.arange(B) // 14]; s[:] = s[0]
                if kind == 3: u[j] = lu; s[j] = ls
            k = np.unique(u, return_index=True)[1]; n3 = 2 * B + len(k)
            fa = np.concatenate([u, p, u[k], np.repeat(tri, 8)]); fb = np.concatenate([v, w, s[k], np.repeat(np.roll(tri, -1), 8)])
            cap = 16 - np.bincount(np.concatenate([fa, fb]), minlength=V); cap[v] -= 1; cap[np.unique(s)] -= 1
            more = E - 1 - len(fa)
            ea = np.concatenate([fa, rng.permutation(np.repeat(c0, cap[c0]))[:more]]); eb = np.concatenate([fb, rng.permutation(np.repeat(c1, cap[c1]))[:more]])
            block = ST * (BL * int(rng.integers(0, B)) + np.arange(BL)) + OF
            forced = np.concatenate([ST * BL * np.arange(B), ST * (BL * np.arange(B) + BL - 1), block, rng.permutation(off)[:24 - BL]])
            num = numbers(rng, np.concatenate([np.arange(2 * B), n3 + np.arange(24)]), forced)
            a[r, g][num] = ea; b[r, g][num] = eb
            y[r, g][:, num[2 * B:n3]] = 0
            up = int(rng.integers(8, 51)); y[r, g][:, num[n3:n3 + 24]] = lo; y[r, g][:, block] = lo + up
            if kind == 1 or r % 2 == 1:
                over = 0 if kind == 0 else 1 if r == 1 else int(rng.choice(np.array([0, 1, 8])))
                th[r, g] = 256 * (up + M) + over - 8 * came
    return pack(rng, y, a, b, th)
def setup_inputs_ends(rng):
    a, b = blank(); y = 63 * rng.integers(0, 2, (N, 8, 16, E)); Q = V // 4; R = E - 1 - 18 * Q
    forced = [0, ST, ST * (L - 2), ST * (L - 1)]
    for t in range(1, RO): forced += [OF * t, ST * (L - 1) + OF * t]
    forced = np.array(forced); FO = len(forced)
    th = (np.arange(N)[:, None] + np.arange(8)[None, :] + N + 1) % 2; th[:, :4] = rng.integers(0, 2, (N, 4))
    for g in range(8):
        pm = rng.permutation(np.arange(2, V - 2)); rest = pm[4:].reshape(-1, 4)
        quad = np.concatenate([np.array([[pm[0], V - 2, V - 1, pm[1]], [0, pm[2], 1, pm[3]]]), np.concatenate([np.sort(rest[:, :2], axis=1), rest[:, 2:]], axis=1)])
        u, v, s, w = rng.permutation(quad).T
        calm = (np.arange(Q) // N < FO) | (rng.random(Q) < 0.5)
        for r in range(N):
            home = np.arange(Q) % N == r
            qa = np.stack([u] * 16 + [v] * 2, axis=1).reshape(-1); qb = np.stack([np.where(home, v, w)] + [s] * 8 + [w] * 7 + [s, w], axis=1).reshape(-1)
            ea = np.concatenate([qa, rng.permutation(np.repeat(v[0::2], 13))[:R]]); eb = np.concatenate([qb, rng.permutation(np.repeat(v[1::2], 13))[:R]])
            num = numbers(rng, 18 * np.flatnonzero(home)[:FO], forced)
            a[r, g][num] = ea; b[r, g][num] = eb; yy = y[r, g]
            yy[:, num[(18 * np.flatnonzero(calm)[:, None] + np.arange(18)).reshape(-1)]] = 0
            yy[:, num[18 * np.flatnonzero(calm & home)]] = 63
            yy[:, num[18 * Q:]] = 63 * rng.integers(0, 2, R)[None, :]
    return pack(rng, y, a, b, KM * th)
def setup_inputs_again(rng):
    a, b = blank(); y = levels(rng); th = rng.integers(300, 3001, (N, 8)); sh = int(rng.integers(0, 2)); tr = V // 6; h = (V - 6 * B) // 2
    i = np.arange(L); mid = i[(i % BL > 0) & (i % BL < BL - 1)]; m = len(mid); at = ST * BL * np.arange(B); la = ST * (BL - 1)
    forced = np.concatenate([at, at + la, at + OF, at + la + OF, ST * mid + OF])
    folds = np.array([[15, 1, 1], [13, 2, 2], [11, 4, 4], [9, 6, 6]])
    for g in range(8):
        pm = rng.permutation(V); low = rng.permutation(2 * B); high = V - 2 * B + rng.permutation(2 * B); rest = 2 * B + rng.permutation(V - 4 * B)
        for r in range(N):
            if (g + sh) % 2 == 0:
                u, uu = rng.permutation(low[:B]), rng.permutation(low[B:]); v, vv = rng.permutation(high[:B]), rng.permutation(high[B:])
                s, ss = rng.permutation(rest[:B]), rng.permutation(rest[B:2 * B])
                c0 = np.concatenate([u, vv, ss, rest[2 * B:2 * B + h]]); free = np.concatenate([uu, rest[2 * B + h:]]); moved = np.concatenate([v, s])
                fa = np.concatenate([u, u, vv, ss]); fb = np.concatenate([v, s, uu, uu])
                cap = np.full(V, 16); cap[np.concatenate([v, s, vv, ss])] = 15; cap = cap - np.bincount(np.concatenate([fa, fb]), minlength=V)
                x = rng.permutation(np.repeat(c0, cap[c0])); z = rng.permutation(np.repeat(free, cap[free]))
                z = np.concatenate([z[:m], rng.permutation(np.concatenate([z[m:], np.repeat(moved, cap[moved])]))])
                more = E - 1 - 4 * B; num = numbers(rng, np.arange(4 * B + m), forced)
                a[r, g][num] = np.concatenate([fa, x[:more]]); b[r, g][num] = np.concatenate([fb, z[:more]])
                y[r, g] = rng.integers(16, 64, (16, E))
                y[r, g][:, np.concatenate([num[B:2 * B], num[3 * B:4 * B]])] = rng.integers(0, 12, (16, 2 * B))
                th[r, g] = 0 if r < 2 else int(rng.integers(0, 2))
            else:
                c = folds[rng.integers(0, 4, tr)]; tri = np.take_along_axis(pm[:3 * tr].reshape(tr, 3), np.argsort(rng.random((tr, 3)), axis=1), 1)
                qa = np.concatenate([np.repeat(tri[:, j], c[:, j]) for j in range(3)]); qb = np.concatenate([np.repeat(tri[:, (j + 1) % 3], c[:, j]) for j in range(3)])
                n = V - 3 * tr; o = rng.permutation(8 * n)[:E - 1 - len(qa)]; dl = rng.integers(1, 10, 8); ot = pm[3 * tr:]
                ea = np.concatenate([qa, ot[o // 8]]); eb = np.concatenate([qb, ot[(o // 8 + dl[o % 8]) % n]])
                num = rng.permutation(E - 1)
                a[r, g][num] = ea; b[r, g][num] = eb
    return pack(rng, y, a, b, th)
def check_inputs(d):
    bad = []
    for k, lo, hi in (("y0", 0, 63), ("ends0", 0, 1024 * (V - 2) + V - 1), ("ne0", 0, NONE), ("th", 0, KM)):
        x = np.asarray(d[k]).astype(np.float64)
        if not (np.min(x) >= lo and np.max(x) <= hi): bad.append("range of " + k)
        elif np.any(x != np.floor(x)): bad.append("whole numbers in " + k)
    if bad: return bad
    en = np.asarray(d["ends0"]).astype(np.int64); u = en >> 10; w = en & 1023; ne = np.asarray(d["ne0"]).astype(np.int64).reshape(N, 8, 16, V)
    if np.any(en[:, :, NONE] != 0): bad.append("ends0 of no edge")
    if np.any(u[:, :, :NONE] >= w[:, :, :NONE]) or np.any(w >= V): bad.append("ends of an edge")
    node = np.zeros((16, 1), np.int64) + np.arange(V)[None, :]
    for r in range(N):
        for g in range(8):
            m = ne[r, g] != NONE; e = ne[r, g][m]; c = node[m]; lo = c == u[r, g][e]; hi = c == w[r, g][e]
            if not np.all(lo | hi) or np.any(np.bincount(e[lo], minlength=E)[:NONE] != 1) or np.any(np.bincount(e[hi], minlength=E)[:NONE] != 1):
                bad.append("lists of rank %d, graph %d" % (r, g))
    return bad
def score(yx, nx, ux, wx, u, v, ye):
    a = np.take_along_axis(nx, u[:, None, :], 2); b = np.take_along_axis(nx, v[:, None, :], 2); both = ux + wx
    s = np.where(a == NONE, -1, np.take_along_axis(both, a.reshape(8, -1), 1).reshape(a.shape) - u[:, None, :])
    f = np.where(b == NONE, -2, np.take_along_axis(both, b.reshape(8, -1), 1).reshape(b.shape) - v[:, None, :])
    c = np.max(np.where(s[:, :, None, :] == f[:, None, :, :], b[:, None, :, :], -1), axis=2)
    ya = np.take_along_axis(yx, a.reshape(8, 1, -1), 2).reshape(8, 16, 16, L); yc = np.take_along_axis(yx, np.maximum(c, 0).reshape(8, 1, -1), 2).reshape(8, 16, 16, L)
    gain = np.sum(np.maximum(ye[:, :, None, :] + M - np.maximum(ya, yc), 0), axis=1)
    return np.sum(np.where(c >= 0, gain, 0), axis=1), a, s, c >= 0, np.sum(ya, axis=1)
def reference(y0, ends0, ne0, th):
    y = y0.astype(np.float32).astype(np.int32).reshape(N, 8, 16, E); en = ends0.astype(np.int64); u = en >> 10; w = en & 1023
    ne = np.array(ne0, np.int64).reshape(N, 8, 16, V); thr = th.astype(np.int64)[:, :, 0]; moves = np.zeros((N, 8), np.int64)
    low = np.tril(np.ones((B, B), bool), -1)[None]
    for t in range(RO):
        lane = ST * np.arange(L) + OF * t
        yn, un, wn, nn, mn = np.array(y), np.array(u), np.array(w), np.array(ne), np.array(moves)
        for r in range(N):
            q = (r + 1 + t) % N; lu, lv, ye = u[r][:, lane], w[r][:, lane], y[r][:, :, lane]
            kap, a, s, closed, tot = score(y[r], ne[r], u[r], w[r], lu, lv, ye)
            kap = kap + score(y[q], ne[q], u[q], w[q], lu, lv, ye)[0]
            up = kap >= (thr[r] + 8 * (moves[r] & (B - 1)))[:, None]
            yn[r][:, :, lane] = np.clip(ye + np.where(up, 1, -1)[:, None, :], 0, 63)
            kb = kap.reshape(8, B, BL); at = BL * np.arange(B)[None, :]
            el = at + np.argmin(kb, axis=2); d = lane[at + BL - 1 - np.argmax(kb[:, :, ::-1], axis=2)]; e = lane[el]
            a, s, closed, tot = [np.take_along_axis(x, el[:, None, :], 2) for x in (a, s, closed, tot)]
            v = np.take_along_axis(w[r], e, 1); p1 = np.take_along_axis(u[r], d, 1); p2 = np.take_along_axis(w[r], d, 1)
            ok = (a != NONE) & ~closed & (s != v[:, None, :]); has = np.any(ok, axis=1)
            k = np.argmin(np.where(ok, tot, 10 ** 6), axis=1)[:, None, :]
            s = np.maximum(np.take_along_axis(s, k, 1)[:, 0], 0); a = np.take_along_axis(a, k, 1)[:, 0]
            four = np.stack([s, v, p1, p2], axis=2)
            hit = np.any(four[:, :, None, :, None] == four[:, None, :, None, :], axis=(3, 4))
            clash = np.any(hit & has[:, None, :] & low, axis=2)
            fs = np.take_along_axis(ne[r], s[:, None, :], 2) == NONE; fv = np.take_along_axis(ne[r], v[:, None, :], 2) == NONE
            go = has & ~clash & np.any(fs, axis=1) & np.any(fv, axis=1)
            ks, kv = np.argmax(fs, axis=1), np.argmax(fv, axis=1)
            for g in range(8):
                i = np.flatnonzero(go[g]); dd, ss, vv = d[g, i], s[g, i], v[g, i]
                nn[r, g] = np.where(np.isin(nn[r, g], dd), NONE, nn[r, g])
                nn[r, g][ks[g, i], ss] = dd; nn[r, g][kv[g, i], vv] = dd
                un[r, g, dd] = np.minimum(ss, vv); wn[r, g, dd] = np.maximum(ss, vv)
                yn[r, g][:, dd] = (y[r, g][:, a[g, i]] + y[r, g][:, e[g, i]]) >> 1
                mn[r, g] += len(i)
        y, u, w, ne, moves = yn, un, wn, nn, mn
    return {"y1": y.reshape(N, 128, E).astype(np.float32).astype(BF), "ends1": (1024 * u + w).astype(np.float32), "ne1": ne.reshape(N, 128, V).astype(np.float32)}

@@ -1,0 +1,806 @@
+from concourse.bass import DstId, RemoteDMATransfer, IndirectOffsetOnAxis
+from concourse.mybir import AluOpType, AxisListType, ActivationFunctionType
+
+F, B, I, U = "float32", "bfloat16", "int32", "uint16"
+RO = 3
+KDS = (8, 8)
+SAMEQ = True
+CAP = 1009 * 16384 + 1023
+CY, PECY, WAKE, LOOK, EARLY = 1.04e-3, 0.52e-3, 0.06, 0.3, 12.0
+DELTA = False
+EQA = 2
+SSQ = "v"
+FE = "avavavavavav"
+TILE = "vva"
+
+SB = {
+    "Yb": (4176, B), "EWin": (4096, B), "FG": (12288, B), "ya": (8192, B), "mm": (8192, B), "mz": (8192, B), "rl": (8192, B),
+    "NB": (1152, F), "FC": (1152, F), "nei": (768, I), "neu": (768, U), "neo": (768, F),
+    "eA": (256, I), "eB": (256, I), "Ef": (256, F), "UV": (512, I), "cB": (512, F), "cC": (512, B),
+    "EW": (48, F), "EWi": (48, I), "LUV": (96, I), "lA": (96, F), "lB": (96, F), "CODE": (96, B),
+    "PC0": (96, B), "PC1": (96, B), "PC2": (96, B), "Z0": (256, B), "Z1": (256, B), "Z2": (256, B),
+    "PZ0": (256, B), "PZ1": (256, B), "PZ2": (256, B), "PS0": (256, F), "PS1": (256, F), "PS2": (256, F),
+    "PK0": (256, F), "PK1": (256, F), "PK2": (256, F), "off": (192, U),
+    "PW": (192, F), "pw": (288, F), "pwa": (48, F), "pwb": (48, F), "CB": (192, B),
+    "pi": (4, I), "pq": (8, I), "pf": (16, F), "thi": (4, I), "Acc": (8, F), "ysave": (8, B),
+    "IO": (160, F), "ML": (256, F), "MG": (128, F), "M64": (256, F), "M32": (128, F), "D": (256, F), "R16": (256, F), "R64": (256, F),
+    "CAPS": (128, F), "CE": (256, B), "icol": (256, B), "codeT": (1024, B), "codeX": (768, B), "DDT": (256, F), "DUM": (20, F),
+    "Ib": (128, B), "If": (128, F), "nI": (128, B), "Is": (128, B), "Ik": (128, B), "BLK": (128, B), "BLm4": (128, B), "BL4": (128, B),
+    "BLz": (128, B), "BLT": (128, B), "BLn": (128, B), "TRI": (128, B), "TRT": (128, B), "FST": (128, B), "FS4": (128, B), "ZS": (144, B),
+    "BC": (768, B), "RP": (1152, B), "IW": (160, B), "msk": (16, F), "PT": (1536, B), "cm128": (64, B),
+    "aU": (512, U), "cU": (512, U), "nbh": (512, B), "nbl": (512, B), "fS": (512, B), "sS": (512, B), "acc": (512, F),
+    "vS": (256, B), "pc": (256, B), "pv": (256, B), "CW": (272, F), "sg": (256, B), "r1": (256, B),
+    "km": (256, F), "ks": (256, F), "sm": (416, F), "f2": (52, I), "NM": (36, I), "si": (12, I), "ou": (96, U),
+    "G1": (128, F), "G2": (128, F), "G3": (128, F), "Q": (256, B), "EQ": (4096, B), "GN": (256, F), "GF": (256, F), "dd": (128, F),
+    "emp": (128, B), "ins": (128, B), "t2": (128, F), "nu2": (128, F), "nrem": (256, F), "remK": (256, F),
+    "t1": (128, F), "u1": (128, F), "zg": (64, B), "yh": (64, B), "ys": (64, B), "goB": (8, B), "en": (96, F),
+}
+MATS = ["BLy", "Ib", "nI", "Is", "Ik", "BLK", "BLm4", "BL4", "BLz", "BLT", "BLn", "TRI", "TRT", "FST", "FS4"]
+SCRATCH = {k: ("sbuf", [128, v[0]], v[1]) for k, v in SB.items() if k not in MATS}
+SCRATCH["MT"] = ("sbuf", [128, 128 * len(MATS)], B)
+for _b in range(8):
+    SCRATCH["bank%d" % _b] = ("psum", [128, 512], F)
+NDMA = 24
+SEMAPHORES = ["sv", "sa", "sp", "sg", "lsem"] + ["dm%d" % k for k in range(NDMA)] + ["%s%d" % (a, t) for a in ("qc", "qz", "qk") for t in range(RO)]
+SIZE = {F: 4, B: 2, I: 4, U: 2}
+QSEM = {"v": "sv", "a": "sa", "p": "sp", "g": "sg"}
+
+
+def rank_program(g, core, T, topo):
+    rank = T.rank_of(core)
+    if rank is None:
+        return
+    N = len(T.cores)
+    A = AluOpType
+    AF = ActivationFunctionType
+    ops = []
+    early = [0.0]
+    eng = {"v": g.vector, "a": g.scalar, "p": g.tensor, "g": g, "s": g.sync}
+
+    def V(name, lo=0, hi=None, st=1, p0=0, p1=128, ps=1):
+        if name in MATS:
+            return ("MT", 128 * MATS.index(name), 128 * MATS.index(name) + 128, 1, 0, 128, 1)
+        return (name, lo, SCRATCH[name][1][1] if hi is None else hi, st, p0, p1, ps)
+
+    def col(name, c):
+        return V(name, c, c + 1)
+
+    def ind(w, o):
+        return ("ind", w, o)
+
+    def ap(v):
+        if not isinstance(v, tuple):
+            return v
+        if v[0] == "ind":
+            return ap(v[1]).indirect(ap(v[2]))
+        pp = slice(v[4], v[5], v[6]) if v[6] != 1 else slice(v[4], v[5])
+        cc = slice(v[1], v[2], v[3]) if v[3] != 1 else slice(v[1], v[2])
+        return T[v[0]][pp, cc]
+
+    def add(q, fn, outs, ins, dma=False, ext=None, two=False):
+        rd, wr = [], []
+        for v in ins:
+            if isinstance(v, tuple):
+                rd.extend([v[1], v[2]] if v[0] == "ind" else [v])
+        for v in outs:
+            if isinstance(v, tuple):
+                if v[0] == "ind":
+                    wr.append(v[1])
+                    rd.append(v[2])
+                else:
+                    wr.append(v)
+        full = [v for v in list(outs) + list(ins) if isinstance(v, tuple)]
+        flat = [v for v in full if v[0] != "ind"]
+        n = max([len(range(v[1], v[2], v[3])) for v in flat] + [1])
+        dts = [SCRATCH[v[0]][2] for v in flat if v[2] - v[1] > 1]
+        lat = 0.0
+        if q is None:
+            cost, lat = 0.0, 3.0
+        elif ext == "send":
+            cost = 0.3
+        elif dma:
+            cost, lat = (1.7 if q == "g" else 0.1), 2.0 + n * len(range(*flat[0][4:7])) * SIZE[SCRATCH[flat[0][0]][2]] / 100e3
+        elif q == "p":
+            cost, lat = PECY * max(64, outs[0][2] - outs[0][1]) * (4 if F in dts[1:] else 1), 0.1
+        elif q == "g":
+            cost = 0.13 + 2 * CY * n
+        elif outs[0][0] == "ind":
+            cost = 0.05 + 3.8 * CY * n
+        elif ins and ins[0][0] == "ind":
+            cost = 0.05 + 1.56 * CY * n
+        elif two and all(SCRATCH[v[0]][0] == "sbuf" for v in ins):
+            cost = 0.05 + CY * max(64, 2 * n)
+        elif q == "v" and not two and all(d in (B, U) for d in dts):
+            cost = 0.05 + CY * max(64, n / 2)
+        else:
+            cost = 0.05 + CY * max(64, n)
+        ops.append({"q": q, "fn": fn, "rd": rd, "wr": wr, "dma": dma, "ext": ext, "cost": cost, "lat": lat, "early": early[0]})
+
+    def ts(o, x, s1, s2, op0, op1=None):
+        if op1 is None:
+            add("v", lambda: g.vector.tensor_scalar(ap(o), ap(x), ap(s1), None, op0), [o], [x, s1])
+        else:
+            add("v", lambda: g.vector.tensor_scalar(ap(o), ap(x), ap(s1), ap(s2), op0, op1), [o], [x, s1, s2])
+
+    def tt(o, x, y, op):
+        add("v", lambda: g.vector.tensor_tensor(ap(o), ap(x), ap(y), op), [o], [x, y], two=True)
+
+    def cp(o, x):
+        add("v", lambda: g.vector.tensor_copy(ap(o), ap(x)), [o], [x])
+
+    def ms(o, c):
+        add("v", lambda: g.vector.memset(ap(o), c), [o], [])
+
+    def scan(o, x, y, op0, op1):
+        add("v", lambda: g.vector.tensor_tensor_scan(ap(o), ap(x), ap(y), 0.0, op0, op1), [o], [x, y])
+
+    def act(o, x, func=AF.Identity, bias=0.0, scale=1.0):
+        add("a", lambda: g.scalar.activation(ap(o), ap(x), func, bias=ap(bias), scale=ap(scale)), [o], [x, bias, scale])
+
+    def mmul(o, l, r, start, stop, behind=None):
+        add("p", lambda: g.tensor.matmul(ap(o), ap(l), ap(r), start, stop), [o], [l, r, behind])
+
+    def iota(o, pat, base=0, cm=0):
+        if SCRATCH[o[0]][2] == I:
+            add("g", lambda: g.iota(ap(o), pat, base, cm), [o], [])
+        else:
+            add("g", lambda: g.iota(ap(o), pat, base, cm, allow_small_or_imprecise_dtypes=True), [o], [])
+
+    def dma(q, o, x):
+        add(q, lambda: eng[q].dma_start(ap(o), ap(x)), [o], [x], dma=True)
+
+    sent = [0]
+
+    def send(items, nq):
+        trs = []
+        for k, (r, s, d, sem) in enumerate(items):
+            dst = T.cores[r]
+            m = 0
+            for e in topo.engines(core, dst)[k * nq:(k + 1) * nq]:
+                m += 1 << e
+            rid, pid = topo.addr(dst)[:2]
+            trs.append(RemoteDMATransfer(dst_ids=[DstId(rid=rid, pnc=pid)], dma_engine_mask=m, remote_sem=T.sem[sem], src=ap(s), dst=ap(d)))
+        sent[0] += nq * len(items)
+        add("g", lambda: g.remote_dma_fused(trs, local_sem=T.sem.lsem), [], [it[1] for it in items], ext="send")
+
+    def arrive(v, sem, n):
+        add(None, None, [v], [], ext=(sem, n))
+
+    bank = ["bank%d" % k for k in range(8)]
+    Ywin = V("Yb", 16, 4112)
+    TAB = 1152
+    lf, gf, pff, m1, c0, m0, c1, l64, kb, zc, thb, bT = [col("pf", k) for k in range(12)]
+
+    dma("s", V("eA"), T.ends0[:])
+    for c in range(4):
+        dma("a", V("eB", 64 * c, 64 * c + 64), T.ends0[:, 1024 * c:1024 * c + 1024])
+    dma("a", V("nei"), T.ne0[:])
+    iota(col("pi", 0), [[0, 1]], 0, 1)
+    iota(V("IO"), [[1, 160]])
+    iota(V("ML"), [[0, 16], [1, 16]])
+    iota(V("MG"), [[1, 8], [0, 16]])
+    early[0] = 60.0
+    iota(V("pwa"), [[5, 3], [16, 4], [1024, 4]])
+    iota(V("pwb"), [[0, 3], [16, 16]])
+    iota(V("M64"), [[0, 4], [1, 64]])
+    iota(V("M32"), [[0, 4], [1, 32]])
+    iota(V("DUM", 0, 16), [[0, 2], [16, 8]], 1024)
+    iota(V("DUM", 16, 20), [[16, 4]], 4096)
+    early[0] = 0.0
+    iota(V("codeX", 0, 128), [[-2, 128]], 512)
+    iota(V("codeX", 128, 640), [[-1, 512]], 256)
+    iota(V("codeX", 640, 768), [[-2, 128]], -256)
+    early[0] = EARLY
+    for n in range(4):
+        ms(V("EWin", 1024 * n, 1024 * n + 1024), 0.0)
+    early[0] = 0.0
+    ts(col("pq", 0), col("pi", 0), 15, None, A.bitwise_and)
+    ts(col("pq", 1), col("pi", 0), 4, None, A.logical_shift_right)
+    ts(col("pq", 3), col("pi", 0), 4, 1, A.logical_shift_right, A.bitwise_and)
+    cp(col("pq", 2), col("pi", 0))
+    cp(V("pf", 0, 4), V("pq", 0, 4))
+    add("g", lambda: g.indirect_dma_start(ap(col("thi", 0)), None, T.th[:], IndirectOffsetOnAxis(ap=ap(col("pq", 1)), axis=0), bounds_check=7),
+        [col("thi", 0)], [col("pq", 1)], dma=True)
+    ts(V("BLK"), V("MG"), gf, None, A.is_equal)
+    ts(V("D"), V("ML"), lf, None, A.is_equal)
+    ts(V("Ib"), V("IO", 0, 128), pff, None, A.is_equal)
+    ts(V("UV", 0, 256), V("eA"), 10, None, A.logical_shift_right)
+    ts(V("UV", 256, 512), V("eA"), 1023, None, A.bitwise_and)
+    ts(V(bank[2]), V("UV"), 128.0, 640.0, A.max, A.min)
+    ts(V("cB"), V("UV"), 2.0, -384.0, A.mult, A.add)
+    early[0] = 2 * EARLY
+    tt(V("cC"), V("cB"), V(bank[2]), A.subtract)
+    early[0] = 0.0
+    dma("s", V("EWin", 0, 4096, 1, 0, 128, 16), V("cC", 0, 256))
+    dma("s", V("EWin", 0, 4096, 1, 1, 128, 16), V("cC", 256, 512))
+    dma("s", Ywin, T.y0[:])
+    cp(V("Ef"), V("eB"))
+    cp(V("neu"), V("nei"))
+    for t in range(RO):
+        for i in range(4):
+            act(V("EW", 16 * t + 4 * i, 16 * t + 4 * i + 4), V("Ef", 16 * i + 5 * t, 256, 64))
+    ts(zc, gf, 16.0, 15.0, A.mult, A.add)
+    ts(V("ZS"), V("IO", 0, 144), zc, None, A.is_equal)
+    cp(V("EWi"), V("EW"))
+    ts(V("LUV", 0, 48), V("EWi"), 10, None, A.logical_shift_right)
+    ts(V("LUV", 48, 96), V("EWi"), 1023, None, A.bitwise_and)
+    ts(V("lA"), V("LUV"), 128.0, 640.0, A.max, A.min)
+    ts(V("lB"), V("LUV"), 2.0, -384.0, A.mult, A.add)
+    early[0] = 1.5 * EARLY
+    tt(V("CODE"), V("lB"), V("lA"), A.subtract)
+    early[0] = 0.0
+    send([((rank + 1 + t) % N, V("CODE"), V("PC%d" % t), "qc%d" % t) for t in range(RO)], 4)
+    for t in range(RO):
+        arrive(V("PC%d" % t), "qc%d" % t, 4)
+    ms(col("EWin", 4095), 768.0)
+    for t in range(RO):
+        for i in range(4):
+            act(V("Z%d" % t, 64 * i, 64 * i + 64), V("Yb", 16 + 16 * i + 5 * t, 4112, 64), bias=8.0)
+    act(col("ysave", 0), col("Yb", 4111))
+    send([((rank + 1 + t) % N, V("Z%d" % t), V("PZ%d" % t), "qz%d" % t) for t in range(RO)], 4)
+    for t in range(RO):
+        arrive(V("PZ%d" % t), "qz%d" % t, 4)
+    iota(V("codeT"), [[1, 1024]], -512)
+    iota(V("icol"), [[1, 4], [0, 64]])
+    iota(V("DDT"), [[-16, 4], [-1024, 4], [-64, 16]], 4095)
+    early[0] = EARLY
+    act(V("nI"), V("Ib"), scale=-1.0)
+    early[0] = 0.0
+
+    def fe_gather(q, ch):
+        o, x = V("FG", 1024 * ch, 1024 * ch + 1024), ind(V("EWin"), V("neu", 64 * ch, 64 * ch + 64))
+        if q == "a":
+            act(o, x)
+        else:
+            cp(o, x)
+
+    def fe_sum(ch):
+        o = V(bank[ch // 8], 64 * (ch % 8), 64 * (ch % 8) + 64)
+        mmul(o, V("Ib"), V("codeX", 64 * ch, 64 * ch + 64), True, False)
+        for k in range(16):
+            mmul(o, V("ZS", 15 - k, 143 - k), V("FG", 1024 * ch + k, 1024 * ch + 1024, 16), False, k == 15)
+
+    for ch in range(12):
+        fe_gather(FE[ch], ch)
+    for ch in range(12):
+        fe_sum(ch)
+    def rsum(o, x):
+        add("v", lambda: g.vector.tensor_reduce(ap(o), ap(x), AxisListType.X, A.add), [o], [x])
+
+    ts(V("IW"), V("IO"), -16.0, pff, A.add, A.is_equal)
+    for n in range(3):
+        rsum(col("msk", n), V("D", 5 * n, 5 * n + 5))
+        early[0] = EARLY
+        for pc in range(3):
+            d = 16 - 5 * pc + 5 * n
+            act(V("RP", 128 * (3 * n + pc), 128 * (3 * n + pc) + 128), V("IW", d, d + 128), scale=col("msk", n))
+        early[0] = 0.0
+    for jj in range(5):
+        rsum(col("msk", 3 + jj), V("D", jj, 15, 5))
+        mk = col("msk", 3 + jj)
+        if DELTA and jj > 0:
+            mk = col("msk", 8 + jj)
+            act(mk, col("msk", 2 + jj), bias=col("msk", 3 + jj), scale=-1.0)
+        early[0] = EARLY
+        act(V("BC", 128 * jj, 128 * jj + 128), V("BLK"), scale=mk)
+        early[0] = 0.0
+    early[0] = EARLY
+    act(V("BC", 640, 768), V("BLK"), scale=col("D", 15))
+    for x, c in (("NB", 1.0), ("FC", 1024.0)):
+        ms(V(x, 1, 256, 2), c)
+        ms(V(x, 769, 1024, 2), c)
+        ms(V(x, 1024, TAB), c)
+    early[0] = 0.0
+    SEG = [(0, 128, 0, 256, 2), (128, 640, 256, 768, 1), (640, 768, 768, 1024, 2)]
+    for (x0, x1, a0, a1, st) in SEG:
+        ts(V("NB", a0, a1, st), V("nei", x0, x1), -1.0, 4095.0, A.mult, A.add)
+    ms(V("Yb", 0, 16), 128.0)
+    ms(V("Yb", 4111, 4176), 128.0)
+
+    for t in range(RO):
+        for n, (x, o) in enumerate((("PC%d" % t, 0), ("CODE", 0), ("PC%d" % t, 48), ("CODE", 48))):
+            act(V("CB", 64 * t + 16 * n, 64 * t + 16 * n + 16), V(x, o + 16 * t, o + 16 * t + 16))
+    ts(V("off", 0, 64), V("CB", 0, 64), 512.0, None, A.add)
+    ts(V("off", 64, 192), V("CB", 64, 192), 512.0, None, A.add)
+    ts(V("FC", 0, 256, 2), V(bank[0], 0, 128), 1024.0, None, A.min)
+    ts(V("FC", 256, 640), V(bank[0], 128, 512), 1024.0, None, A.min)
+    ts(V("FC", 640, 768), V(bank[1], 0, 128), 1024.0, None, A.min)
+    ts(V("FC", 768, 1024, 2), V(bank[1], 128, 256), 1024.0, None, A.min)
+
+    def late_consts_v():
+        act(m0, m1, bias=1.0, scale=-1.0)
+        act(c0, m1, scale=256.0)
+        act(c1, m1, bias=256.0, scale=-256.0)
+        act(l64, lf, scale=65536.0)
+        act(kb, lf, bias=512.0, scale=1024.0)
+        ts(bT, col("thi", 0), -4.0, 0.5, A.mult, A.add)
+        act(thb, bT, bias=2048.0)
+        act(col("Acc", 0), lf, scale=0.0)
+        act(V("cm128"), V("IO", 0, 64), bias=-128.0, scale=0.0)
+        act(V("CW", 256, 272), V("IO", 0, 16), bias=float(1 << 24), scale=0.0)
+        act(V("DUM"), V("DUM"), bias=lf)
+        act(V("pw", 0, 48), V("pwa"), bias=l64, scale=1024.0)
+        act(V("pw", 144, 192), V("pwb"), bias=lf)
+        act(V("pw", 48, 96), V("pw", 144, 192), bias=512.0, scale=1024.0)
+        act(V("pw", 96, 144), V("CODE", 0, 48), bias=512.0 * 1025, scale=1024.0)
+        act(V("pw", 192, 240), V("CODE", 48, 96))
+        act(V("pw", 240, 288), V("CODE", 48, 96))
+        tt(V("pw", 0, 144), V("pw", 0, 144), V("pw", 144, 288), A.add)
+        act(V("PW"), V("ML", 0, 192), scale=0.0)
+        for t in range(RO):
+            for o, x in ((0, 48), (32, 96), (48, 0)):
+                act(V("PW", 64 * t + o, 64 * t + o + 16), V("pw", x + 16 * t, x + 16 * t + 16))
+        ts(V("km", 0, 128), V("ML", 0, 128), lf, None, A.is_gt)
+        tt(V("TRI"), V("km", 0, 128), V("BLK"), A.mult)
+        tt(V("FST"), V("Ib"), V("TRI"), A.subtract)
+        act(V("R16"), V("ML"), AF.Sign)
+        act(V("R64"), V("M64"), AF.Sign)
+        act(V("CAPS"), V("M32"), AF.Relu, bias=float(CAP), scale=-float(CAP))
+        act(V("M64"), V("M64"), AF.Sign, bias=31.5, scale=-1.0)
+        act(V("CE"), V("M64"), AF.Relu, scale=8192.0)
+
+    def early_consts_a():
+        act(V("BLm4"), V("BLK"), scale=-4.0)
+        act(V("BL4"), V("BLK"), scale=4.0)
+        act(V("BLz"), V("BLK"), scale=4.0 * KDS[0])
+        act(V("BLy"), V("BLK"), scale=4.0 * KDS[1])
+        act(V("If"), V("Ib"))
+        act(V("Is"), V("Ib"), scale=-2.0 ** -27)
+        act(V("Ik"), V("Ib"), scale=1024.0)
+
+    def late_consts_a():
+        act(V("BLT"), V("BLK"), scale=8192.0)
+        act(V("BLn"), V("BLK"), scale=-8192.0)
+        act(V("TRT"), V("TRI"), scale=8192.0)
+        act(V("FS4"), V("FST"), scale=4096.0)
+
+    early_consts_a()
+
+    tm_, mx_, eq_, sel, f1 = 80, 160, 224, 288, 352
+    qw = lambda a, b, st=1: V("en", a, b, st)
+    has, go, ngo, gE = V("en", 16, 20), V("en", 20, 24), V("en", 24, 28), V("en", 28, 32)
+    oC, oH, oD, oA, oE, oQ, oS = [V("ou", a, b) for a, b in ((0, 8), (8, 24), (28, 36), (36, 40), (40, 44), (44, 60), (64, 84))]
+
+    def book_keeping(t):
+        if t < RO - 1:
+            mmul(V(bank[4], 0, 2), V("BLK"), V("goB", 0, 2), True, False)
+            mmul(V(bank[4], 0, 2), V("BLK"), V("goB", 2, 4), False, True)
+            act(col("Acc", 1), col(bank[4], 0), bias=col("Acc", 0))
+            act(col("Acc", 0), col(bank[4], 1), bias=col("Acc", 1))
+            act(col("Acc", 2), col("Acc", 0), AF.Sign, bias=-63.5)
+            act(col("Acc", 3), col("Acc", 0), AF.Sign, bias=-127.5)
+            act(col("Acc", 4), col("Acc", 0), bias=thb, scale=-32.0)
+            act(col("Acc", 5), col("Acc", 2), bias=col("Acc", 4), scale=1024.0)
+            act(bT, col("Acc", 3), bias=col("Acc", 5), scale=1024.0)
+        ts(V("en", 32, 40), qw(0, 8), -256.0, 256.0, A.max, A.min)
+        act(ngo, go, scale=-1.0)
+        tt(V("en", 40, 48), qw(0, 8), V("en", 32, 40), A.add)
+        tt(V("en", 48, 52), V("en", 40, 48, 2), V("en", 41, 48, 2), A.min)
+        tt(V("en", 52, 56), V("en", 40, 48, 2), V("en", 41, 48, 2), A.max)
+        act(V("en", 56, 60), V("en", 48, 52), bias=393600.0, scale=512.0)
+        act(V("en", 60, 64), V("en", 52, 56), scale=0.5)
+        tt(V("en", 32, 36), V("en", 56, 60), V("en", 60, 64), A.add)
+        tt(gE, V("en", 32, 36), go, A.mult)
+        for c in range(4):
+            act(V("en", 80 + c, 96, 4), V("sm", eq_ + 32 + c, eq_ + 48, 4), bias=1.0, scale=col("en", 24 + c))
+        for c in range(4):
+            act(V("en", 64 + c, 80, 4), V("sm", eq_ + 32 + c, eq_ + 48, 4), scale=col("en", 28 + c))
+
+    def book_keeping2(t):
+        tt(V("en", 80, 96), V("en", 80, 96), V("EW", 16 * t, 16 * t + 16), A.mult)
+        tt(V("en", 80, 96), V("en", 80, 96), V("en", 64, 80), A.add)
+        for i in range(4):
+            act(V("Ef", 16 * i + 5 * t, 256, 64), V("en", 80 + 4 * i, 84 + 4 * i))
+
+    def ya_gather(h, q, n=1):
+        c = 256 * h + 64 * q
+        act(V("ya", 16 * c, 16 * (c + 64 * n)), ind(Ywin, V("aU", c, c + 64 * n)))
+
+    def yc_gather(h, q, n=1):
+        c = 256 * h + 64 * q
+        tt(V("mm", 16 * c, 16 * (c + 64 * n)), ind(V("Yb", 0, 4112), V("cU", c, c + 64 * n)), V("ya", 16 * c, 16 * (c + 64 * n)), A.max)
+
+    rot = [0]
+
+    for t in range(RO):
+        last = t == RO - 1
+        oU, oV = V("off", 64 * t, 64 * t + 32), V("off", 64 * t + 32, 64 * t + 64)
+        z = [V("PZ%d" % t), V("Z%d" % t)]
+        act(V("nbh"), ind(V("NB"), oV))
+        ts(V("aU"), ind(V("NB"), oU), -1.0, 4095.0, A.mult, A.add)
+        tt(V("nbl"), ind(V("NB"), oV), V("nbh"), A.subtract)
+        act(V("fS"), ind(V("FC"), oV), scale=-8192.0)
+        if SSQ == "v":
+            ts(V("sS"), ind(V("FC"), oU), -8192.0, None, A.mult)
+        else:
+            act(V("sS"), ind(V("FC"), oU), scale=-8192.0)
+        ya_gather(0, 0)
+        if t == 0:
+            early[0] = -10.0
+            late_consts_v()
+            early[0] = 0.0
+        else:
+            book_keeping(t - 1)
+        for n in range(3):
+            b = V(bank[5 + n])
+            for pc, x in enumerate(("nbh", "nbl", "fS")):
+                mmul(b, V("RP", 128 * (3 * n + pc), 128 * (3 * n + pc) + 128), V(x), pc == 0, pc == 2)
+            if TILE[n] == "v":
+                cp(V("PT", 512 * n, 512 * n + 512), b)
+            else:
+                act(V("PT", 512 * n, 512 * n + 512), b)
+        for j in range(16):
+            b = V(bank[(0, 1, 2, 5, 6, 7)[j % 6]])
+            if DELTA and j > 0:
+                jj, n = divmod(j - 1, 3)
+                b, w = V(bank[n]), V(bank[5 + (j + 1) % 3])
+                if jj == 0:
+                    mmul(b, V("nI"), V("sS"), True, False)
+                mmul(b, V("BC", 128 * jj, 128 * jj + 128), V("PT", 512 * n, 512 * n + 512), False, jj == 4)
+                act(w, b, AF.Abs)
+                tt(V("acc"), w, V("acc"), A.min)
+                continue
+            if DELTA:
+                b = V(bank[4])
+            if j == 0:
+                bc = V("BC", 640, 768)
+                mmul(b, bc, V("nbh"), True, False)
+                mmul(b, bc, V("nbl"), False, False)
+                mmul(b, bc, V("fS"), False, False)
+                mmul(b, V("nI"), V("sS"), False, True)
+            else:
+                n, jj = divmod(j - 1, 5)
+                mmul(b, V("nI"), V("sS"), True, False)
+                mmul(b, V("BC", 128 * jj, 128 * jj + 128), V("PT", 512 * n, 512 * n + 512), False, True)
+            if j == 0:
+                act(V("acc"), b, AF.Abs)
+            else:
+                act(b, b, AF.Abs)
+                tt(V("acc"), b, V("acc"), A.min)
+        ts(V("cU"), V("acc"), -1.0, 4111.0, A.mult, A.add)
+        mmul(V(bank[3], 0, 256), V("Ib"), z[0], True, True, V("cU", 0, 2))
+        mmul(V(bank[3], 256, 512), V("Ib"), z[1], True, True)
+        if t > 0:
+            book_keeping2(t - 1)
+        KD = KDS[1]
+
+        def relu_part(h, sub):
+            c = 256 * h + 128 * sub
+            KA = list(range(KDS[h], 16))
+            for k0 in range(0, len(KA), 4):
+                ks = KA[k0:k0 + 4]
+                bn = bank[rot[0] % 3]
+                rot[0] += 1
+                for n, k in enumerate(ks):
+                    o = V(bn, 128 * n, 128 * n + 128)
+                    mmul(o, V("Ib"), V(z[h][0], 128 * sub, 128 * sub + 128), True, False)
+                    mmul(o, V("nI"), V("mm", 16 * c + k, 16 * (c + 128), 16), False, True)
+                r0 = 4096 * h + 2048 * sub + 128 * k0
+                act(V("rl", r0, r0 + 128 * len(ks)), V(bn, 0, 128 * len(ks)), AF.Relu)
+
+        def relu_sum(h, sub, stop):
+            for n in range(16 - KDS[h]):
+                r0 = 4096 * h + 2048 * sub + 128 * n
+                mmul(V(bank[4 + h], 128 * sub, 128 * sub + 128), V("BL4"), V("rl", r0, r0 + 128), False, stop and n == 15 - KDS[h])
+
+        def min_part(h):
+            for k in range(KDS[h]):
+                o = V("mz", 4096 * h + 256 * k, 4096 * h + 256 * k + 256)
+                tt(o, V(bank[3], 256 * h, 256 * h + 256), V("mm", 4096 * h + k, 4096 * h + 4096, 16), A.min)
+
+        def min_sum(h, k0, k1):
+            for k in range(k0, k1):
+                mmul(V(bank[4 + h], 0, 256), V("BLm4"), V("mz", 4096 * h + 256 * k, 4096 * h + 256 * k + 256), False, False)
+
+        ya_gather(0, 1)
+        yc_gather(0, 0)
+        ya_gather(0, 2)
+        yc_gather(0, 1)
+        ya_gather(0, 3)
+        mmul(V(bank[4], 0, 256), V("BLz"), z[0], True, False)
+        yc_gather(0, 2)
+        relu_part(0, 0)
+        ya_gather(1, 0)
+        yc_gather(0, 3)
+        relu_sum(0, 0, False)
+        relu_part(0, 1)
+        min_part(0)
+        min_sum(0, 0, KDS[0])
+        relu_sum(0, 1, True)
+        ya_gather(1, 1)
+        act(V("PS%d" % t), V(bank[4], 0, 256))
+        send([((rank - 1 - t) % N, V("PS%d" % t), V("PK%d" % t), "qk%d" % t)], 8)
+        arrive(V("PK%d" % t), "qk%d" % t, 8)
+        yc_gather(1, 0)
+        ya_gather(1, 2)
+        yc_gather(1, 1)
+        ya_gather(1, 3)
+        mmul(V(bank[5], 0, 256), V("BLy"), z[1], True, False)
+        mmul(V(bank[5], 0, 256), V("Ib"), V("icol"), False, False)
+        yc_gather(1, 2)
+        relu_part(1, 0)
+        act(V("vS"), ind(V("codeT"), V("off", 64 * t + 48, 64 * t + 64)), scale=-8192.0)
+        act(V("pc"), V("acc", 256, 512), AF.Relu, bias=4096.0, scale=-1.0)
+        yc_gather(1, 3)
+        mmul(V(bank[7], 0, 256), V("Ib"), V("sS", 256, 512), True, False)
+        mmul(V(bank[7], 0, 256), V("nI"), V("vS"), False, True)
+        for k in range(16):
+            mmul(V(bank[6], 0, 256), V("ZS", 15 - k, 143 - k), V("ya", 4096 + k, 8192, 16), k == 0, False)
+        mmul(V(bank[6], 0, 256), V("Is"), V("sS", 256, 512), False, False)
+        mmul(V(bank[6], 0, 256), V("Ik"), V("pc"), False, False)
+        relu_sum(1, 0, False)
+        mmul(V(bank[5], 0, 256), V("If"), V("PK%d" % t), False, False)
+        act(V(bank[7], 0, 256), V(bank[7], 0, 256), AF.Abs)
+        relu_part(1, 1)
+        min_part(1)
+        min_sum(1, 0, KD - 2)
+        relu_sum(1, 1, False)
+        act(V("pv"), V(bank[7], 0, 256), AF.Relu, bias=4096.0, scale=-1.0)
+        min_sum(1, KD - 2, KD - 1)
+        mmul(V(bank[5], 0, 256), V("BLm4"), V("mz", 4096 + 256 * (KD - 1), 4096 + 256 * KD), False, True)
+        mmul(V(bank[6], 0, 256), V("Ik"), V("pv"), False, True)
+        act(V("CW", 0, 256), V(bank[6], 0, 256), bias=kb, scale=16384.0)
+        if t == 0:
+            late_consts_a()
+        tt(V("km"), V(bank[5], 0, 256), V("D"), A.mult)
+        act(V("sg"), V(bank[5], 0, 256), AF.Sign, bias=bT)
+        scan(V("ks"), V("R16"), V("km"), A.mult, A.add)
+        kw = V("ks", 15, 256, 16)
+        cp(V("sm", 0, 16), kw)
+        cp(V("sm", 16, 32), kw)
+        ts(V("sm", 32, 48), kw, -1.0, None, A.mult)
+        act(V("sm", 48, 64), kw, scale=-1.0)
+        act(V("sm", 64, 80), kw, scale=-1.0)
+        mmul(V(bank[0], 0, 256), V("Ib"), z[1], True, False)
+        mmul(V(bank[0], 0, 256), V("Ib"), V("sg"), False, True)
+        mmul(V(bank[7], 0, 256), V("Ib"), V("CE"), True, False)
+        act(V("r1"), V(bank[0], 0, 256), AF.Relu, bias=71.0, scale=-1.0)
+        for i in range(4):
+            act(V("Yb", 16 + 16 * i + 5 * t, 4112, 64), V("r1", 64 * i, 64 * i + 64), AF.Relu, bias=63.0, scale=-1.0)
+        if last:
+            act(col("Yb", 4111), col("ysave", 0))
+        tt(V("sm", tm_, tm_ + 76), V("sm", 0, 76), V("sm", 4, 80), A.min)
+        tt(V("sm", mx_, mx_ + 64), V("sm", tm_, tm_ + 64), V("sm", tm_ + 8, tm_ + 72), A.min)
+        tt(V("sm", eq_, eq_ + 64), V("sm", 0, 64), V("sm", mx_, mx_ + 64), A.is_equal)
+        tt(V("sm", sel, sel + 64), V("sm", eq_, eq_ + 64), V("PW", 64 * t, 64 * t + 64), A.mult)
+        tt(V("sm", f1, f1 + 56), V("sm", sel, sel + 56), V("sm", sel + 8, sel + 64), A.add)
+        tt(V("f2"), V("sm", f1, f1 + 52), V("sm", f1 + 4, f1 + 56), A.add)
+        ecol, kk, xi, k1, e16 = V("NM", 32, 36), V("NM", 28, 32), V("si", 0, 4), V("si", 4, 8), V("si", 8, 12)
+        ts(ecol, V("f2", 0, 4), 10, None, A.logical_shift_right)
+        ts(V("ou", 0, 8, 2), ecol, m0, c0, A.mult, A.add)
+        ts(V("ou", 1, 8, 2), ecol, m1, c1, A.mult, A.add)
+        act(V("G1"), ind(V("CW"), oC))
+        ts(V("NM", 1, 8, 2), V("f2", 0, 4), 1023, None, A.bitwise_and)
+        ts(V("NM", 8, 16, 2), V("f2", 32, 36), 10, None, A.logical_shift_right)
+        ts(V("NM", 9, 16, 2), V("f2", 32, 36), 1023, None, A.bitwise_and)
+        add("v", lambda: g.vector.transpose(ap(V("G2")), ap(V("G1"))), [V("G2")], [V("G1")])
+        ts(V("NM", 20, 28, 2), V("f2", 48, 52), 1023, None, A.bitwise_and)
+        ts(V("NM", 21, 28, 2), V("f2", 48, 52), 1023, None, A.bitwise_and)
+        ts(V("NM", 16, 20), V("f2", 48, 52), 10, None, A.logical_shift_right)
+        ts(e16, V("f2", 0, 4), 6, 4080, A.logical_shift_right, A.bitwise_and)
+        scan(V("G3"), V("CAPS"), V("G2"), A.max, A.min)
+        cp(V("ou", 45, 60, 4), V("NM", 1, 8, 2))
+        cp(xi, V("G3", 31, 128, 32))
+        cp(V("ou", 46, 60, 4), V("NM", 8, 16, 2))
+        ts(V("NM", 0, 8, 2), xi, 1023, None, A.bitwise_and)
+        cp(V("ou", 47, 60, 4), V("NM", 9, 16, 2))
+        cp(V("ou", 44, 60, 4), V("NM", 0, 8, 2))
+        act(has, V("G3", 31, 128, 32), AF.Relu, bias=1009.0 * 16384, scale=-1.0)
+        act(V("Q"), ind(V("codeT"), oQ))
+        ts(k1, xi, 10, 15, A.logical_shift_right, A.bitwise_and)
+        tt(kk, k1, e16, A.add)
+        cp(V("ou", 8, 44), V("NM"))
+        act(V("GN"), ind(V("NB"), oH))
+        ts(qw(0, 16), V("NM", 0, 16), -512.0, None, A.add)
+        act(V("emp"), V("GN", 0, 128), AF.Relu, bias=1.0, scale=-1.0)
+        act(V("dd"), ind(V("DDT"), oD), bias=-5.0 * t)
+        mmul(V(bank[1], 0, 128), V("FST"), V("emp"), True, True)
+        mmul(V(bank[2], 0, 128), V("FS4"), V("emp"), True, False)
+        mmul(V(bank[2], 0, 128), V("If"), V("dd"), False, True)
+        act(V("ins"), V(bank[1], 0, 128), AF.Relu)
+        act(V("t2"), V(bank[2], 0, 128), AF.Relu, bias=-4096.0)
+        if not last:
+            act(V("GF"), ind(V("FC"), oH))
+            mmul(V(bank[1], 128, 256), V("FS4"), V("emp"), True, False)
+            for n in range(8):
+                x = 64 * (n // 2) + 16 * (1 - n % 2)
+                mmul(V(bank[1], 128 + 16 * n, 144 + 16 * n), V("nI"), V("Q", x, x + 16), False, n == 7)
+            act(V("nu2"), V(bank[1], 128, 256), AF.Relu, bias=-3072.0)
+        n = 0
+        if EQA:
+            act(col("en", 39), col("en", 19), scale=-1.0)
+        for c in (3, 2, 1, 0):
+            for sl in (2 * c, 2 * c + 1, 8 + 2 * c, 9 + 2 * c):
+                e0 = 256 * n
+                n += 1
+                if n <= EQA:
+                    act(V("EQ", e0, e0 + 64), V("Q", 192, 256), AF.Abs, bias=col("en", sl), scale=-1.0)
+                    act(V("EQ", e0 + 192, e0 + 256), V("EQ", e0, e0 + 64), AF.Relu, bias=col("en", 19), scale=col("en", 39))
+                else:
+                    ts(V("EQ", e0 + 64 * c, e0 + 256), V("Q", 64 * c, 256), col("en", sl), col("en", 16 + c), A.is_equal, A.mult)
+                mmul(V(bank[7], 64 * c, 64 * c + 64), V("TRT"), V("EQ", e0 + 64 * c, e0 + 64 * c + 64), False, False)
+                if c < 3:
+                    mmul(V(bank[7], 64 * c + 64, 256), V("BLT"), V("EQ", e0 + 64 * c + 64, e0 + 256), False, False)
+        for c in range(4):
+            mmul(V(bank[7], 64 * c, 64 * c + 32), V("BLn"), V("ins", 32 * c, 32 * c + 32), False, c == 3)
+        act(V("zg"), ind(V("Z%d" % t), oE))
+        act(V("yh"), ind(V("ya", 4096, 8192), oA))
+        mmul(V(bank[0], 0, 64), V("Ib"), V("zg"), True, False)
+        mmul(V(bank[0], 0, 64), V("Ib"), V("yh"), False, True)
+        act(V("ys"), V(bank[0], 0, 64), bias=123.75, scale=0.5)
+        tt(V("km"), V(bank[7], 0, 256), V("D"), A.mult)
+        tt(V("nrem", 0, 128), V("GN", 0, 128), V("dd"), A.not_equal)
+        scan(V("ks"), V("R64"), V("km"), A.mult, A.add)
+        tt(V("nrem", 128, 256), V("GN", 128, 256), V("dd"), A.not_equal)
+        if not last:
+            act(V("remK"), V("nrem"), bias=1024.0, scale=-2048.0)
+        vw = V("ks", 63, 256, 64)
+        for a0, a1, st in ((0, 8, 2), (1, 8, 2), (8, 16, 2), (9, 16, 2), (16, 20, 1)):
+            tt(V("sm", a0, a1, st), V("NM", a0, a1, st), vw, A.add)
+        tt(V("t1"), V("GN", 0, 128), V("nrem", 0, 128), A.mult)
+        tt(V("sm", 20, 40), V("sm", 0, 20), V("DUM"), A.min)
+        cp(oS, V("sm", 20, 40))
+        act(go, vw, AF.Relu, bias=1.0, scale=-1.0)
+        oS0, oS1, oSY = V("ou", 64, 72), V("ou", 72, 80), V("ou", 80, 84)
+
+        def put_y():
+            tt(ind(V("Yb", 16, 4176), oSY), V("ys"), V("cm128"), A.add)
+
+        if last:
+            early[0] = 5.0
+            put_y()
+            early[0] = 0.0
+            dma("s", T.y1[:, 0:2048], V("Yb", 16, 2064))
+            dma("a", T.y1[:, 2048:4096], V("Yb", 2064, 4112))
+        tt(ind(V("NB"), oS1), V("GN", 128, 256), V("nrem", 128, 256), A.mult)
+        tt(ind(V("NB"), oS0), V("t1"), V("t2"), A.add)
+        if not last:
+            tt(V("u1"), V("GF", 0, 128), V("remK", 0, 128), A.max)
+            tt(ind(V("FC"), oS1), V("GF", 128, 256), V("remK", 128, 256), A.max)
+            tt(ind(V("FC"), oS0), V("u1"), V("nu2"), A.subtract)
+            early[0] = -4.0
+            put_y()
+            early[0] = 0.0
+            act(V("goB", 0, 4), go)
+
+    for (x0, x1, a0, a1, st) in SEG:
+        act(V("neo", x0, x1), V("NB", a0, a1, st), bias=4095.0, scale=-1.0)
+    dma("s", T.ne1[:], V("neo"))
+    book_keeping(RO - 1)
+    book_keeping2(RO - 1)
+    for c in range(4):
+        dma("a" if c % 2 else "s", T.ends1[:, 1024 * c:1024 * c + 1024], V("Ef", 64 * c, 64 * c + 64))
+
+    def meet(x, y, wide):
+        if x[0] != y[0]:
+            return False
+        if x[5] <= y[4] or y[5] <= x[4]:
+            return False
+        if x[6] == y[6] and x[6] > 1 and x[4] % x[6] != y[4] % y[6]:
+            return False
+        s = SIZE[SCRATCH[x[0]][2]]
+        a0, a1, b0, b1 = x[1] * s, x[2] * s, y[1] * s, y[2] * s
+        if wide:
+            a0, b0, a1, b1 = a0 // 16 * 16, b0 // 16 * 16, -(-a1 // 16) * 16, -(-b1 // 16) * 16
+        if not (a0 < b1 and b0 < a1):
+            return False
+        if wide or (x[3] == 1 and y[3] == 1):
+            return True
+        return len(set(range(x[1], x[2], x[3])) & set(range(y[1], y[2], y[3]))) > 0
+
+    touch = {}
+    lastdma = {}
+    lastsend = [None]
+    for n, op in enumerate(ops):
+        q = op["q"]
+        asy = op["dma"] or q is None
+        sync, after = set(), set()
+        for w, v in [(False, v) for v in op["rd"]] + [(True, v) for v in op["wr"]]:
+            psum = SCRATCH[v[0]][0] == "psum"
+            for (m, w2, v2) in touch.get(v[0], []):
+                o2 = ops[m]
+                asy2 = o2["dma"] or o2["q"] is None
+                same = o2["q"] == q and not asy and not asy2
+                if psum and not same:
+                    sync.add(m)
+                elif psum and q == "p":
+                    after.add(m)
+                elif (w or w2) and meet(v, v2, asy or asy2):
+                    (after if same and w and not SAMEQ else sync).add(m)
+        if (op["dma"] and q != "g") or op["ext"] == "send":
+            if q in lastdma:
+                after.add(lastdma[q])
+            lastdma[q] = n
+        if op["ext"] == "send":
+            lastsend[0] = n
+        if q is None:
+            after.add(lastsend[0])
+        op["sync"], op["after"] = sync, after - sync
+        for v in op["rd"]:
+            touch.setdefault(v[0], []).append((n, False, v))
+        for v in op["wr"]:
+            touch.setdefault(v[0], []).append((n, True, v))
+    succ = [[] for op in ops]
+    for n, op in enumerate(ops):
+        for m in op["sync"]:
+            succ[m].append((n, True))
+        for m in op["after"]:
+            succ[m].append((n, False))
+    prio = [0.0] * len(ops)
+    for n in range(len(ops) - 1, -1, -1):
+        op = ops[n]
+        prio[n] = op["early"] + op["cost"] + max([0.0] + [prio[m] + (op["lat"] + WAKE if sy or ops[m]["q"] is None else 0.0) for m, sy in succ[n]] + [op["lat"]])
+    left = [len(op["sync"]) + len(op["after"]) for op in ops]
+    rdy = [0.0] * len(ops)
+    free = {q: 0.0 for q in eng}
+    cand = [n for n in range(len(ops)) if left[n] == 0]
+    order = []
+    while cand:
+        st = {n: max(rdy[n], free.get(ops[n]["q"], 0.0)) for n in cand}
+        n0 = min(cand, key=lambda n: (st[n], -prio[n], n))
+        q = ops[n0]["q"]
+        n = max([m for m in cand if ops[m]["q"] == q and st[m] <= st[n0] + LOOK * min(1.0, ops[n0]["cost"])], key=lambda m: (prio[m], -m))
+        op = ops[n]
+        cand.remove(n)
+        order.append(n)
+        end = st[n] + op["cost"]
+        if q is not None:
+            free[q] = end
+        for m, sy in succ[n]:
+            rdy[m] = max(rdy[m], end + (op["lat"] + WAKE if sy or ops[m]["q"] is None else 0.0))
+            left[m] -= 1
+            if left[m] == 0:
+                cand.append(m)
+    known = {q: {} for q in eng}
+    seq = {q: 0 for q in eng}
+    ndma = [0]
+    for pos, n in enumerate(order):
+        op = ops[n]
+        q = op["q"]
+        op["pos"] = pos
+        if op["dma"]:
+            op["key"] = "dm%d" % ndma[0]
+            op["idx"] = 16
+            ndma[0] += 1
+        elif q is None:
+            op["key"], op["idx"] = op["ext"]
+        else:
+            seq[q] += 1
+            op["key"], op["idx"] = q, seq[q]
+        op["waits"] = []
+        if q is not None:
+            for m in sorted(op["sync"], key=lambda m: -ops[m]["pos"]):
+                o2 = ops[m]
+                if known[q].get(o2["key"], 0) < o2["idx"]:
+                    op["waits"].append(m)
+                    o2["need"] = True
+                    known[q][o2["key"]] = o2["idx"]
+                    for k2, v2 in o2["clock"].items():
+                        if known[q].get(k2, 0) < v2:
+                            known[q][k2] = v2
+            op["clock"] = dict(known[q])
+        else:
+            op["clock"] = {}
+    cnt = {q: 0 for q in QSEM}
+    tail = []
+    for n in order:
+        op = ops[n]
+        q = op["q"]
+        if q is None:
+            op["sem"], op["val"] = op["ext"]
+            continue
+        for m in op["waits"]:
+            eng[q].wait_ge(T.sem[ops[m]["sem"]], ops[m]["val"])
+        ins = op["fn"]()
+        if op["dma"]:
+            op["sem"], op["val"] = op["key"], 16
+            ins.then_inc(T.sem[op["sem"]], 16)
+            if not op.get("need"):
+                tail.append(op)
+        elif op.get("need"):
+            cnt[q] += 1
+            op["sem"], op["val"] = QSEM[q], cnt[q]
+            ins.then_inc(T.sem[op["sem"]], 1)
+    g.wait_ge(T.sem.lsem, sent[0])
+    for op in tail:
+        eng[op["q"]].wait_ge(T.sem[op["sem"]], 16)

@@ -1,17 +1,22 @@
+import numpy as np
 from concourse.bass import DstId, RemoteDMATransfer, IndirectOffsetOnAxis
 from concourse.mybir import AluOpType, AxisListType, ActivationFunctionType
 
 F, B, I, U = "float32", "bfloat16", "int32", "uint16"
 RO = 3
-KDS = (8, 8)
+KDS = (7, 8)
 SAMEQ = True
 CAP = 1009 * 16384 + 1023
-CY, PECY, WAKE, LOOK, EARLY = 1.04e-3, 0.52e-3, 0.06, 0.3, 12.0
+CY, PECY, WAKE, LOOK, EARLY = 0.9e-3, 0.45e-3, 0.1, 0.3, 12.0
 DELTA = False
+BOOST, BOOST2, BOOST3, TLATE = 0.0, 0.0, 0.0, 0.0
+PLAN = {}
+ROUNDS, JIT, SEED = 10, 0.3, 1
+KO, LATE = (0, 13), 2
 EQA = 2
 SSQ = "v"
 FE = "avavavavavav"
-TILE = "vva"
+TILE = "vvv"
 
 SB = {
     "Yb": (4176, B), "EWin": (4096, B), "FG": (12288, B), "ya": (8192, B), "mm": (8192, B), "mz": (8192, B), "rl": (8192, B),
@@ -28,14 +33,14 @@ SB = {
     "Ib": (128, B), "If": (128, F), "nI": (128, B), "Is": (128, B), "Ik": (128, B), "BLK": (128, B), "BLm4": (128, B), "BL4": (128, B),
     "BLz": (128, B), "BLT": (128, B), "BLn": (128, B), "TRI": (128, B), "TRT": (128, B), "FST": (128, B), "FS4": (128, B), "ZS": (144, B),
     "BC": (768, B), "RP": (1152, B), "IW": (160, B), "msk": (16, F), "PT": (1536, B), "cm128": (64, B),
-    "aU": (512, U), "cU": (512, U), "nbh": (512, B), "nbl": (512, B), "fS": (512, B), "sS": (512, B), "acc": (512, F),
+    "aU": (512, U), "cU": (512, U), "nbh": (512, B), "nbl": (512, B), "fS": (512, B), "sS": (512, B), "acc": (512, F), "acd": (512, F),
     "vS": (256, B), "pc": (256, B), "pv": (256, B), "CW": (272, F), "sg": (256, B), "r1": (256, B),
     "km": (256, F), "ks": (256, F), "sm": (416, F), "f2": (52, I), "NM": (36, I), "si": (12, I), "ou": (96, U),
     "G1": (128, F), "G2": (128, F), "G3": (128, F), "Q": (256, B), "EQ": (4096, B), "GN": (256, F), "GF": (256, F), "dd": (128, F),
-    "emp": (128, B), "ins": (128, B), "t2": (128, F), "nu2": (128, F), "nrem": (256, F), "remK": (256, F),
-    "t1": (128, F), "u1": (128, F), "zg": (64, B), "yh": (64, B), "ys": (64, B), "goB": (8, B), "en": (96, F),
+    "emp": (128, B), "ins": (128, B), "t2": (128, F), "nu2": (128, F),
+    "nIf": (128, F), "zg": (64, B), "yh": (64, B), "ys": (64, B), "goB": (8, B), "en": (112, F), "ax": (256, B), "rd": (256, F), "rf": (256, F), "cn": (128, F), "cf": (128, F),
 }
-MATS = ["BLy", "Ib", "nI", "Is", "Ik", "BLK", "BLm4", "BL4", "BLz", "BLT", "BLn", "TRI", "TRT", "FST", "FS4"]
+MATS = ["BLx", "BLy", "Ib", "nI", "Is", "Ik", "BLK", "BLm4", "BL4", "BLz", "BLT", "BLn", "TRI", "TRT", "FST", "FS4"]
 SCRATCH = {k: ("sbuf", [128, v[0]], v[1]) for k, v in SB.items() if k not in MATS}
 SCRATCH["MT"] = ("sbuf", [128, 128 * len(MATS)], B)
 for _b in range(8):
@@ -99,7 +104,7 @@ def rank_program(g, core, T, topo):
         elif ext == "send":
             cost = 0.3
         elif dma:
-            cost, lat = (1.7 if q == "g" else 0.1), 2.0 + n * len(range(*flat[0][4:7])) * SIZE[SCRATCH[flat[0][0]][2]] / 100e3
+            cost, lat = (1.7 if q == "g" else 0.1), 2.0 + n * len(range(*flat[0][4:7])) * SIZE[SCRATCH[flat[0][0]][2]] / 180e3
         elif q == "p":
             cost, lat = PECY * max(64, outs[0][2] - outs[0][1]) * (4 if F in dts[1:] else 1), 0.1
         elif q == "g":
@@ -214,7 +219,7 @@ def rank_program(g, core, T, topo):
     dma("s", V("EWin", 0, 4096, 1, 0, 128, 16), V("cC", 0, 256))
     dma("s", V("EWin", 0, 4096, 1, 1, 128, 16), V("cC", 256, 512))
     dma("s", Ywin, T.y0[:])
-    cp(V("Ef"), V("eB"))
+    add("v", lambda: g.vector.tensor_copy(ap(V("Ef")), ap(V("eB"))), [V("Ef")], [V("eB"), V("cB", 0, 2)])
     cp(V("neu"), V("nei"))
     for t in range(RO):
         for i in range(4):
@@ -343,7 +348,8 @@ def rank_program(g, core, T, topo):
         act(V("BLm4"), V("BLK"), scale=-4.0)
         act(V("BL4"), V("BLK"), scale=4.0)
         act(V("BLz"), V("BLK"), scale=4.0 * KDS[0])
-        act(V("BLy"), V("BLK"), scale=4.0 * KDS[1])
+        act(V("BLx"), V("BLK"), scale=4.0 * KO[0])
+        act(V("BLy"), V("BLK"), scale=4.0 * KO[1])
         act(V("If"), V("Ib"))
         act(V("Is"), V("Ib"), scale=-2.0 ** -27)
         act(V("Ik"), V("Ib"), scale=1024.0)
@@ -372,25 +378,25 @@ def rank_program(g, core, T, topo):
             act(col("Acc", 4), col("Acc", 0), bias=thb, scale=-32.0)
             act(col("Acc", 5), col("Acc", 2), bias=col("Acc", 4), scale=1024.0)
             act(bT, col("Acc", 3), bias=col("Acc", 5), scale=1024.0)
+        for c in range(4):
+            act(V("en", 80 + c, 96, 4), V("en", 64 + c, 80, 4), scale=col("en", 20 + c))
+        mmul(V(bank[6], 0, 16), V("If"), V("en", 80, 96), True, False)
+        mmul(V(bank[6], 0, 16), V("If"), V("EW", 16 * t, 16 * t + 16), False, True)
+        for i in range(4):
+            act(V("Ef", 16 * i + 5 * t, 256, 64), V(bank[6], 4 * i, 4 * i + 4))
+
+    def new_ends(t):
         ts(V("en", 32, 40), qw(0, 8), -256.0, 256.0, A.max, A.min)
-        act(ngo, go, scale=-1.0)
         tt(V("en", 40, 48), qw(0, 8), V("en", 32, 40), A.add)
         tt(V("en", 48, 52), V("en", 40, 48, 2), V("en", 41, 48, 2), A.min)
         tt(V("en", 52, 56), V("en", 40, 48, 2), V("en", 41, 48, 2), A.max)
         act(V("en", 56, 60), V("en", 48, 52), bias=393600.0, scale=512.0)
         act(V("en", 60, 64), V("en", 52, 56), scale=0.5)
-        tt(V("en", 32, 36), V("en", 56, 60), V("en", 60, 64), A.add)
-        tt(gE, V("en", 32, 36), go, A.mult)
         for c in range(4):
-            act(V("en", 80 + c, 96, 4), V("sm", eq_ + 32 + c, eq_ + 48, 4), bias=1.0, scale=col("en", 24 + c))
+            act(col("en", 28 + c), col("en", 56 + c), bias=col("en", 60 + c))
         for c in range(4):
-            act(V("en", 64 + c, 80, 4), V("sm", eq_ + 32 + c, eq_ + 48, 4), scale=col("en", 28 + c))
-
-    def book_keeping2(t):
-        tt(V("en", 80, 96), V("en", 80, 96), V("EW", 16 * t, 16 * t + 16), A.mult)
-        tt(V("en", 80, 96), V("en", 80, 96), V("en", 64, 80), A.add)
-        for i in range(4):
-            act(V("Ef", 16 * i + 5 * t, 256, 64), V("en", 80 + 4 * i, 84 + 4 * i))
+            act(V("en", 96 + c, 112, 4), V("EW", 16 * t + c, 16 * t + 16, 4), bias=col("en", 28 + c), scale=-1.0)
+        tt(V("en", 64, 80), V("en", 96, 112), V("sm", eq_ + 32, eq_ + 48), A.mult)
 
     def ya_gather(h, q, n=1):
         c = 256 * h + 64 * q
@@ -407,30 +413,38 @@ def rank_program(g, core, T, topo):
         oU, oV = V("off", 64 * t, 64 * t + 32), V("off", 64 * t + 32, 64 * t + 64)
         z = [V("PZ%d" % t), V("Z%d" % t)]
         act(V("nbh"), ind(V("NB"), oV))
-        ts(V("aU"), ind(V("NB"), oU), -1.0, 4095.0, A.mult, A.add)
+        early[0] = BOOST * (t > 0)
+        ts(V("aU", 0, 64), ind(V("NB"), V("off", 64 * t, 64 * t + 4)), -1.0, 4095.0, A.mult, A.add)
+        early[0] = 0.0
+        ts(V("aU", 64, 512), ind(V("NB"), V("off", 64 * t + 4, 64 * t + 32)), -1.0, 4095.0, A.mult, A.add)
         tt(V("nbl"), ind(V("NB"), oV), V("nbh"), A.subtract)
         act(V("fS"), ind(V("FC"), oV), scale=-8192.0)
         if SSQ == "v":
             ts(V("sS"), ind(V("FC"), oU), -8192.0, None, A.mult)
         else:
             act(V("sS"), ind(V("FC"), oU), scale=-8192.0)
+        early[0] = BOOST2 * (t > 0)
         ya_gather(0, 0)
+        early[0] = 0.0
         if t == 0:
             early[0] = -10.0
             late_consts_v()
             early[0] = 0.0
         else:
+            new_ends(t - 1)
             book_keeping(t - 1)
         for n in range(3):
             b = V(bank[5 + n])
+            early[0] = -TLATE * n
             for pc, x in enumerate(("nbh", "nbl", "fS")):
                 mmul(b, V("RP", 128 * (3 * n + pc), 128 * (3 * n + pc) + 128), V(x), pc == 0, pc == 2)
             if TILE[n] == "v":
                 cp(V("PT", 512 * n, 512 * n + 512), b)
             else:
                 act(V("PT", 512 * n, 512 * n + 512), b)
+        early[0] = 0.0
         for j in range(16):
-            b = V(bank[(0, 1, 2, 5, 6, 7)[j % 6]])
+            b = V(bank[(0, 1, 2, 3, 5, 6, 7)[j % 7]])
             if DELTA and j > 0:
                 jj, n = divmod(j - 1, 3)
                 b, w = V(bank[n]), V(bank[5 + (j + 1) % 3])
@@ -447,26 +461,37 @@ def rank_program(g, core, T, topo):
                 mmul(b, bc, V("nbh"), True, False)
                 mmul(b, bc, V("nbl"), False, False)
                 mmul(b, bc, V("fS"), False, False)
+                early[0] = BOOST3
                 mmul(b, V("nI"), V("sS"), False, True)
+                early[0] = 0.0
             else:
                 n, jj = divmod(j - 1, 5)
                 mmul(b, V("nI"), V("sS"), True, False)
                 mmul(b, V("BC", 128 * jj, 128 * jj + 128), V("PT", 512 * n, 512 * n + 512), False, True)
-            if j == 0:
-                act(V("acc"), b, AF.Abs)
+            ac = V("acc" if j % 2 == 0 else "acd")
+            if j < 2:
+                act(ac, b, AF.Abs)
             else:
                 act(b, b, AF.Abs)
-                tt(V("acc"), b, V("acc"), A.min)
-        ts(V("cU"), V("acc"), -1.0, 4111.0, A.mult, A.add)
+                tt(V(bank[4]) if j == 15 else ac, b, ac, A.min)
+        for h in range(2):
+            tt(V("acc", 256 * h, 256 * h + 256), V(bank[4], 256 * h, 256 * h + 256), V("acc", 256 * h, 256 * h + 256), A.min)
+        for h in range(2):
+            ts(V("cU", 256 * h, 256 * h + 256), V("acc", 256 * h, 256 * h + 256), -1.0, 4111.0, A.mult, A.add)
         mmul(V(bank[3], 0, 256), V("Ib"), z[0], True, True, V("cU", 0, 2))
         mmul(V(bank[3], 256, 512), V("Ib"), z[1], True, True)
-        if t > 0:
-            book_keeping2(t - 1)
-        KD = KDS[1]
+        def min_half(sub, stop):
+            o = V(bank[5], 128 * sub, 128 * sub + 128)
+            for k in range(KO[sub]):
+                r0 = 4096 + 2048 * sub + 128 * k
+                tt(V("mz", r0, r0 + 128), V(bank[3], 256 + 128 * sub, 384 + 128 * sub), V("mm", 4096 + 2048 * sub + k, 6144 + 2048 * sub, 16), A.min)
+                if stop and k == KO[sub] - LATE:
+                    relu_sum(1, 1, False)
+                mmul(o, V("BLm4"), V("mz", r0, r0 + 128), False, stop and k == KO[sub] - 1)
 
         def relu_part(h, sub):
             c = 256 * h + 128 * sub
-            KA = list(range(KDS[h], 16))
+            KA = list(range(KO[sub] if h else KDS[0], 16))
             for k0 in range(0, len(KA), 4):
                 ks = KA[k0:k0 + 4]
                 bn = bank[rot[0] % 3]
@@ -479,7 +504,7 @@ def rank_program(g, core, T, topo):
                 act(V("rl", r0, r0 + 128 * len(ks)), V(bn, 0, 128 * len(ks)), AF.Relu)
 
         def relu_sum(h, sub, stop):
-            for n in range(16 - KDS[h]):
+            for n in range(16 - (KO[sub] if h else KDS[0])):
                 r0 = 4096 * h + 2048 * sub + 128 * n
                 mmul(V(bank[4 + h], 128 * sub, 128 * sub + 128), V("BL4"), V("rl", r0, r0 + 128), False, stop and n == 15 - KDS[h])
 
@@ -515,8 +540,10 @@ def rank_program(g, core, T, topo):
         ya_gather(1, 2)
         yc_gather(1, 1)
         ya_gather(1, 3)
-        mmul(V(bank[5], 0, 256), V("BLy"), z[1], True, False)
-        mmul(V(bank[5], 0, 256), V("Ib"), V("icol"), False, False)
+        mmul(V(bank[5], 0, 256), V("Ib"), V("icol"), True, False)
+        mmul(V(bank[5], 0, 128), V("BLx"), V(z[1][0], 0, 128), False, False)
+        mmul(V(bank[5], 128, 256), V("BLy"), V(z[1][0], 128, 256), False, False)
+        min_half(0, False)
         yc_gather(1, 2)
         relu_part(1, 0)
         act(V("vS"), ind(V("codeT"), V("off", 64 * t + 48, 64 * t + 64)), scale=-8192.0)
@@ -532,12 +559,8 @@ def rank_program(g, core, T, topo):
         mmul(V(bank[5], 0, 256), V("If"), V("PK%d" % t), False, False)
         act(V(bank[7], 0, 256), V(bank[7], 0, 256), AF.Abs)
         relu_part(1, 1)
-        min_part(1)
-        min_sum(1, 0, KD - 2)
-        relu_sum(1, 1, False)
+        min_half(1, True)
         act(V("pv"), V(bank[7], 0, 256), AF.Relu, bias=4096.0, scale=-1.0)
-        min_sum(1, KD - 2, KD - 1)
-        mmul(V(bank[5], 0, 256), V("BLm4"), V("mz", 4096 + 256 * (KD - 1), 4096 + 256 * KD), False, True)
         mmul(V(bank[6], 0, 256), V("Ik"), V("pv"), False, True)
         act(V("CW", 0, 256), V(bank[6], 0, 256), bias=kb, scale=16384.0)
         if t == 0:
@@ -606,6 +629,15 @@ def rank_program(g, core, T, topo):
                 x = 64 * (n // 2) + 16 * (1 - n % 2)
                 mmul(V(bank[1], 128 + 16 * n, 144 + 16 * n), V("nI"), V("Q", x, x + 16), False, n == 7)
             act(V("nu2"), V(bank[1], 128, 256), AF.Relu, bias=-3072.0)
+        act(V(bank[3], 0, 128), V("dd"))
+        tt(V("rd", 0, 128), V("GN", 0, 128), V(bank[3], 0, 128), A.not_equal)
+        tt(V("rd", 128, 256), V("GN", 128, 256), V(bank[3], 0, 128), A.not_equal)
+        act(V(bank[4], 0, 128), V("GN", 0, 128))
+        tt(V("cn"), V(bank[4], 0, 128), V("rd", 0, 128), A.mult)
+        if not last:
+            act(V("rf", 128, 256), V("rd", 128, 256), bias=1024.0, scale=-2048.0)
+            act(V(bank[5], 0, 128), V("rd", 0, 128), bias=1024.0, scale=-2048.0)
+            tt(V("cf"), V("GF", 0, 128), V(bank[5], 0, 128), A.max)
         n = 0
         if EQA:
             act(col("en", 39), col("en", 19), scale=-1.0)
@@ -629,15 +661,12 @@ def rank_program(g, core, T, topo):
         mmul(V(bank[0], 0, 64), V("Ib"), V("yh"), False, True)
         act(V("ys"), V(bank[0], 0, 64), bias=123.75, scale=0.5)
         tt(V("km"), V(bank[7], 0, 256), V("D"), A.mult)
-        tt(V("nrem", 0, 128), V("GN", 0, 128), V("dd"), A.not_equal)
         scan(V("ks"), V("R64"), V("km"), A.mult, A.add)
-        tt(V("nrem", 128, 256), V("GN", 128, 256), V("dd"), A.not_equal)
-        if not last:
-            act(V("remK"), V("nrem"), bias=1024.0, scale=-2048.0)
+        if last:
+            new_ends(t)
         vw = V("ks", 63, 256, 64)
         for a0, a1, st in ((0, 8, 2), (1, 8, 2), (8, 16, 2), (9, 16, 2), (16, 20, 1)):
             tt(V("sm", a0, a1, st), V("NM", a0, a1, st), vw, A.add)
-        tt(V("t1"), V("GN", 0, 128), V("nrem", 0, 128), A.mult)
         tt(V("sm", 20, 40), V("sm", 0, 20), V("DUM"), A.min)
         cp(oS, V("sm", 20, 40))
         act(go, vw, AF.Relu, bias=1.0, scale=-1.0)
@@ -652,13 +681,12 @@ def rank_program(g, core, T, topo):
             early[0] = 0.0
             dma("s", T.y1[:, 0:2048], V("Yb", 16, 2064))
             dma("a", T.y1[:, 2048:4096], V("Yb", 2064, 4112))
-        tt(ind(V("NB"), oS1), V("GN", 128, 256), V("nrem", 128, 256), A.mult)
-        tt(ind(V("NB"), oS0), V("t1"), V("t2"), A.add)
+        tt(ind(V("NB"), oS1), V("GN", 128, 256), V("rd", 128, 256), A.mult)
+        tt(ind(V("NB"), oS0), V("cn"), V("t2"), A.add)
         if not last:
-            tt(V("u1"), V("GF", 0, 128), V("remK", 0, 128), A.max)
-            tt(ind(V("FC"), oS1), V("GF", 128, 256), V("remK", 128, 256), A.max)
-            tt(ind(V("FC"), oS0), V("u1"), V("nu2"), A.subtract)
-            early[0] = -4.0
+            tt(ind(V("FC"), oS1), V("GF", 128, 256), V("rf", 128, 256), A.max)
+            tt(ind(V("FC"), oS0), V("cf"), V("nu2"), A.subtract)
+            early[0] = 0.0
             put_y()
             early[0] = 0.0
             act(V("goB", 0, 4), go)
@@ -667,7 +695,6 @@ def rank_program(g, core, T, topo):
         act(V("neo", x0, x1), V("NB", a0, a1, st), bias=4095.0, scale=-1.0)
     dma("s", T.ne1[:], V("neo"))
     book_keeping(RO - 1)
-    book_keeping2(RO - 1)
     for c in range(4):
         dma("a" if c % 2 else "s", T.ends1[:, 1024 * c:1024 * c + 1024], V("Ef", 64 * c, 64 * c + 64))
 
@@ -751,6 +778,58 @@ def rank_program(g, core, T, topo):
             left[m] -= 1
             if left[m] == 0:
                 cand.append(m)
+    fw = [[] for op in ops]
+    bw = [[] for op in ops]
+    for n, op in enumerate(ops):
+        for m, sy in succ[n]:
+            lag = op["lat"] + WAKE if sy or ops[m]["q"] is None else 0.0
+            fw[m].append((n, lag))
+            bw[n].append((m, lag))
+
+    def place(seqn, pre, back):
+        end = [0.0] * len(ops)
+        busy = {q: [] for q in eng}
+        for n in seqn:
+            op = ops[n]
+            r = max([op["lat"] if back else 0.0] + [end[m] + lag for m, lag in pre[n]])
+            if op["q"] is not None:
+                iv = busy[op["q"]]
+                k = len(iv)
+                while k > 0 and iv[k - 1][1] > r:
+                    k -= 1
+                while k < len(iv) and iv[k][0] < r + op["cost"] - 1e-9:
+                    r = max(r, iv[k][1])
+                    k += 1
+                iv.insert(k, (r, r + op["cost"]))
+            end[n] = r + op["cost"]
+        return end
+
+    if "order" not in PLAN:
+        best = None
+        rng = np.random.default_rng(SEED)
+        for it in range(ROUNDS + 1):
+            at = {n: k for k, n in enumerate(order)}
+            end = place(order, fw, False)
+            order = sorted(order, key=lambda n: (end[n] - ops[n]["cost"], at[n]))
+            span = max(end[n] + ops[n]["lat"] for n in order)
+            PLAN.setdefault("spans", []).append(span)
+            if best is None or span < best[0]:
+                best = (span, order, end)
+            order, end = best[1], best[2]
+            at = {n: k for k, n in enumerate(order)}
+            back = sorted(order, key=lambda n: (-end[n], -at[n]))
+            keep = [op["cost"] for op in ops]
+            if it > 0:
+                for op, x in zip(ops, rng.random(len(ops)).tolist()):
+                    op["cost"] = op["cost"] * (1.0 + JIT * (2 * x - 1))
+            end = place(back, bw, True)
+            for op, x in zip(ops, keep):
+                op["cost"] = x
+            at = {n: k for k, n in enumerate(back)}
+            order = sorted(back, key=lambda n: (-end[n], -at[n]))
+        PLAN["order"] = best[1]
+        PLAN["span"] = best[0]
+    order = PLAN["order"]
     known = {q: {} for q in eng}
     seq = {q: 0 for q in eng}
     ndma = [0]

@@ -2,52 +2,48 @@ import numpy as np
 from concourse.bass import DstId, RemoteDMATransfer, IndirectOffsetOnAxis
 from concourse.mybir import AluOpType, AxisListType, ActivationFunctionType
 
-F, B, I, U = "float32", "bfloat16", "int32", "uint16"
+F, B, I, U, H = "float32", "bfloat16", "int32", "uint16", "float16"
 RO = 3
-KDS = (7, 8)
-SAMEQ = True
 CAP = 1009 * 16384 + 1023
-CY, PECY, WAKE, LOOK, EARLY = 0.9e-3, 0.45e-3, 0.1, 0.3, 12.0
-DELTA = False
-BOOST, BOOST2, BOOST3, TLATE = 0.0, 0.0, 0.0, 0.0
+PEN, BIG = 2.0 ** 25, 2.0 ** 25
+KTOP = 256.0 * 35216 + 255
+CY, PECY, WAKE, LOOK, EARLY = 0.83e-3, 0.417e-3, 0.1, 0.3, 12.0
 PLAN = {}
 ROUNDS, JIT, SEED = 10, 0.3, 1
-KO, LATE = (0, 13), 2
-EQA = 2
-SSQ = "v"
 FE = "avavavavavav"
-TILE = "vvv"
+PART = ((0, 128), (128, 128))
+OWN = ((0, 64, "a"), (64, 64, "a"), (128, 64, "v"), (192, 64, "v"))
+X0, X1 = min([256] + [a for a, n, e in OWN if e == "v"]), 512
+EQA, FLAT = 1, 4.5
+TAB = 4160
 
 SB = {
-    "Yb": (4176, B), "EWin": (4096, B), "FG": (12288, B), "ya": (8192, B), "mm": (8192, B), "mz": (8192, B), "rl": (8192, B),
-    "NB": (1152, F), "FC": (1152, F), "nei": (768, I), "neu": (768, U), "neo": (768, F),
-    "eA": (256, I), "eB": (256, I), "Ef": (256, F), "UV": (512, I), "cB": (512, F), "cC": (512, B),
-    "EW": (48, F), "EWi": (48, I), "LUV": (96, I), "lA": (96, F), "lB": (96, F), "CODE": (96, B),
-    "PC0": (96, B), "PC1": (96, B), "PC2": (96, B), "Z0": (256, B), "Z1": (256, B), "Z2": (256, B),
-    "PZ0": (256, B), "PZ1": (256, B), "PZ2": (256, B), "PS0": (256, F), "PS1": (256, F), "PS2": (256, F),
-    "PK0": (256, F), "PK1": (256, F), "PK2": (256, F), "off": (192, U),
-    "PW": (192, F), "pw": (288, F), "pwa": (48, F), "pwb": (48, F), "CB": (192, B),
-    "pi": (4, I), "pq": (8, I), "pf": (16, F), "thi": (4, I), "Acc": (8, F), "ysave": (8, B),
-    "IO": (160, F), "ML": (256, F), "MG": (128, F), "M64": (256, F), "M32": (128, F), "D": (256, F), "R16": (256, F), "R64": (256, F),
-    "CAPS": (128, F), "CE": (256, B), "icol": (256, B), "codeT": (1024, B), "codeX": (768, B), "DDT": (256, F), "DUM": (20, F),
-    "Ib": (128, B), "If": (128, F), "nI": (128, B), "Is": (128, B), "Ik": (128, B), "BLK": (128, B), "BLm4": (128, B), "BL4": (128, B),
-    "BLz": (128, B), "BLT": (128, B), "BLn": (128, B), "TRI": (128, B), "TRT": (128, B), "FST": (128, B), "FS4": (128, B), "ZS": (144, B),
-    "BC": (768, B), "RP": (1152, B), "IW": (160, B), "msk": (16, F), "PT": (1536, B), "cm128": (64, B),
-    "aU": (512, U), "cU": (512, U), "nbh": (512, B), "nbl": (512, B), "fS": (512, B), "sS": (512, B), "acc": (512, F), "acd": (512, F),
-    "vS": (256, B), "pc": (256, B), "pv": (256, B), "CW": (272, F), "sg": (256, B), "r1": (256, B),
-    "km": (256, F), "ks": (256, F), "sm": (416, F), "f2": (52, I), "NM": (36, I), "si": (12, I), "ou": (96, U),
-    "G1": (128, F), "G2": (128, F), "G3": (128, F), "Q": (256, B), "EQ": (4096, B), "GN": (256, F), "GF": (256, F), "dd": (128, F),
-    "emp": (128, B), "ins": (128, B), "t2": (128, F), "nu2": (128, F),
-    "nIf": (128, F), "zg": (64, B), "yh": (64, B), "ys": (64, B), "goB": (8, B), "en": (112, F), "ax": (256, B), "rd": (256, F), "rf": (256, F), "cn": (128, F), "cf": (128, F),
+    "Yb": (4176, B), "EWin": (4096, B), "FG": (12288, B), "ya": (8192, B), "mm": (8192, B), "m15": (256, B), "mz": (16 * (256 - X0), B),
+    "zr0": (16 * (X1 - X0), B), "zr1": (16 * (X1 - X0), B),
+    "NB": (TAB, F), "FC": (TAB, F), "EF": (TAB, F), "nei": (768, I), "neu": (768, U), "neo": (768, F),
+    "eA": (256, I), "Ef": (256, F), "UV": (512, I), "cB": (512, F), "cC": (512, B), "TR": (96, B),
+    "ZZ0": (512, B), "ZZ1": (512, B), "ZZ2": (512, B), "off": (240, U),
+    "pi": (4, I), "pq": (8, I), "pf": (48, F), "thi": (4, I), "ysave": (8, B), "MK": (12, F),
+    "IO": (176, F), "ML": (256, B), "MG": (128, B), "M4": (256, B), "M64": (256, B), "M32": (128, B),
+    "RB16": (192, F), "RB64": (256, F), "CAPS": (128, F), "CE": (256, B), "PC": (256, B), "PENK": (256, B), "PEN16": (256, B),
+    "icolK": (256, B), "icol2": (512, B), "codeT": (1024, B), "codeX": (768, B), "numT": (1024, F),
+    "If": (128, F), "ZS": (144, B), "IW": (160, B), "PT": (1024, H), "cm128": (64, B),
+    "aU": (512, U), "cU": (512, U), "bV": (512, H), "FS": (1024, B), "TT": (512, B), "acc": (512, F), "acd": (512, F),
+    "pc": (256, B), "pv": (256, B), "CW": (272, F), "sg": (256, B), "r1": (256, B), "KA": (256, F),
+    "ke": (256, F), "kd": (256, F), "k3": (192, F), "kv": (256, F), "si": (40, I), "ou": (96, U), "NM": (20, F), "has": (16, F), "EA": (256, B),
+    "G1": (128, F), "G2": (128, F), "G3": (128, F), "Q3": (192, B), "Q": (256, B), "EQ": (4096, B), "GN": (256, F), "GF": (256, F),
+    "dd": (128, F), "emp": (128, B), "ins": (128, B), "MX": (256, F), "rd": (256, F),
+    "zg": (64, B), "yh": (64, B), "ys": (64, B), "GB": (8, B), "nsv": (192, F), "mn": (64, F), "en": (64, F),
 }
-MATS = ["BLx", "BLy", "Ib", "nI", "Is", "Ik", "BLK", "BLm4", "BL4", "BLz", "BLT", "BLn", "TRI", "TRT", "FST", "FS4"]
-SCRATCH = {k: ("sbuf", [128, v[0]], v[1]) for k, v in SB.items() if k not in MATS}
+MATS = (["nI", "Is", "Ik", "In8k", "BLK", "BL256", "BLn256", "BL4096", "BL8k", "BLn8k", "TRn", "T1", "FST", "FS4", "BC0", "BC1"]
+        + ["RP%d" % k for k in range(4)] + ["BT%d" % k for k in range(8)] + ["SH%d" % k for k in range(4)])
+SCRATCH = {k: ("sbuf", [128, v[0]], v[1]) for k, v in SB.items()}
 SCRATCH["MT"] = ("sbuf", [128, 128 * len(MATS)], B)
 for _b in range(8):
     SCRATCH["bank%d" % _b] = ("psum", [128, 512], F)
-NDMA = 24
-SEMAPHORES = ["sv", "sa", "sp", "sg", "lsem"] + ["dm%d" % k for k in range(NDMA)] + ["%s%d" % (a, t) for a in ("qc", "qz", "qk") for t in range(RO)]
-SIZE = {F: 4, B: 2, I: 4, U: 2}
+NDMA = 16
+SEMAPHORES = ["sv", "sa", "sp", "sg", "lsem"] + ["dm%d" % k for k in range(NDMA)] + ["%s%d" % (a, t) for a in ("qc", "qz", "qk", "qm", "lk", "lm") for t in range(RO)]
+SIZE = {F: 4, B: 2, I: 4, U: 2, H: 2}
 QSEM = {"v": "sv", "a": "sa", "p": "sp", "g": "sg"}
 
 
@@ -59,6 +55,7 @@ def rank_program(g, core, T, topo):
     A = AluOpType
     AF = ActivationFunctionType
     ops = []
+    group = {}
     early = [0.0]
     eng = {"v": g.vector, "a": g.scalar, "p": g.tensor, "g": g, "s": g.sync}
 
@@ -82,7 +79,7 @@ def rank_program(g, core, T, topo):
         cc = slice(v[1], v[2], v[3]) if v[3] != 1 else slice(v[1], v[2])
         return T[v[0]][pp, cc]
 
-    def add(q, fn, outs, ins, dma=False, ext=None, two=False):
+    def add(q, fn, outs, ins, dma=False, ext=None, two=False, way=3.0, left=None):
         rd, wr = [], []
         for v in ins:
             if isinstance(v, tuple):
@@ -99,27 +96,28 @@ def rank_program(g, core, T, topo):
         n = max([len(range(v[1], v[2], v[3])) for v in flat] + [1])
         dts = [SCRATCH[v[0]][2] for v in flat if v[2] - v[1] > 1]
         lat = 0.0
+        fix = 0.065 if q == "a" else 0.05
         if q is None:
-            cost, lat = 0.0, 3.0
+            cost, lat = 0.0, way
         elif ext == "send":
-            cost = 0.3
+            cost, lat = 0.3, (way if left else 0.0)
         elif dma:
             cost, lat = (1.7 if q == "g" else 0.1), 2.0 + n * len(range(*flat[0][4:7])) * SIZE[SCRATCH[flat[0][0]][2]] / 180e3
         elif q == "p":
-            cost, lat = PECY * max(64, outs[0][2] - outs[0][1]) * (4 if F in dts[1:] else 1), 0.1
+            cost, lat = PECY * max(64, len(range(*outs[0][1:4]))) * (4 if SCRATCH[ins[0][0]][2] == F else 1), 0.1
         elif q == "g":
-            cost = 0.13 + 2 * CY * n
+            cost = 0.17 + 2 * CY * n
         elif outs[0][0] == "ind":
-            cost = 0.05 + 3.8 * CY * n
+            cost = fix + 3.8 * CY * n
         elif ins and ins[0][0] == "ind":
-            cost = 0.05 + 1.56 * CY * n
+            cost = fix + 1.56 * CY * n
         elif two and all(SCRATCH[v[0]][0] == "sbuf" for v in ins):
-            cost = 0.05 + CY * max(64, 2 * n)
-        elif q == "v" and not two and all(d in (B, U) for d in dts):
-            cost = 0.05 + CY * max(64, n / 2)
+            cost = fix + CY * max(64, 2 * n)
+        elif q == "v" and not two and all(SIZE[d] == 2 for d in dts):
+            cost = fix + CY * max(64, n / 2)
         else:
-            cost = 0.05 + CY * max(64, n)
-        ops.append({"q": q, "fn": fn, "rd": rd, "wr": wr, "dma": dma, "ext": ext, "cost": cost, "lat": lat, "early": early[0]})
+            cost = fix + CY * max(64, n)
+        ops.append({"q": q, "fn": fn, "rd": rd, "wr": wr, "dma": dma, "ext": ext, "cost": cost, "lat": lat, "early": early[0], "left": left})
 
     def ts(o, x, s1, s2, op0, op1=None):
         if op1 is None:
@@ -136,14 +134,24 @@ def rank_program(g, core, T, topo):
     def ms(o, c):
         add("v", lambda: g.vector.memset(ap(o), c), [o], [])
 
-    def scan(o, x, y, op0, op1):
+    def scan(o, x, y, op0=A.max, op1=A.min):
         add("v", lambda: g.vector.tensor_tensor_scan(ap(o), ap(x), ap(y), 0.0, op0, op1), [o], [x, y])
+
+    def transpose(o, x):
+        add("v", lambda: g.vector.transpose(ap(o), ap(x)), [o], [x])
 
     def act(o, x, func=AF.Identity, bias=0.0, scale=1.0):
         add("a", lambda: g.scalar.activation(ap(o), ap(x), func, bias=ap(bias), scale=ap(scale)), [o], [x, bias, scale])
 
-    def mmul(o, l, r, start, stop, behind=None):
-        add("p", lambda: g.tensor.matmul(ap(o), ap(l), ap(r), start, stop), [o], [l, r, behind])
+    def mmul(o, l, r, start, stop):
+        add("p", lambda: g.tensor.matmul(ap(o), ap(l), ap(r), start, stop), [o], [l, r])
+        group[o[0]] = group.get(o[0], 0) + start
+        if not start and not stop:
+            ops[-1]["inner"] = group[o[0]]
+
+    def msum(o, terms):
+        for n, (l, r) in enumerate(terms):
+            mmul(o, l, r, n == 0, n == len(terms) - 1)
 
     def iota(o, pat, base=0, cm=0):
         if SCRATCH[o[0]][2] == I:
@@ -151,12 +159,15 @@ def rank_program(g, core, T, topo):
         else:
             add("g", lambda: g.iota(ap(o), pat, base, cm, allow_small_or_imprecise_dtypes=True), [o], [])
 
+    def pick(o, x, pat, op, fill, base, cm):
+        add("g", lambda: g.affine_select(ap(o), ap(x), pat, op, fill, base, cm), [o], [x])
+
     def dma(q, o, x):
         add(q, lambda: eng[q].dma_start(ap(o), ap(x)), [o], [x], dma=True)
 
     sent = [0]
 
-    def send(items, nq):
+    def send(items, nq, behind=()):
         trs = []
         for k, (r, s, d, sem) in enumerate(items):
             dst = T.cores[r]
@@ -166,32 +177,37 @@ def rank_program(g, core, T, topo):
             rid, pid = topo.addr(dst)[:2]
             trs.append(RemoteDMATransfer(dst_ids=[DstId(rid=rid, pnc=pid)], dma_engine_mask=m, remote_sem=T.sem[sem], src=ap(s), dst=ap(d)))
         sent[0] += nq * len(items)
-        add("g", lambda: g.remote_dma_fused(trs, local_sem=T.sem.lsem), [], [it[1] for it in items], ext="send")
+        add("g", lambda: g.remote_dma_fused(trs, local_sem=T.sem.lsem), [], [it[1] for it in items] + list(behind), ext="send")
 
-    def arrive(v, sem, n):
-        add(None, None, [v], [], ext=(sem, n))
+    def fold_min(r, srcs, d, sem, left):
+        dst = T.cores[r]
+        rid, pid = topo.addr(dst)[:2]
+        tr = RemoteDMATransfer(dst_ids=[DstId(rid=rid, pnc=pid)], dma_engine_mask=topo.mask(core, dst), remote_sem=T.sem[sem],
+                               srcs=[ap(s) for s in srcs], dsts=[ap(d)], alu_op=3)
+        n = len(topo.engines(core, dst))
+        add("g", lambda: g.remote_dma_fused([tr], local_sem=T.sem[left]), [], srcs, ext="send", way=FLAT, left=(left, n))
+        arrive(d, sem, n, 0.0)
 
-    bank = ["bank%d" % k for k in range(8)]
+    def arrive(v, sem, n, way=3.0):
+        add(None, None, [v], [], ext=(sem, n), way=way)
+
+    def bk(n, lo=0, hi=512, st=1):
+        return V("bank%d" % n, lo, hi, st)
+
     Ywin = V("Yb", 16, 4112)
-    TAB = 1152
-    lf, gf, pff, m1, c0, m0, c1, l64, kb, zc, thb, bT = [col("pf", k) for k in range(12)]
+    Ib = V("IW", 16, 144)
+    NBw, FCw = V("NB", 0, 1024), V("FC", 0, 1024)
+    names = ("lf gf pff m1 hf par hi8 m0 lo8 hi8s lo8s wpar tc0 c0 c1 kb zc l4 l64 dA dB dC0 dC1 dC2 du0 du1 du2 du3 "
+             "bT0 bT1 bT2 th2 a0 a1 a2 a3").split()
+    P = {n: col("pf", k) for k, n in enumerate(names)}
+    lf, m0, m1 = P["lf"], P["m0"], P["m1"]
 
     dma("s", V("eA"), T.ends0[:])
-    for c in range(4):
-        dma("a", V("eB", 64 * c, 64 * c + 64), T.ends0[:, 1024 * c:1024 * c + 1024])
     dma("a", V("nei"), T.ne0[:])
     iota(col("pi", 0), [[0, 1]], 0, 1)
-    iota(V("IO"), [[1, 160]])
-    iota(V("ML"), [[0, 16], [1, 16]])
+    iota(V("IO"), [[1, 176]], -16)
     iota(V("MG"), [[1, 8], [0, 16]])
-    early[0] = 60.0
-    iota(V("pwa"), [[5, 3], [16, 4], [1024, 4]])
-    iota(V("pwb"), [[0, 3], [16, 16]])
-    iota(V("M64"), [[0, 4], [1, 64]])
-    iota(V("M32"), [[0, 4], [1, 32]])
-    iota(V("DUM", 0, 16), [[0, 2], [16, 8]], 1024)
-    iota(V("DUM", 16, 20), [[16, 4]], 4096)
-    early[0] = 0.0
+    iota(V("ML"), [[0, 16], [1, 16]])
     iota(V("codeX", 0, 128), [[-2, 128]], 512)
     iota(V("codeX", 128, 640), [[-1, 512]], 256)
     iota(V("codeX", 640, 768), [[-2, 128]], -256)
@@ -199,481 +215,347 @@ def rank_program(g, core, T, topo):
     for n in range(4):
         ms(V("EWin", 1024 * n, 1024 * n + 1024), 0.0)
     early[0] = 0.0
-    ts(col("pq", 0), col("pi", 0), 15, None, A.bitwise_and)
-    ts(col("pq", 1), col("pi", 0), 4, None, A.logical_shift_right)
-    ts(col("pq", 3), col("pi", 0), 4, 1, A.logical_shift_right, A.bitwise_and)
-    cp(col("pq", 2), col("pi", 0))
-    cp(V("pf", 0, 4), V("pq", 0, 4))
+    pi = col("pi", 0)
+    ts(col("pq", 0), pi, 15, None, A.bitwise_and)
+    ts(col("pq", 1), pi, 4, None, A.logical_shift_right)
+    cp(col("pq", 2), pi)
+    for c, (sh, m) in enumerate(((4, 1), (1, 7), (0, 1), (3, 1))):
+        ts(col("pq", 3 + c), pi, sh, m, A.logical_shift_right, A.bitwise_and)
+    cp(V("pf", 0, 7), V("pq", 0, 7))
     add("g", lambda: g.indirect_dma_start(ap(col("thi", 0)), None, T.th[:], IndirectOffsetOnAxis(ap=ap(col("pq", 1)), axis=0), bounds_check=7),
         [col("thi", 0)], [col("pq", 1)], dma=True)
-    ts(V("BLK"), V("MG"), gf, None, A.is_equal)
-    ts(V("D"), V("ML"), lf, None, A.is_equal)
-    ts(V("Ib"), V("IO", 0, 128), pff, None, A.is_equal)
     ts(V("UV", 0, 256), V("eA"), 10, None, A.logical_shift_right)
     ts(V("UV", 256, 512), V("eA"), 1023, None, A.bitwise_and)
-    ts(V(bank[2]), V("UV"), 128.0, 640.0, A.max, A.min)
+    ts(bk(2), V("UV"), 128.0, 640.0, A.max, A.min)
     ts(V("cB"), V("UV"), 2.0, -384.0, A.mult, A.add)
     early[0] = 2 * EARLY
-    tt(V("cC"), V("cB"), V(bank[2]), A.subtract)
+    tt(V("cC"), V("cB"), bk(2), A.subtract)
     early[0] = 0.0
     dma("s", V("EWin", 0, 4096, 1, 0, 128, 16), V("cC", 0, 256))
     dma("s", V("EWin", 0, 4096, 1, 1, 128, 16), V("cC", 256, 512))
     dma("s", Ywin, T.y0[:])
-    add("v", lambda: g.vector.tensor_copy(ap(V("Ef")), ap(V("eB"))), [V("Ef")], [V("eB"), V("cB", 0, 2)])
+    cp(V("Ef"), V("eA"))
+    dma("a", V("EF", 0, 4096, 1, 0, 128, 16), V("Ef"))
     cp(V("neu"), V("nei"))
-    for t in range(RO):
-        for i in range(4):
-            act(V("EW", 16 * t + 4 * i, 16 * t + 4 * i + 4), V("Ef", 16 * i + 5 * t, 256, 64))
-    ts(zc, gf, 16.0, 15.0, A.mult, A.add)
-    ts(V("ZS"), V("IO", 0, 144), zc, None, A.is_equal)
-    cp(V("EWi"), V("EW"))
-    ts(V("LUV", 0, 48), V("EWi"), 10, None, A.logical_shift_right)
-    ts(V("LUV", 48, 96), V("EWi"), 1023, None, A.bitwise_and)
-    ts(V("lA"), V("LUV"), 128.0, 640.0, A.max, A.min)
-    ts(V("lB"), V("LUV"), 2.0, -384.0, A.mult, A.add)
-    early[0] = 1.5 * EARLY
-    tt(V("CODE"), V("lB"), V("lA"), A.subtract)
-    early[0] = 0.0
-    send([((rank + 1 + t) % N, V("CODE"), V("PC%d" % t), "qc%d" % t) for t in range(RO)], 4)
-    for t in range(RO):
-        arrive(V("PC%d" % t), "qc%d" % t, 4)
     ms(col("EWin", 4095), 768.0)
+    early[0] = 60.0
+    for n, x, sc, bi in (("m0", "m1", -1.0, 1.0), ("lo8", "hi8", -1.0, 1.0), ("hi8s", "hi8", 2.0 ** -13, 0.0), ("lo8s", "lo8", 2.0 ** -13, 0.0),
+                         ("wpar", "par", 8191.0, 1.0), ("tc0", "lf", 1.0, "pff"), ("zc", "gf", 16.0, 15.0), ("l4", "lf", 4.0, 0.0),
+                         ("a0", "m1", 256.0, 0.0), ("a1", "m0", 256.0, 0.0), ("c0", "l4", "m0", "a0"), ("c1", "l4", "m1", "a1"),
+                         ("kb", "lf", 1024.0, 512.0), ("l64", "lf", 64.0, 0.0), ("dA", "lf", 4.0, 255.0), ("dB", "lf", 4.0, 511.0)):
+        act(P[n], P[x], bias=P.get(bi, bi), scale=P.get(sc, sc))
     for t in range(RO):
-        for i in range(4):
-            act(V("Z%d" % t, 64 * i, 64 * i + 64), V("Yb", 16 + 16 * i + 5 * t, 4112, 64), bias=8.0)
-    act(col("ysave", 0), col("Yb", 4111))
-    send([((rank + 1 + t) % N, V("Z%d" % t), V("PZ%d" % t), "qz%d" % t) for t in range(RO)], 4)
-    for t in range(RO):
-        arrive(V("PZ%d" % t), "qz%d" % t, 4)
-    iota(V("codeT"), [[1, 1024]], -512)
-    iota(V("icol"), [[1, 4], [0, 64]])
-    iota(V("DDT"), [[-16, 4], [-1024, 4], [-64, 16]], 4095)
-    early[0] = EARLY
-    act(V("nI"), V("Ib"), scale=-1.0)
+        act(P["dC%d" % t], lf, bias=3568.0 + 5 * t, scale=64.0)
+    for c in range(4):
+        act(P["du%d" % c], lf, bias=4096.0 + 16 * c)
     early[0] = 0.0
+    ts(V("IW"), V("IO", 0, 160), P["pff"], None, A.is_equal)
+    ts(V("BLK"), V("MG"), P["gf"], None, A.is_equal)
+    ts(V("ZS"), V("IO", 16, 160), P["zc"], None, A.is_equal)
+    for k, (d, m) in enumerate(((16, m0), (0, m0), (32, m1), (16, m1))):
+        act(V("SH%d" % k), V("IW", d, d + 128), scale=m)
+    for t in range(RO):
+        transpose(V("TR", 32 * t, 32 * t + 32), V("cC", 5 * t, 512, 16))
+        for n, k in enumerate((0, 2, 0)):
+            msum(bk(3, 48 * t + 16 * n, 48 * t + 16 * n + 16), [(V("SH%d" % (k + h)), V("TR", 32 * t + 16 * h, 32 * t + 16 * h + 16)) for h in range(2)])
+    early[0] = 1.5 * EARLY
+    for t in range(RO):
+        ts(V("off", 80 * t + 32, 80 * t + 80), bk(3, 48 * t, 48 * t + 48), 512.0, None, A.add)
+    early[0] = 0.0
+    send([((rank + 1 + t) % N, V("off", 80 * t + 48, 80 * t + 80), V("off", 80 * t, 80 * t + 32), "qc%d" % t) for t in range(RO)], 4)
+    for t in range(RO):
+        arrive(V("off", 80 * t, 80 * t + 32), "qc%d" % t, 4)
+    for t in range(RO):
+        act(V("ZZ%d" % t, 0, 256), V("Yb", 16 + 5 * t, 4112, 16), bias=8.0)
+    act(col("ysave", 0), col("Yb", 4111))
 
-    def fe_gather(q, ch):
+    for ch in range(12):
         o, x = V("FG", 1024 * ch, 1024 * ch + 1024), ind(V("EWin"), V("neu", 64 * ch, 64 * ch + 64))
-        if q == "a":
+        if FE[ch] == "a":
             act(o, x)
         else:
             cp(o, x)
-
-    def fe_sum(ch):
-        o = V(bank[ch // 8], 64 * (ch % 8), 64 * (ch % 8) + 64)
-        mmul(o, V("Ib"), V("codeX", 64 * ch, 64 * ch + 64), True, False)
-        for k in range(16):
-            mmul(o, V("ZS", 15 - k, 143 - k), V("FG", 1024 * ch + k, 1024 * ch + 1024, 16), False, k == 15)
-
     for ch in range(12):
-        fe_gather(FE[ch], ch)
-    for ch in range(12):
-        fe_sum(ch)
-    def rsum(o, x):
-        add("v", lambda: g.vector.tensor_reduce(ap(o), ap(x), AxisListType.X, A.add), [o], [x])
+        msum(bk(ch // 8, 64 * (ch % 8), 64 * (ch % 8) + 64), [(Ib, V("codeX", 64 * ch, 64 * ch + 64))]
+             + [(V("ZS", 15 - k, 143 - k), V("FG", 1024 * ch + k, 1024 * ch + 1024, 16)) for k in range(16)])
 
-    ts(V("IW"), V("IO"), -16.0, pff, A.add, A.is_equal)
-    for n in range(3):
-        rsum(col("msk", n), V("D", 5 * n, 5 * n + 5))
-        early[0] = EARLY
-        for pc in range(3):
-            d = 16 - 5 * pc + 5 * n
-            act(V("RP", 128 * (3 * n + pc), 128 * (3 * n + pc) + 128), V("IW", d, d + 128), scale=col("msk", n))
-        early[0] = 0.0
-    for jj in range(5):
-        rsum(col("msk", 3 + jj), V("D", jj, 15, 5))
-        mk = col("msk", 3 + jj)
-        if DELTA and jj > 0:
-            mk = col("msk", 8 + jj)
-            act(mk, col("msk", 2 + jj), bias=col("msk", 3 + jj), scale=-1.0)
-        early[0] = EARLY
-        act(V("BC", 128 * jj, 128 * jj + 128), V("BLK"), scale=mk)
-        early[0] = 0.0
-    early[0] = EARLY
-    act(V("BC", 640, 768), V("BLK"), scale=col("D", 15))
-    for x, c in (("NB", 1.0), ("FC", 1024.0)):
+    early[0] = 40.0
+    ts(V("MK", 0, 8), V("IO", 16, 24), P["hf"], P["wpar"], A.is_equal, A.mult)
+    ts(V("MK", 8, 10), V("IO", 16, 18), lf, None, A.is_equal)
+    for n in range(2):
+        for pc in range(2):
+            d = 16 + 16 * n - pc
+            ts(V("RP%d" % (2 * n + pc)), V("IO", d, d + 128), P["tc0"], P[("lo8", "hi8")[n] + ("", "s")[pc]], A.is_equal, A.mult)
+    for jj in range(8):
+        act(V("BT%d" % jj), V("BLK"), scale=col("MK", jj))
+    for j in range(2):
+        act(V("BC%d" % j), V("BLK"), scale=col("MK", 8 + j))
+    act(V("nI"), Ib, scale=-1.0)
+    for x, c in (("NB", 1.0), ("FC", 0.0)):
         ms(V(x, 1, 256, 2), c)
         ms(V(x, 769, 1024, 2), c)
-        ms(V(x, 1024, TAB), c)
-    early[0] = 0.0
     SEG = [(0, 128, 0, 256, 2), (128, 640, 256, 768, 1), (640, 768, 768, 1024, 2)]
     for (x0, x1, a0, a1, st) in SEG:
         ts(V("NB", a0, a1, st), V("nei", x0, x1), -1.0, 4095.0, A.mult, A.add)
+    for n, x, sc in (("BL256", "BLK", 256.0), ("BLn256", "BLK", -256.0), ("BL4096", "BLK", 4096.0), ("BL8k", "BLK", 8192.0), ("BLn8k", "BLK", -8192.0)):
+        act(V(n), V(x), scale=sc)
+    for n, sc in (("If", 1.0), ("Is", 2.0 ** -27), ("Ik", 1024.0), ("In8k", -8192.0)):
+        act(V(n), Ib, scale=sc)
+    ms(V("PC", 0, 128), -4096.0)
+    ms(V("PC", 128, 256), -3072.0)
+    ms(V("cm128"), -128.0)
+    ms(V("CW", 256, 272), float(1 << 24))
     ms(V("Yb", 0, 16), 128.0)
-    ms(V("Yb", 4111, 4176), 128.0)
-
+    ts(V("PEN16"), V("ML"), lf, PEN, A.not_equal, A.mult)
+    act(V("RB16"), V("ML", 0, 192), bias=BIG / 2, scale=-BIG)
+    early[0] = 0.0
+    ms(col("Yb", 4111), 128.0)
+    act(V("FC", 0, 256, 2), bk(0, 0, 128), AF.Relu, bias=1024.0, scale=-1.0)
+    act(V("FC", 256, 640), bk(0, 128, 512), AF.Relu, bias=1024.0, scale=-1.0)
+    act(V("FC", 640, 768), bk(1, 0, 128), AF.Relu, bias=1024.0, scale=-1.0)
+    act(V("FC", 768, 1024, 2), bk(1, 128, 256), AF.Relu, bias=1024.0, scale=-1.0)
+    send([((rank + 1 + t) % N, V("ZZ%d" % t, 0, 256), V("ZZ%d" % t, 256, 512), "qz%d" % t) for t in range(RO)], 4, [FCw])
     for t in range(RO):
-        for n, (x, o) in enumerate((("PC%d" % t, 0), ("CODE", 0), ("PC%d" % t, 48), ("CODE", 48))):
-            act(V("CB", 64 * t + 16 * n, 64 * t + 16 * n + 16), V(x, o + 16 * t, o + 16 * t + 16))
-    ts(V("off", 0, 64), V("CB", 0, 64), 512.0, None, A.add)
-    ts(V("off", 64, 192), V("CB", 64, 192), 512.0, None, A.add)
-    ts(V("FC", 0, 256, 2), V(bank[0], 0, 128), 1024.0, None, A.min)
-    ts(V("FC", 256, 640), V(bank[0], 128, 512), 1024.0, None, A.min)
-    ts(V("FC", 640, 768), V(bank[1], 0, 128), 1024.0, None, A.min)
-    ts(V("FC", 768, 1024, 2), V(bank[1], 128, 256), 1024.0, None, A.min)
+        arrive(V("ZZ%d" % t, 256, 512), "qz%d" % t, 4)
 
-    def late_consts_v():
-        act(m0, m1, bias=1.0, scale=-1.0)
-        act(c0, m1, scale=256.0)
-        act(c1, m1, bias=256.0, scale=-256.0)
-        act(l64, lf, scale=65536.0)
-        act(kb, lf, bias=512.0, scale=1024.0)
-        ts(bT, col("thi", 0), -4.0, 0.5, A.mult, A.add)
-        act(thb, bT, bias=2048.0)
-        act(col("Acc", 0), lf, scale=0.0)
-        act(V("cm128"), V("IO", 0, 64), bias=-128.0, scale=0.0)
-        act(V("CW", 256, 272), V("IO", 0, 16), bias=float(1 << 24), scale=0.0)
-        act(V("DUM"), V("DUM"), bias=lf)
-        act(V("pw", 0, 48), V("pwa"), bias=l64, scale=1024.0)
-        act(V("pw", 144, 192), V("pwb"), bias=lf)
-        act(V("pw", 48, 96), V("pw", 144, 192), bias=512.0, scale=1024.0)
-        act(V("pw", 96, 144), V("CODE", 0, 48), bias=512.0 * 1025, scale=1024.0)
-        act(V("pw", 192, 240), V("CODE", 48, 96))
-        act(V("pw", 240, 288), V("CODE", 48, 96))
-        tt(V("pw", 0, 144), V("pw", 0, 144), V("pw", 144, 288), A.add)
-        act(V("PW"), V("ML", 0, 192), scale=0.0)
-        for t in range(RO):
-            for o, x in ((0, 48), (32, 96), (48, 0)):
-                act(V("PW", 64 * t + o, 64 * t + o + 16), V("pw", x + 16 * t, x + 16 * t + 16))
-        ts(V("km", 0, 128), V("ML", 0, 128), lf, None, A.is_gt)
-        tt(V("TRI"), V("km", 0, 128), V("BLK"), A.mult)
-        tt(V("FST"), V("Ib"), V("TRI"), A.subtract)
-        act(V("R16"), V("ML"), AF.Sign)
-        act(V("R64"), V("M64"), AF.Sign)
+    def late_consts():
+        iota(V("M4"), [[0, 4], [1, 16], [0, 4]])
+        iota(V("icolK"), [[64, 4], [0, 16], [1, 4]])
+        iota(V("M64"), [[0, 4], [1, 64]])
+        iota(V("M32"), [[0, 4], [1, 32]])
+        iota(V("CE"), [[0, 4], [8192, 2], [0, 32]], -8704)
+        iota(V("icol2"), [[0, 2], [1, 256]])
+        iota(V("codeT"), [[1, 1024]], -512)
+        iota(V("numT", 0, 256), [[1, 128], [0, 2]])
+        iota(V("numT", 256, 768), [[1, 512]], 128)
+        iota(V("numT", 768, 1024), [[1, 128], [0, 2]], 640)
+        ts(V("PENK"), V("M4"), lf, PEN, A.not_equal, A.mult)
+        act(V("RB64"), V("M64"), bias=BIG / 2, scale=-BIG)
         act(V("CAPS"), V("M32"), AF.Relu, bias=float(CAP), scale=-float(CAP))
-        act(V("M64"), V("M64"), AF.Sign, bias=31.5, scale=-1.0)
-        act(V("CE"), V("M64"), AF.Relu, scale=8192.0)
-
-    def early_consts_a():
-        act(V("BLm4"), V("BLK"), scale=-4.0)
-        act(V("BL4"), V("BLK"), scale=4.0)
-        act(V("BLz"), V("BLK"), scale=4.0 * KDS[0])
-        act(V("BLx"), V("BLK"), scale=4.0 * KO[0])
-        act(V("BLy"), V("BLK"), scale=4.0 * KO[1])
-        act(V("If"), V("Ib"))
-        act(V("Is"), V("Ib"), scale=-2.0 ** -27)
-        act(V("Ik"), V("Ib"), scale=1024.0)
-
-    def late_consts_a():
-        act(V("BLT"), V("BLK"), scale=8192.0)
-        act(V("BLn"), V("BLK"), scale=-8192.0)
-        act(V("TRT"), V("TRI"), scale=8192.0)
+        pick(V("TRn"), V("BLn8k"), [[1, 128]], A.is_gt, 0.0, 0, -1)
+        act(V("T1"), V("TRn"), scale=2.0 ** -13)
+        pick(V("FST"), V("T1"), [[1, 128]], A.not_equal, 1.0, 0, -1)
         act(V("FS4"), V("FST"), scale=4096.0)
+        ts(P["bT0"], col("thi", 0), -256.0, 30.0, A.mult, A.add)
+        act(P["th2"], P["bT0"], bias=65536.0)
 
-    early_consts_a()
+    late_consts()
 
-    tm_, mx_, eq_, sel, f1 = 80, 160, 224, 288, 352
-    qw = lambda a, b, st=1: V("en", a, b, st)
-    has, go, ngo, gE = V("en", 16, 20), V("en", 20, 24), V("en", 24, 28), V("en", 28, 32)
-    oC, oH, oD, oA, oE, oQ, oS = [V("ou", a, b) for a, b in ((0, 8), (8, 24), (28, 36), (36, 40), (40, 44), (44, 60), (64, 84))]
+    def spread_z(t):
+        for k in range(16):
+            pick(V("zr%d" % (t % 2), k, None, 16), V("ZZ%d" % t, X0, X1), [[0, X1 - X0]], A.is_ge, 0.0, 0, 0)
 
-    def book_keeping(t):
-        if t < RO - 1:
-            mmul(V(bank[4], 0, 2), V("BLK"), V("goB", 0, 2), True, False)
-            mmul(V(bank[4], 0, 2), V("BLK"), V("goB", 2, 4), False, True)
-            act(col("Acc", 1), col(bank[4], 0), bias=col("Acc", 0))
-            act(col("Acc", 0), col(bank[4], 1), bias=col("Acc", 1))
-            act(col("Acc", 2), col("Acc", 0), AF.Sign, bias=-63.5)
-            act(col("Acc", 3), col("Acc", 0), AF.Sign, bias=-127.5)
-            act(col("Acc", 4), col("Acc", 0), bias=thb, scale=-32.0)
-            act(col("Acc", 5), col("Acc", 2), bias=col("Acc", 4), scale=1024.0)
-            act(bT, col("Acc", 3), bias=col("Acc", 5), scale=1024.0)
-        for c in range(4):
-            act(V("en", 80 + c, 96, 4), V("en", 64 + c, 80, 4), scale=col("en", 20 + c))
-        mmul(V(bank[6], 0, 16), V("If"), V("en", 80, 96), True, False)
-        mmul(V(bank[6], 0, 16), V("If"), V("EW", 16 * t, 16 * t + 16), False, True)
-        for i in range(4):
-            act(V("Ef", 16 * i + 5 * t, 256, 64), V(bank[6], 4 * i, 4 * i + 4))
-
-    def new_ends(t):
-        ts(V("en", 32, 40), qw(0, 8), -256.0, 256.0, A.max, A.min)
-        tt(V("en", 40, 48), qw(0, 8), V("en", 32, 40), A.add)
-        tt(V("en", 48, 52), V("en", 40, 48, 2), V("en", 41, 48, 2), A.min)
-        tt(V("en", 52, 56), V("en", 40, 48, 2), V("en", 41, 48, 2), A.max)
-        act(V("en", 56, 60), V("en", 48, 52), bias=393600.0, scale=512.0)
-        act(V("en", 60, 64), V("en", 52, 56), scale=0.5)
-        for c in range(4):
-            act(col("en", 28 + c), col("en", 56 + c), bias=col("en", 60 + c))
-        for c in range(4):
-            act(V("en", 96 + c, 112, 4), V("EW", 16 * t + c, 16 * t + 16, 4), bias=col("en", 28 + c), scale=-1.0)
-        tt(V("en", 64, 80), V("en", 96, 112), V("sm", eq_ + 32, eq_ + 48), A.mult)
-
-    def ya_gather(h, q, n=1):
-        c = 256 * h + 64 * q
-        act(V("ya", 16 * c, 16 * (c + 64 * n)), ind(Ywin, V("aU", c, c + 64 * n)))
-
-    def yc_gather(h, q, n=1):
-        c = 256 * h + 64 * q
-        tt(V("mm", 16 * c, 16 * (c + 64 * n)), ind(V("Yb", 0, 4112), V("cU", c, c + 64 * n)), V("ya", 16 * c, 16 * (c + 64 * n)), A.max)
-
+    oC, oE, oD, oN, oQ, oA, oS = 0, 8, 12, 20, 36, 52, 56
+    ou = lambda a, n, st=1: V("ou", a, a + n, st)
+    si = lambda a: V("si", a, a + 4)
     rot = [0]
+    spread_z(0)
 
     for t in range(RO):
         last = t == RO - 1
-        oU, oV = V("off", 64 * t, 64 * t + 32), V("off", 64 * t + 32, 64 * t + 64)
-        z = [V("PZ%d" % t), V("Z%d" % t)]
-        act(V("nbh"), ind(V("NB"), oV))
-        early[0] = BOOST * (t > 0)
-        ts(V("aU", 0, 64), ind(V("NB"), V("off", 64 * t, 64 * t + 4)), -1.0, 4095.0, A.mult, A.add)
-        early[0] = 0.0
-        ts(V("aU", 64, 512), ind(V("NB"), V("off", 64 * t + 4, 64 * t + 32)), -1.0, 4095.0, A.mult, A.add)
-        tt(V("nbl"), ind(V("NB"), oV), V("nbh"), A.subtract)
-        act(V("fS"), ind(V("FC"), oV), scale=-8192.0)
-        if SSQ == "v":
-            ts(V("sS"), ind(V("FC"), oU), -8192.0, None, A.mult)
-        else:
-            act(V("sS"), ind(V("FC"), oU), scale=-8192.0)
-        early[0] = BOOST2 * (t > 0)
-        ya_gather(0, 0)
-        early[0] = 0.0
-        if t == 0:
-            early[0] = -10.0
-            late_consts_v()
-            early[0] = 0.0
-        else:
-            new_ends(t - 1)
-            book_keeping(t - 1)
-        for n in range(3):
-            b = V(bank[5 + n])
-            early[0] = -TLATE * n
-            for pc, x in enumerate(("nbh", "nbl", "fS")):
-                mmul(b, V("RP", 128 * (3 * n + pc), 128 * (3 * n + pc) + 128), V(x), pc == 0, pc == 2)
-            if TILE[n] == "v":
-                cp(V("PT", 512 * n, 512 * n + 512), b)
-            else:
-                act(V("PT", 512 * n, 512 * n + 512), b)
-        early[0] = 0.0
+        o0 = 80 * t
+        ZZ = "ZZ%d" % t
+        z = [V(ZZ, 256, 512), V(ZZ, 0, 256)]
+        sS, fV = V("FS", 256, 768), [V("FS", 0, 256), V("FS", 768, 1024)]
+        act(V("FS"), ind(FCw, V("off", o0, o0 + 64)), bias=8192.0 * 1024, scale=-8192.0)
+        ts(V("aU", 0, 64), ind(NBw, V("off", o0 + 16, o0 + 20)), -1.0, 4095.0, A.mult, A.add)
+        for h in range(2):
+            ts(V("bV", 256 * h, 256 * h + 256), ind(NBw, V("off", o0 + 48 * h, o0 + 48 * h + 16)), -2048.0, None, A.add)
+        ts(V("aU", 64, 512), ind(NBw, V("off", o0 + 20, o0 + 48)), -1.0, 4095.0, A.mult, A.add)
+
+        def ya_gather(c):
+            act(V("ya", 16 * c, 16 * c + 1024), ind(Ywin, V("aU", c, c + 64)))
+
+        def yc_gather(c):
+            tt(V("mm", 16 * c, 16 * c + 1024), ind(V("Yb", 0, 4112), V("cU", c, c + 64)), V("ya", 16 * c, 16 * c + 1024), A.max)
+
+        ya_gather(0)
+        for n in range(2):
+            mmul(bk(6 + n), V("RP%d" % (2 * n)), V("bV"), True, False)
+            for h in range(2):
+                mmul(bk(6 + n, 256 * h, 256 * h + 256), V("RP%d" % (2 * n + 1)), fV[h], False, h == 1)
+            cp(V("PT", 512 * n, 512 * n + 512), bk(6 + n))
         for j in range(16):
-            b = V(bank[(0, 1, 2, 3, 5, 6, 7)[j % 7]])
-            if DELTA and j > 0:
-                jj, n = divmod(j - 1, 3)
-                b, w = V(bank[n]), V(bank[5 + (j + 1) % 3])
-                if jj == 0:
-                    mmul(b, V("nI"), V("sS"), True, False)
-                mmul(b, V("BC", 128 * jj, 128 * jj + 128), V("PT", 512 * n, 512 * n + 512), False, jj == 4)
-                act(w, b, AF.Abs)
-                tt(V("acc"), w, V("acc"), A.min)
-                continue
-            if DELTA:
-                b = V(bank[4])
-            if j == 0:
-                bc = V("BC", 640, 768)
-                mmul(b, bc, V("nbh"), True, False)
-                mmul(b, bc, V("nbl"), False, False)
-                mmul(b, bc, V("fS"), False, False)
-                early[0] = BOOST3
-                mmul(b, V("nI"), V("sS"), False, True)
-                early[0] = 0.0
+            bn = (0, 1, 2, 3, 6, 7)[j % 6]
+            b = bk(bn)
+            mmul(b, V("nI"), sS, True, False)
+            if j < 2:
+                mmul(b, V("BC%d" % j), V("bV"), False, False)
+                for h in range(2):
+                    mmul(bk(bn, 256 * h, 256 * h + 256), V("BC%d" % j), fV[h], False, h == 1)
             else:
-                n, jj = divmod(j - 1, 5)
-                mmul(b, V("nI"), V("sS"), True, False)
-                mmul(b, V("BC", 128 * jj, 128 * jj + 128), V("PT", 512 * n, 512 * n + 512), False, True)
+                mmul(b, V("BT%d" % (j % 8)), V("PT", 512 * (j // 8), 512 * (j // 8) + 512), False, True)
             ac = V("acc" if j % 2 == 0 else "acd")
             if j < 2:
-                act(ac, b, AF.Abs)
+                act(ac, b, AF.Abs, bias=2048.0)
             else:
-                act(b, b, AF.Abs)
-                tt(V(bank[4]) if j == 15 else ac, b, ac, A.min)
+                act(b, b, AF.Abs, bias=2048.0)
+                tt(bk(4) if j == 15 else ac, b, ac, A.min)
         for h in range(2):
-            tt(V("acc", 256 * h, 256 * h + 256), V(bank[4], 256 * h, 256 * h + 256), V("acc", 256 * h, 256 * h + 256), A.min)
-        for h in range(2):
+            tt(V("acc", 256 * h, 256 * h + 256), bk(4, 256 * h, 256 * h + 256), V("acc", 256 * h, 256 * h + 256), A.min)
             ts(V("cU", 256 * h, 256 * h + 256), V("acc", 256 * h, 256 * h + 256), -1.0, 4111.0, A.mult, A.add)
-        mmul(V(bank[3], 0, 256), V("Ib"), z[0], True, True, V("cU", 0, 2))
-        mmul(V(bank[3], 256, 512), V("Ib"), z[1], True, True)
-        def min_half(sub, stop):
-            o = V(bank[5], 128 * sub, 128 * sub + 128)
-            for k in range(KO[sub]):
-                r0 = 4096 + 2048 * sub + 128 * k
-                tt(V("mz", r0, r0 + 128), V(bank[3], 256 + 128 * sub, 384 + 128 * sub), V("mm", 4096 + 2048 * sub + k, 6144 + 2048 * sub, 16), A.min)
-                if stop and k == KO[sub] - LATE:
-                    relu_sum(1, 1, False)
-                mmul(o, V("BLm4"), V("mz", r0, r0 + 128), False, stop and k == KO[sub] - 1)
+        for n in range(2):
+            mmul(bk(5, 256 * n, 256 * n + 256), V("BC%d" % (1 - n)), V("EWin", 5 * t, 4096, 16), True, True)
+        act(V("TT"), bk(5))
+        mmul(bk(3, X0, 256), Ib, V(ZZ, X0, 256), True, True)
 
-        def relu_part(h, sub):
-            c = 256 * h + 128 * sub
-            KA = list(range(KO[sub] if h else KDS[0], 16))
-            for k0 in range(0, len(KA), 4):
-                ks = KA[k0:k0 + 4]
-                bn = bank[rot[0] % 3]
+        def score(a, n, e, stop):
+            c = 256 + a
+            o = bk(5, a, a + n)
+            za = V(ZZ, a, a + n)
+            if e == "v":
+                x = 16 * (a - X0)
+                tt(V("m15", a, a + n), bk(3, a, a + n), V("mm", 16 * c + 15, 16 * (c + n), 16), A.min)
+                ms(V("mm", 16 * c + 15, 16 * (c + n), 16), 0.0)
+                scan(V("mz", x, x + 16 * n), V("zr%d" % (t % 2), x, x + 16 * n), V("mm", 16 * c, 16 * (c + n)))
+                mmul(o, V("BL4096"), za, False, False)
+                mmul(o, V("BLn256"), V("m15", a, a + n), False, False)
+                for k in range(15):
+                    mmul(o, V("BLn256"), V("mz", x + k, x + 16 * n, 16), False, stop and k == 14)
+                return
+            per = 512 // n
+            r0 = 16 * a
+            for k0 in range(0, 16, per):
+                bn = rot[0] % 3
                 rot[0] += 1
-                for n, k in enumerate(ks):
-                    o = V(bn, 128 * n, 128 * n + 128)
-                    mmul(o, V("Ib"), V(z[h][0], 128 * sub, 128 * sub + 128), True, False)
-                    mmul(o, V("nI"), V("mm", 16 * c + k, 16 * (c + 128), 16), False, True)
-                r0 = 4096 * h + 2048 * sub + 128 * k0
-                act(V("rl", r0, r0 + 128 * len(ks)), V(bn, 0, 128 * len(ks)), AF.Relu)
+                for k in range(per):
+                    msum(bk(bn, n * k, n * k + n), [(Ib, za), (V("nI"), V("mm", 16 * c + k0 + k, 16 * (c + n), 16))])
+                act(V("EQ", r0 + n * k0, r0 + n * k0 + 512), bk(bn), AF.Relu)
+            for k in range(16):
+                mmul(o, V("BL256"), V("EQ", r0 + n * k, r0 + n * k + n), False, stop and k == 15)
 
-        def relu_sum(h, sub, stop):
-            for n in range(16 - (KO[sub] if h else KDS[0])):
-                r0 = 4096 * h + 2048 * sub + 128 * n
-                mmul(V(bank[4 + h], 128 * sub, 128 * sub + 128), V("BL4"), V("rl", r0, r0 + 128), False, stop and n == 15 - KDS[h])
-
-        def min_part(h):
-            for k in range(KDS[h]):
-                o = V("mz", 4096 * h + 256 * k, 4096 * h + 256 * k + 256)
-                tt(o, V(bank[3], 256 * h, 256 * h + 256), V("mm", 4096 * h + k, 4096 * h + 4096, 16), A.min)
-
-        def min_sum(h, k0, k1):
-            for k in range(k0, k1):
-                mmul(V(bank[4 + h], 0, 256), V("BLm4"), V("mz", 4096 * h + 256 * k, 4096 * h + 256 * k + 256), False, False)
-
-        ya_gather(0, 1)
-        yc_gather(0, 0)
-        ya_gather(0, 2)
-        yc_gather(0, 1)
-        ya_gather(0, 3)
-        mmul(V(bank[4], 0, 256), V("BLz"), z[0], True, False)
-        yc_gather(0, 2)
-        relu_part(0, 0)
-        ya_gather(1, 0)
-        yc_gather(0, 3)
-        relu_sum(0, 0, False)
-        relu_part(0, 1)
-        min_part(0)
-        min_sum(0, 0, KDS[0])
-        relu_sum(0, 1, True)
-        ya_gather(1, 1)
-        act(V("PS%d" % t), V(bank[4], 0, 256))
-        send([((rank - 1 - t) % N, V("PS%d" % t), V("PK%d" % t), "qk%d" % t)], 8)
-        arrive(V("PK%d" % t), "qk%d" % t, 8)
-        yc_gather(1, 0)
-        ya_gather(1, 2)
-        yc_gather(1, 1)
-        ya_gather(1, 3)
-        mmul(V(bank[5], 0, 256), V("Ib"), V("icol"), True, False)
-        mmul(V(bank[5], 0, 128), V("BLx"), V(z[1][0], 0, 128), False, False)
-        mmul(V(bank[5], 128, 256), V("BLy"), V(z[1][0], 128, 256), False, False)
-        min_half(0, False)
-        yc_gather(1, 2)
-        relu_part(1, 0)
-        act(V("vS"), ind(V("codeT"), V("off", 64 * t + 48, 64 * t + 64)), scale=-8192.0)
+        for a, n in PART:
+            for c in range(a, a + n, 64):
+                if c > 0:
+                    ya_gather(c)
+                yc_gather(c)
+            x, y = 16 * (256 + a - X0), 4096 * t + 16 * a
+            fold_min((rank - 1 - t) % N, [V("zr%d" % (t % 2), x, x + 16 * n), V("mm", 16 * a, 16 * (a + n))], V("FG", y, y + 16 * n),
+                     ("qm", "qk")[a == 0] + str(t), ("lm", "lk")[a == 0] + str(t))
+        if not last:
+            spread_z(t + 1)
+        mmul(bk(5, 0, 256), Ib, V("icolK"), True, False)
+        mmul(bk(5, 0, 256), Ib, V("PENK"), False, False)
+        for c in range(256, 512, 64):
+            ya_gather(c)
         act(V("pc"), V("acc", 256, 512), AF.Relu, bias=4096.0, scale=-1.0)
-        yc_gather(1, 3)
-        mmul(V(bank[7], 0, 256), V("Ib"), V("sS", 256, 512), True, False)
-        mmul(V(bank[7], 0, 256), V("nI"), V("vS"), False, True)
-        for k in range(16):
-            mmul(V(bank[6], 0, 256), V("ZS", 15 - k, 143 - k), V("ya", 4096 + k, 8192, 16), k == 0, False)
-        mmul(V(bank[6], 0, 256), V("Is"), V("sS", 256, 512), False, False)
-        mmul(V(bank[6], 0, 256), V("Ik"), V("pc"), False, False)
-        relu_sum(1, 0, False)
-        mmul(V(bank[5], 0, 256), V("If"), V("PK%d" % t), False, False)
-        act(V(bank[7], 0, 256), V(bank[7], 0, 256), AF.Abs)
-        relu_part(1, 1)
-        min_half(1, True)
-        act(V("pv"), V(bank[7], 0, 256), AF.Relu, bias=4096.0, scale=-1.0)
-        mmul(V(bank[6], 0, 256), V("Ik"), V("pv"), False, True)
-        act(V("CW", 0, 256), V(bank[6], 0, 256), bias=kb, scale=16384.0)
-        if t == 0:
-            late_consts_a()
-        tt(V("km"), V(bank[5], 0, 256), V("D"), A.mult)
-        act(V("sg"), V(bank[5], 0, 256), AF.Sign, bias=bT)
-        scan(V("ks"), V("R16"), V("km"), A.mult, A.add)
-        kw = V("ks", 15, 256, 16)
-        cp(V("sm", 0, 16), kw)
-        cp(V("sm", 16, 32), kw)
-        ts(V("sm", 32, 48), kw, -1.0, None, A.mult)
-        act(V("sm", 48, 64), kw, scale=-1.0)
-        act(V("sm", 64, 80), kw, scale=-1.0)
-        mmul(V(bank[0], 0, 256), V("Ib"), z[1], True, False)
-        mmul(V(bank[0], 0, 256), V("Ib"), V("sg"), False, True)
-        mmul(V(bank[7], 0, 256), V("Ib"), V("CE"), True, False)
-        act(V("r1"), V(bank[0], 0, 256), AF.Relu, bias=71.0, scale=-1.0)
-        for i in range(4):
-            act(V("Yb", 16 + 16 * i + 5 * t, 4112, 64), V("r1", 64 * i, 64 * i + 64), AF.Relu, bias=63.0, scale=-1.0)
+        msum(bk(7, 0, 256), [(Ib, V("FS", 512, 768)), (V("In8k"), V("TT", 0, 256))])
+        act(bk(7, 0, 256), bk(7, 0, 256), AF.Abs)
+        act(V("pv"), bk(7, 0, 256), AF.Relu, bias=4096.0, scale=-1.0)
+        mmul(bk(6, 0, 256), V("Is"), V("FS", 512, 768), True, False)
+        for c in range(0, 256, 64):
+            for k in range(16):
+                mmul(bk(6, c, c + 64), V("ZS", 15 - k, 143 - k), V("ya", 4096 + 16 * c + k, 5120 + 16 * c, 16), False, False)
+        mmul(bk(6, 0, 256), V("Ik"), V("pc"), False, False)
+        mmul(bk(6, 0, 256), V("Ik"), V("pv"), False, True)
+        act(V("CW", 0, 256), bk(6, 0, 256), bias=P["kb"], scale=16384.0)
+        mmul(bk(5, 0, 256), V("BL4096"), z[1], False, False)
+        for a, n in PART:
+            for k in range(16):
+                mmul(bk(5, a, a + n), V("BLn256"), V("FG", 4096 * t + 16 * a + k, 4096 * t + 16 * (a + n), 16), False, False)
+        for m, (a, n, e) in enumerate(OWN):
+            for c in range(a, a + n, 64):
+                yc_gather(256 + c)
+            score(a, n, e, m == len(OWN) - 1)
+        scan(V("ke"), V("RB64"), bk(5, 0, 256))
+        act(V("KA"), bk(5, 0, 256), AF.Abs, bias=KTOP, scale=-1.0)
+        act(V("sg"), bk(5, 0, 256), AF.Sign, bias=P["bT%d" % t])
+        le, ld, xi, sc, k1, e16, kk = si(4), si(12), si(16), si(20), si(24), si(28), si(32)
+        cp(si(0), V("ke", 63, 256, 64))
+        ts(le, si(0), 255, None, A.bitwise_and)
+        ts(ou(oC, 8, 2), le, m0, P["c0"], A.mult, A.add)
+        ts(ou(oC + 1, 7, 2), le, m1, P["c1"], A.mult, A.add)
+        act(V("G1"), ind(V("CW"), ou(oC, 8)))
+        ts(ou(oE, 4), le, P["l4"], None, A.add)
+        scan(V("kd"), V("RB64"), V("KA"))
+        cp(si(8), V("kd", 63, 256, 64))
+        ts(ld, si(8), 255, None, A.bitwise_and)
+        ts(ou(oD, 4), ld, -1.0, P["dA"], A.mult, A.add)
+        ts(ou(oD + 4, 4), ld, -1.0, P["dB"], A.mult, A.add)
+        ts(V("NM", 16, 20), ld, -16.0, P["dC%d" % t], A.mult, A.add)
+        act(V("Q3"), ind(V("TT"), ou(oE, 12)))
+        msum(bk(1, 0, 192), [(Ib, V("PEN16", 0, 192)), (Ib, V("Q3"))])
+        transpose(V("G2"), V("G1"))
+        scan(V("G3"), V("CAPS"), V("G2"))
+        cp(xi, V("G3", 31, 128, 32))
+        ts(sc, xi, 1023, None, A.bitwise_and)
+        scan(V("k3"), V("RB16"), bk(1, 0, 192))
+        for sl in range(3):
+            ts(ou(oQ + 1 + sl, 15 - sl, 4), V("k3", 64 * sl + 15, 64 * sl + 64, 16), 512.0, None, A.add)
+        cp(ou(oQ, 16, 4), sc)
+        act(V("Q"), ind(V("codeT"), ou(oQ, 16)))
+        cp(ou(oN, 4), sc)
+        ts(ou(oN + 4, 12), V("k3", 15, 192, 16), 512.0, None, A.add)
+        ts(V("NM", 0, 4), sc, -512.0, None, A.add)
+        act(V("NM", 4, 16), V("k3", 15, 192, 16))
+        act(V("has", 0, 4), V("G3", 31, 128, 32), AF.Relu, bias=1009.0 * 16384, scale=-1.0)
+        if EQA:
+            act(V("has", 4, 8), V("has", 0, 4), AF.Sign)
+            act(col("has", 8), col("has", 7), scale=-1.0)
+            for sl in range(4):
+                act(V("EA", 64 * sl, 64 * sl + 64), V("Q", 192, 256), AF.Abs, bias=col("NM", 4 * sl + 3), scale=-1.0)
+            act(V("EQ", 0, 256), V("EA"), AF.Relu, bias=col("has", 7), scale=col("has", 8))
+        msum(bk(0, 0, 256), [(Ib, z[1]), (V("BLK"), V("sg"))])
+        act(V("r1"), bk(0, 0, 256), AF.Relu, bias=86.0, scale=-1.0)
+        act(V("Yb", 16 + 5 * t, 4112, 16), V("r1"), AF.Relu, bias=63.0, scale=-1.0)
         if last:
             act(col("Yb", 4111), col("ysave", 0))
-        tt(V("sm", tm_, tm_ + 76), V("sm", 0, 76), V("sm", 4, 80), A.min)
-        tt(V("sm", mx_, mx_ + 64), V("sm", tm_, tm_ + 64), V("sm", tm_ + 8, tm_ + 72), A.min)
-        tt(V("sm", eq_, eq_ + 64), V("sm", 0, 64), V("sm", mx_, mx_ + 64), A.is_equal)
-        tt(V("sm", sel, sel + 64), V("sm", eq_, eq_ + 64), V("PW", 64 * t, 64 * t + 64), A.mult)
-        tt(V("sm", f1, f1 + 56), V("sm", sel, sel + 56), V("sm", sel + 8, sel + 64), A.add)
-        tt(V("f2"), V("sm", f1, f1 + 52), V("sm", f1 + 4, f1 + 56), A.add)
-        ecol, kk, xi, k1, e16 = V("NM", 32, 36), V("NM", 28, 32), V("si", 0, 4), V("si", 4, 8), V("si", 8, 12)
-        ts(ecol, V("f2", 0, 4), 10, None, A.logical_shift_right)
-        ts(V("ou", 0, 8, 2), ecol, m0, c0, A.mult, A.add)
-        ts(V("ou", 1, 8, 2), ecol, m1, c1, A.mult, A.add)
-        act(V("G1"), ind(V("CW"), oC))
-        ts(V("NM", 1, 8, 2), V("f2", 0, 4), 1023, None, A.bitwise_and)
-        ts(V("NM", 8, 16, 2), V("f2", 32, 36), 10, None, A.logical_shift_right)
-        ts(V("NM", 9, 16, 2), V("f2", 32, 36), 1023, None, A.bitwise_and)
-        add("v", lambda: g.vector.transpose(ap(V("G2")), ap(V("G1"))), [V("G2")], [V("G1")])
-        ts(V("NM", 20, 28, 2), V("f2", 48, 52), 1023, None, A.bitwise_and)
-        ts(V("NM", 21, 28, 2), V("f2", 48, 52), 1023, None, A.bitwise_and)
-        ts(V("NM", 16, 20), V("f2", 48, 52), 10, None, A.logical_shift_right)
-        ts(e16, V("f2", 0, 4), 6, 4080, A.logical_shift_right, A.bitwise_and)
-        scan(V("G3"), V("CAPS"), V("G2"), A.max, A.min)
-        cp(V("ou", 45, 60, 4), V("NM", 1, 8, 2))
-        cp(xi, V("G3", 31, 128, 32))
-        cp(V("ou", 46, 60, 4), V("NM", 8, 16, 2))
-        ts(V("NM", 0, 8, 2), xi, 1023, None, A.bitwise_and)
-        cp(V("ou", 47, 60, 4), V("NM", 9, 16, 2))
-        cp(V("ou", 44, 60, 4), V("NM", 0, 8, 2))
-        act(has, V("G3", 31, 128, 32), AF.Relu, bias=1009.0 * 16384, scale=-1.0)
-        act(V("Q"), ind(V("codeT"), oQ))
-        ts(k1, xi, 10, 15, A.logical_shift_right, A.bitwise_and)
-        tt(kk, k1, e16, A.add)
-        cp(V("ou", 8, 44), V("NM"))
-        act(V("GN"), ind(V("NB"), oH))
-        ts(qw(0, 16), V("NM", 0, 16), -512.0, None, A.add)
+        act(V("GN"), ind(NBw, ou(oN, 16)))
+        act(V("dd"), ind(V("icol2"), ou(oD, 8)), bias=4095.0 - 5 * t, scale=-16.0)
         act(V("emp"), V("GN", 0, 128), AF.Relu, bias=1.0, scale=-1.0)
-        act(V("dd"), ind(V("DDT"), oD), bias=-5.0 * t)
-        mmul(V(bank[1], 0, 128), V("FST"), V("emp"), True, True)
-        mmul(V(bank[2], 0, 128), V("FS4"), V("emp"), True, False)
-        mmul(V(bank[2], 0, 128), V("If"), V("dd"), False, True)
-        act(V("ins"), V(bank[1], 0, 128), AF.Relu)
-        act(V("t2"), V(bank[2], 0, 128), AF.Relu, bias=-4096.0)
+        mmul(bk(2, 0, 128), V("FST"), V("emp"), True, True)
+        act(V("ins"), bk(2, 0, 128), AF.Relu)
+        for h in range(2):
+            mmul(bk(4, 128 * h, 128 * h + 128), V("If"), V("dd"), True, True)
+        tt(V("rd"), V("GN"), bk(4, 0, 256), A.not_equal)
+        w = 128 if last else 256
+        mmul(bk(3, 0, w), Ib, V("PC", 0, w), True, False)
+        mmul(bk(3, 0, 128), V("If"), V("dd"), False, False)
+        mmul(bk(3, 0, 128), V("FS4"), V("emp"), False, last)
         if not last:
-            act(V("GF"), ind(V("FC"), oH))
-            mmul(V(bank[1], 128, 256), V("FS4"), V("emp"), True, False)
+            act(V("GF"), ind(FCw, ou(oN, 16)))
+            mmul(bk(3, 128, 256), V("FS4"), V("emp"), False, False)
             for n in range(8):
-                x = 64 * (n // 2) + 16 * (1 - n % 2)
-                mmul(V(bank[1], 128 + 16 * n, 144 + 16 * n), V("nI"), V("Q", x, x + 16), False, n == 7)
-            act(V("nu2"), V(bank[1], 128, 256), AF.Relu, bias=-3072.0)
-        act(V(bank[3], 0, 128), V("dd"))
-        tt(V("rd", 0, 128), V("GN", 0, 128), V(bank[3], 0, 128), A.not_equal)
-        tt(V("rd", 128, 256), V("GN", 128, 256), V(bank[3], 0, 128), A.not_equal)
-        act(V(bank[4], 0, 128), V("GN", 0, 128))
-        tt(V("cn"), V(bank[4], 0, 128), V("rd", 0, 128), A.mult)
-        if not last:
-            act(V("rf", 128, 256), V("rd", 128, 256), bias=1024.0, scale=-2048.0)
-            act(V(bank[5], 0, 128), V("rd", 0, 128), bias=1024.0, scale=-2048.0)
-            tt(V("cf"), V("GF", 0, 128), V(bank[5], 0, 128), A.max)
+                sl, c = divmod(n, 4)
+                x = 64 * c + 16 * (1 - sl)
+                mmul(bk(3, 128 + 16 * n, 144 + 16 * n), V("nI"), V("Q", x, x + 16), False, n == 7)
+            tt(V("MX", 128, 256), bk(3, 128, 256), V("GF", 0, 128), A.max)
+        tt(V("MX", 0, 128), bk(3, 0, 128), V("GN", 0, 128), A.max)
+        mmul(bk(7, 0, 256), Ib, V("PEN16"), True, False)
+        mmul(bk(7, 0, 256), Ib, V("CE"), False, False)
         n = 0
-        if EQA:
-            act(col("en", 39), col("en", 19), scale=-1.0)
-        for c in (3, 2, 1, 0):
-            for sl in (2 * c, 2 * c + 1, 8 + 2 * c, 9 + 2 * c):
-                e0 = 256 * n
+        for m in range(8):
+            s2, c2 = divmod(m, 4)
+            mmul(bk(7, 64 * c2 + 16 * s2, 64 * c2 + 16 * s2 + 16), V("BL8k"), V("ins", 16 * m, 16 * m + 16), False, False)
+        for sl in range(4 * EQA):
+            mmul(bk(7, 192, 256), V("TRn"), V("EQ", 64 * sl, 64 * sl + 64), False, False)
+        for c in range(4 - EQA):
+            for sl in range(4):
                 n += 1
-                if n <= EQA:
-                    act(V("EQ", e0, e0 + 64), V("Q", 192, 256), AF.Abs, bias=col("en", sl), scale=-1.0)
-                    act(V("EQ", e0 + 192, e0 + 256), V("EQ", e0, e0 + 64), AF.Relu, bias=col("en", 19), scale=col("en", 39))
-                else:
-                    ts(V("EQ", e0 + 64 * c, e0 + 256), V("Q", 64 * c, 256), col("en", sl), col("en", 16 + c), A.is_equal, A.mult)
-                mmul(V(bank[7], 64 * c, 64 * c + 64), V("TRT"), V("EQ", e0 + 64 * c, e0 + 64 * c + 64), False, False)
+                e0 = 256 * n - (0 if EQA else 256)
+                ts(V("EQ", e0 + 64 * c, e0 + 256), V("Q", 64 * c, 256), col("NM", 4 * sl + c), col("has", c), A.is_equal, A.min)
                 if c < 3:
-                    mmul(V(bank[7], 64 * c + 64, 256), V("BLT"), V("EQ", e0 + 64 * c + 64, e0 + 256), False, False)
+                    mmul(bk(7, 64 * c + 64, 256), V("BLn8k"), V("EQ", e0 + 64 * c + 64, e0 + 256), False, False)
+                mmul(bk(7, 64 * c, 64 * c + 64), V("TRn"), V("EQ", e0 + 64 * c, e0 + 64 * c + 64), False, c == 3 - EQA and sl == 3)
+        scan(V("kv"), V("RB64"), bk(7, 0, 256))
         for c in range(4):
-            mmul(V(bank[7], 64 * c, 64 * c + 32), V("BLn"), V("ins", 32 * c, 32 * c + 32), False, c == 3)
-        act(V("zg"), ind(V("Z%d" % t), oE))
-        act(V("yh"), ind(V("ya", 4096, 8192), oA))
-        mmul(V(bank[0], 0, 64), V("Ib"), V("zg"), True, False)
-        mmul(V(bank[0], 0, 64), V("Ib"), V("yh"), False, True)
-        act(V("ys"), V(bank[0], 0, 64), bias=123.75, scale=0.5)
-        tt(V("km"), V(bank[7], 0, 256), V("D"), A.mult)
-        scan(V("ks"), V("R64"), V("km"), A.mult, A.add)
-        if last:
-            new_ends(t)
-        vw = V("ks", 63, 256, 64)
-        for a0, a1, st in ((0, 8, 2), (1, 8, 2), (8, 16, 2), (9, 16, 2), (16, 20, 1)):
-            tt(V("sm", a0, a1, st), V("NM", a0, a1, st), vw, A.add)
-        tt(V("sm", 20, 40), V("sm", 0, 20), V("DUM"), A.min)
-        cp(oS, V("sm", 20, 40))
-        act(go, vw, AF.Relu, bias=1.0, scale=-1.0)
-        oS0, oS1, oSY = V("ou", 64, 72), V("ou", 72, 80), V("ou", 80, 84)
+            ts(ou(oS + c, 20 - c, 4), V("NM", c, 20, 4), col("kv", 64 * c + 63), P["du%d" % c], A.subtract, A.min)
+        ts(k1, xi, 10, 15, A.logical_shift_right, A.bitwise_and)
+        ts(e16, le, 16.0, P["l64"], A.mult, A.add)
+        tt(kk, k1, e16, A.add)
+        cp(ou(oA, 4), kk)
+        act(V("zg"), ind(z[1], ou(oE, 4)))
+        act(V("yh"), ind(V("ya", 4096, 8192), ou(oA, 4)))
+        msum(bk(0, 256, 320), [(Ib, V("zg")), (Ib, V("yh"))])
+        act(V("ys"), bk(0, 256, 320), bias=123.75, scale=0.5)
 
         def put_y():
-            tt(ind(V("Yb", 16, 4176), oSY), V("ys"), V("cm128"), A.add)
+            tt(ind(V("Yb", 16, 4176), ou(oS + 16, 4)), V("ys"), V("cm128"), A.add)
+
+        def put(tab, old, new):
+            for sl in (2, 3, 0, 1):
+                x = V(old, 64 * sl, 64 * sl + 64) if sl > 1 else V("MX", new + 64 * sl, new + 64 * sl + 64)
+                tt(ind(V(tab), ou(oS + 4 * sl, 4)), x, V("rd", 64 * sl, 64 * sl + 64), A.mult)
 
         if last:
             early[0] = 5.0
@@ -681,22 +563,36 @@ def rank_program(g, core, T, topo):
             early[0] = 0.0
             dma("s", T.y1[:, 0:2048], V("Yb", 16, 2064))
             dma("a", T.y1[:, 2048:4096], V("Yb", 2064, 4112))
-        tt(ind(V("NB"), oS1), V("GN", 128, 256), V("rd", 128, 256), A.mult)
-        tt(ind(V("NB"), oS0), V("cn"), V("t2"), A.add)
+        else:
+            put("FC", "GF", 128)
+        put("NB", "GN", 0)
         if not last:
-            tt(ind(V("FC"), oS1), V("GF", 128, 256), V("rf", 128, 256), A.max)
-            tt(ind(V("FC"), oS0), V("cf"), V("nu2"), A.subtract)
-            early[0] = 0.0
             put_y()
-            early[0] = 0.0
-            act(V("goB", 0, 4), go)
+            act(V("GB", 4 * t, 4 * t + 4), V("kv", 63, 256, 64), AF.Relu, bias=513.0)
+            msum(bk(6, 64, 65), [(V("BLK"), col("GB", c)) for c in range(4 * t + 4)])
+            cnt = bk(6, 64, 65)
+            if t == 0:
+                act(P["a0"], cnt, AF.Relu, bias=-63.0)
+                act(P["a1"], cnt, bias=P["bT0"], scale=-2048.0)
+                act(P["bT1"], P["a0"], bias=P["a1"], scale=131072.0)
+            else:
+                act(P["a0"], cnt, AF.Sign, bias=-63.5)
+                act(P["a1"], cnt, bias=P["th2"], scale=-2048.0)
+                act(P["a2"], cnt, AF.Relu, bias=-127.0)
+                act(P["a3"], P["a0"], bias=P["a1"], scale=65536.0)
+                act(P["bT2"], P["a2"], bias=P["a3"], scale=131072.0)
+        for n, (o, f) in enumerate(((oN, 1.0), (oN + 4, -1.0), (oN, -1024.0))):
+            act(V("nsv", 64 * n, 64 * n + 64), ind(V("numT"), ou(o, 4)), scale=f)
+        msum(bk(6, 128, 192), [(V("If"), V("nsv", 0, 64)), (V("If"), V("nsv", 64, 128))])
+        act(V("mn"), bk(6, 128, 192), AF.Relu, scale=1023.0)
+        msum(bk(6, 0, 64), [(V("If"), V("nsv", 128, 192)), (V("If"), V("nsv", 64, 128)), (V("If"), V("mn"))])
+        act(V("en"), bk(6, 0, 64), scale=-1.0)
+        cp(ind(V("EF"), ou(oS + 16, 4)), V("en"))
 
     for (x0, x1, a0, a1, st) in SEG:
         act(V("neo", x0, x1), V("NB", a0, a1, st), bias=4095.0, scale=-1.0)
     dma("s", T.ne1[:], V("neo"))
-    book_keeping(RO - 1)
-    for c in range(4):
-        dma("a" if c % 2 else "s", T.ends1[:, 1024 * c:1024 * c + 1024], V("Ef", 64 * c, 64 * c + 64))
+    dma("a", T.ends1[:], V("EF", 0, 4096, 1, 0, 128, 16))
 
     def meet(x, y, wide):
         if x[0] != y[0]:
@@ -720,20 +616,21 @@ def rank_program(g, core, T, topo):
     lastsend = [None]
     for n, op in enumerate(ops):
         q = op["q"]
-        asy = op["dma"] or q is None
+        asy = op["dma"] or q is None or op["left"] is not None
         sync, after = set(), set()
         for w, v in [(False, v) for v in op["rd"]] + [(True, v) for v in op["wr"]]:
             psum = SCRATCH[v[0]][0] == "psum"
             for (m, w2, v2) in touch.get(v[0], []):
                 o2 = ops[m]
-                asy2 = o2["dma"] or o2["q"] is None
+                asy2 = o2["dma"] or o2["q"] is None or o2["left"] is not None
                 same = o2["q"] == q and not asy and not asy2
                 if psum and not same:
                     sync.add(m)
                 elif psum and q == "p":
-                    after.add(m)
+                    if op.get("inner", -1) != o2.get("inner", -2):
+                        after.add(m)
                 elif (w or w2) and meet(v, v2, asy or asy2):
-                    (after if same and w and not SAMEQ else sync).add(m)
+                    sync.add(m)
         if (op["dma"] and q != "g") or op["ext"] == "send":
             if q in lastdma:
                 after.add(lastdma[q])
@@ -843,6 +740,8 @@ def rank_program(g, core, T, topo):
             ndma[0] += 1
         elif q is None:
             op["key"], op["idx"] = op["ext"]
+        elif op["left"]:
+            op["key"], op["idx"] = op["left"]
         else:
             seq[q] += 1
             op["key"], op["idx"] = q, seq[q]
@@ -871,7 +770,11 @@ def rank_program(g, core, T, topo):
         for m in op["waits"]:
             eng[q].wait_ge(T.sem[ops[m]["sem"]], ops[m]["val"])
         ins = op["fn"]()
-        if op["dma"]:
+        if op["left"]:
+            op["sem"], op["val"] = op["left"]
+            if not op.get("need"):
+                tail.append(op)
+        elif op["dma"]:
             op["sem"], op["val"] = op["key"], 16
             ins.then_inc(T.sem[op["sem"]], 16)
             if not op.get("need"):
@@ -882,4 +785,4 @@ def rank_program(g, core, T, topo):
             ins.then_inc(T.sem[op["sem"]], 1)
     g.wait_ge(T.sem.lsem, sent[0])
     for op in tail:
-        eng[op["q"]].wait_ge(T.sem[op["sem"]], 16)
+        eng[op["q"]].wait_ge(T.sem[op["sem"]], op["val"])

@@ -1,48 +1,49 @@
 import numpy as np
 from concourse.bass import DstId, RemoteDMATransfer, IndirectOffsetOnAxis
-from concourse.mybir import AluOpType, AxisListType, ActivationFunctionType
+from concourse.mybir import AluOpType, ActivationFunctionType
 
 F, B, I, U, H = "float32", "bfloat16", "int32", "uint16", "float16"
 RO = 3
 CAP = 1009 * 16384 + 1023
-PEN, BIG = 2.0 ** 25, 2.0 ** 25
+PEN, BIG = 2.0 ** 50, 2.0 ** 25
 KTOP = 256.0 * 35216 + 255
-CY, PECY, WAKE, LOOK, EARLY = 0.83e-3, 0.417e-3, 0.1, 0.3, 12.0
+CY, PECY, WAKE, LOOK, EARLY, FLAT = 1.0e-3, 0.5e-3, 0.13, 0.3, 12.0, 5.0
 PLAN = {}
-ROUNDS, JIT, SEED = 10, 0.3, 1
+ROUNDS, JIT, SEED = 8, 0.3, 2
 FE = "avavavavavav"
-PART = ((0, 128), (128, 128))
+PART = ((0, 128), (128, 64), (192, 64))
 OWN = ((0, 64, "a"), (64, 64, "a"), (128, 64, "v"), (192, 64, "v"))
-X0, X1 = min([256] + [a for a, n, e in OWN if e == "v"]), 512
-EQA, FLAT = 1, 4.5
+X0 = min(a for a, n, e in OWN if e == "v")
 TAB = 4160
+SINT = True
 
 SB = {
-    "Yb": (4176, B), "EWin": (4096, B), "FG": (12288, B), "ya": (8192, B), "mm": (8192, B), "m15": (256, B), "mz": (16 * (256 - X0), B),
-    "zr0": (16 * (X1 - X0), B), "zr1": (16 * (X1 - X0), B),
-    "NB": (TAB, F), "FC": (TAB, F), "EF": (TAB, F), "nei": (768, I), "neu": (768, U), "neo": (768, F),
-    "eA": (256, I), "Ef": (256, F), "UV": (512, I), "cB": (512, F), "cC": (512, B), "TR": (96, B),
+    "Yb": (6224, B), "EWin": (4096, B), "FG": (12288, B), "ya": (8192, B), "mm": (8192, B), "m15": (256, B), "mz": (16 * (256 - X0), B),
+    "zr0": (8192 - 16 * X0, B), "zr1": (8192 - 16 * X0, B), "L0": (4096, B),
+    "FC": (TAB, F), "NB": (TAB, F), "EF": (2048 + TAB, F), "nei": (768, I), "neu": (768, U),
+    "eA": (256, I), "Ef": (256, F), "UV": (512, I), "cB": (512, F), "cC": (512, B), "TR": (96, B), "HL": (512, B),
     "ZZ0": (512, B), "ZZ1": (512, B), "ZZ2": (512, B), "off": (240, U),
-    "pi": (4, I), "pq": (8, I), "pf": (48, F), "thi": (4, I), "ysave": (8, B), "MK": (12, F),
-    "IO": (176, F), "ML": (256, B), "MG": (128, B), "M4": (256, B), "M64": (256, B), "M32": (128, B),
-    "RB16": (192, F), "RB64": (256, F), "CAPS": (128, F), "CE": (256, B), "PC": (256, B), "PENK": (256, B), "PEN16": (256, B),
-    "icolK": (256, B), "icol2": (512, B), "codeT": (1024, B), "codeX": (768, B), "numT": (1024, F),
-    "If": (128, F), "ZS": (144, B), "IW": (160, B), "PT": (1024, H), "cm128": (64, B),
-    "aU": (512, U), "cU": (512, U), "bV": (512, H), "FS": (1024, B), "TT": (512, B), "acc": (512, F), "acd": (512, F),
+    "pi": (4, I), "pq": (8, I), "pf": (48, F), "thi": (4, I), "pb": (16, F), "ysave": (8, B), "MK": (12, F),
+    "IO": (176, F), "ML": (256, B), "MG": (128, B), "M4": (256, B), "M16": (256, B), "M64": (256, B), "M32": (128, B),
+    "RB16": (192, F), "RB64": (256, F), "CAPS": (128, F), "CE": (256, B), "PC": (256, B), "C4": (256, B), "PENK": (256, B), "PEN16": (256, B),
+    "icolK": (256, B), "codeT": (1024, B), "codeX": (768, B), "numT": (1024, F),
+    "If": (128, F), "ZS": (144, B), "ZS2": (144, B), "IW": (160, B), "PT": (1024, H), "cm128": (64, B),
+    "aU": (512, U), "cU": (512, U), "bV": (512, H), "FS": (1024, B), "acc": (512, F), "acd": (512, F),
     "pc": (256, B), "pv": (256, B), "CW": (272, F), "sg": (256, B), "r1": (256, B), "KA": (256, F),
-    "ke": (256, F), "kd": (256, F), "k3": (192, F), "kv": (256, F), "si": (40, I), "ou": (96, U), "NM": (20, F), "has": (16, F), "EA": (256, B),
-    "G1": (128, F), "G2": (128, F), "G3": (128, F), "Q3": (192, B), "Q": (256, B), "EQ": (4096, B), "GN": (256, F), "GF": (256, F),
-    "dd": (128, F), "emp": (128, B), "ins": (128, B), "MX": (256, F), "rd": (256, F),
+    "ke": (256, I if SINT else F), "kd": (256, I if SINT else F), "k3": (192, F), "kv": (256, F), "si": (40, I), "ou": (96, U), "NM": (20, F),
+    "has": (4, F), "EA": (256, B), "G1": (128, F), "G2": (128, F), "G3": (128, I if SINT else F), "Q3": (128, B), "Q": (256, B), "QS": (64, B),
+    "GN": (256, F), "GF": (256, F), "emp": (128, B), "MX": (256, F), "rd": (256, F),
     "zg": (64, B), "yh": (64, B), "ys": (64, B), "GB": (8, B), "nsv": (192, F), "mn": (64, F), "en": (64, F),
 }
-MATS = (["nI", "Is", "Ik", "In8k", "BLK", "BL256", "BLn256", "BL4096", "BL8k", "BLn8k", "TRn", "T1", "FST", "FS4", "BC0", "BC1"]
+MATS = (["nI", "Is", "BD", "B1n", "BLK", "BLn256", "BL4096", "BLn8k", "TRn", "T1", "FST", "BC0", "BC1"]
         + ["RP%d" % k for k in range(4)] + ["BT%d" % k for k in range(8)] + ["SH%d" % k for k in range(4)])
 SCRATCH = {k: ("sbuf", [128, v[0]], v[1]) for k, v in SB.items()}
 SCRATCH["MT"] = ("sbuf", [128, 128 * len(MATS)], B)
 for _b in range(8):
     SCRATCH["bank%d" % _b] = ("psum", [128, 512], F)
 NDMA = 16
-SEMAPHORES = ["sv", "sa", "sp", "sg", "lsem"] + ["dm%d" % k for k in range(NDMA)] + ["%s%d" % (a, t) for a in ("qc", "qz", "qk", "qm", "lk", "lm") for t in range(RO)]
+SEMAPHORES = (["sv", "sa", "sp", "sg", "lsem", "lz"] + ["dm%d" % k for k in range(NDMA)] + ["%s%d" % (a, t) for a in ("qc", "qz") for t in range(RO)]
+              + ["%s%d_%d" % (a, t, u) for a in "ql" for t in range(RO) for u in range(len(PART))])
 SIZE = {F: 4, B: 2, I: 4, U: 2, H: 2}
 QSEM = {"v": "sv", "a": "sa", "p": "sp", "g": "sg"}
 
@@ -56,12 +57,19 @@ def rank_program(g, core, T, topo):
     AF = ActivationFunctionType
     ops = []
     group = {}
+    hints = []
     early = [0.0]
     eng = {"v": g.vector, "a": g.scalar, "p": g.tensor, "g": g, "s": g.sync}
 
     def V(name, lo=0, hi=None, st=1, p0=0, p1=128, ps=1):
         if name in MATS:
             return ("MT", 128 * MATS.index(name), 128 * MATS.index(name) + 128, 1, 0, 128, 1)
+        if name == "neo":
+            return ("FC", 2048 + lo, 2048 + (768 if hi is None else hi), st, p0, p1, ps)
+        if name[:2] == "zr":
+            return (name, lo - 16 * X0, hi - 16 * X0, st, p0, p1, ps)
+        if name == "EQ":
+            return ("FG", lo, hi, st, p0, p1, ps)
         return (name, lo, SCRATCH[name][1][1] if hi is None else hi, st, p0, p1, ps)
 
     def col(name, c):
@@ -96,17 +104,17 @@ def rank_program(g, core, T, topo):
         n = max([len(range(v[1], v[2], v[3])) for v in flat] + [1])
         dts = [SCRATCH[v[0]][2] for v in flat if v[2] - v[1] > 1]
         lat = 0.0
-        fix = 0.065 if q == "a" else 0.05
+        fix = 0.06
         if q is None:
             cost, lat = 0.0, way
         elif ext == "send":
-            cost, lat = 0.3, (way if left else 0.0)
+            cost, lat = 0.5, (way if left else 0.0)
         elif dma:
-            cost, lat = (1.7 if q == "g" else 0.1), 2.0 + n * len(range(*flat[0][4:7])) * SIZE[SCRATCH[flat[0][0]][2]] / 180e3
+            cost, lat = (1.7 if q == "g" else 0.1), way
         elif q == "p":
-            cost, lat = PECY * max(64, len(range(*outs[0][1:4]))) * (4 if SCRATCH[ins[0][0]][2] == F else 1), 0.1
+            cost, lat = PECY * max(64, len(range(*outs[0][1:4]))) * (4 if SCRATCH[ins[0][0]][2] == F else 1), 0.2
         elif q == "g":
-            cost = 0.17 + 2 * CY * n
+            cost = 1.3 * (0.17 + 2 * CY * n)
         elif outs[0][0] == "ind":
             cost = fix + 3.8 * CY * n
         elif ins and ins[0][0] == "ind":
@@ -134,8 +142,8 @@ def rank_program(g, core, T, topo):
     def ms(o, c):
         add("v", lambda: g.vector.memset(ap(o), c), [o], [])
 
-    def scan(o, x, y, op0=A.max, op1=A.min):
-        add("v", lambda: g.vector.tensor_tensor_scan(ap(o), ap(x), ap(y), 0.0, op0, op1), [o], [x, y])
+    def scan(o, x, y):
+        add("v", lambda: g.vector.tensor_tensor_scan(ap(o), ap(x), ap(y), 0.0, A.max, A.min), [o], [x, y])
 
     def transpose(o, x):
         add("v", lambda: g.vector.transpose(ap(o), ap(x)), [o], [x])
@@ -159,11 +167,17 @@ def rank_program(g, core, T, topo):
         else:
             add("g", lambda: g.iota(ap(o), pat, base, cm, allow_small_or_imprecise_dtypes=True), [o], [])
 
-    def pick(o, x, pat, op, fill, base, cm):
-        add("g", lambda: g.affine_select(ap(o), ap(x), pat, op, fill, base, cm), [o], [x])
+    def fill(o, c):
+        iota(o, [[0, len(range(*o[1:4]))]], c)
 
-    def dma(q, o, x):
-        add(q, lambda: eng[q].dma_start(ap(o), ap(x)), [o], [x], dma=True)
+    def pick(o, x, pat, op, other, base, cm):
+        add("g", lambda: g.affine_select(ap(o), ap(x), pat, op, other, base, cm), [o], [x])
+
+    def gcopy(o, x):
+        pick(o, x, [[0, len(range(*o[1:4]))]], A.is_ge, 0.0, 0, 0)
+
+    def dma(q, o, x, way):
+        add(q, lambda: eng[q].dma_start(ap(o), ap(x)), [o], [x], dma=True, way=way)
 
     sent = [0]
 
@@ -178,14 +192,16 @@ def rank_program(g, core, T, topo):
             trs.append(RemoteDMATransfer(dst_ids=[DstId(rid=rid, pnc=pid)], dma_engine_mask=m, remote_sem=T.sem[sem], src=ap(s), dst=ap(d)))
         sent[0] += nq * len(items)
         add("g", lambda: g.remote_dma_fused(trs, local_sem=T.sem.lsem), [], [it[1] for it in items] + list(behind), ext="send")
+        for r, s, d, sem in items:
+            arrive(d, sem, nq)
 
-    def fold_min(r, srcs, d, sem, left):
+    def fold(r, srcs, d, sem, left, how=3, way=FLAT):
         dst = T.cores[r]
         rid, pid = topo.addr(dst)[:2]
         tr = RemoteDMATransfer(dst_ids=[DstId(rid=rid, pnc=pid)], dma_engine_mask=topo.mask(core, dst), remote_sem=T.sem[sem],
-                               srcs=[ap(s) for s in srcs], dsts=[ap(d)], alu_op=3)
+                               srcs=[ap(s) for s in srcs], dsts=[ap(d)], alu_op=how)
         n = len(topo.engines(core, dst))
-        add("g", lambda: g.remote_dma_fused([tr], local_sem=T.sem[left]), [], srcs, ext="send", way=FLAT, left=(left, n))
+        add("g", lambda: g.remote_dma_fused([tr], local_sem=T.sem[left]), [], srcs, ext="send", way=way, left=(left, n))
         arrive(d, sem, n, 0.0)
 
     def arrive(v, sem, n, way=3.0):
@@ -197,13 +213,14 @@ def rank_program(g, core, T, topo):
     Ywin = V("Yb", 16, 4112)
     Ib = V("IW", 16, 144)
     NBw, FCw = V("NB", 0, 1024), V("FC", 0, 1024)
-    names = ("lf gf pff m1 hf par hi8 m0 lo8 hi8s lo8s wpar tc0 c0 c1 kb zc l4 l64 dA dB dC0 dC1 dC2 du0 du1 du2 du3 "
-             "bT0 bT1 bT2 th2 a0 a1 a2 a3").split()
+    names = ("lf gf pff m1 hf par hi8 m0 lo8 hi8s lo8s wpar tc0 c0 c1 kb zc lt2 s16 bd l64 l4 dE0 dE1 dE2 dC0 dC1 dC2 dD0 dD1 dD2 "
+             "du0 du1 du2 du3 bT0 bT1 bT2 th2 a0 a1 a2 a3").split()
     P = {n: col("pf", k) for k, n in enumerate(names)}
     lf, m0, m1 = P["lf"], P["m0"], P["m1"]
 
-    dma("s", V("eA"), T.ends0[:])
-    dma("a", V("nei"), T.ne0[:])
+    dma("s", V("eA"), T.ends0[:], 2.5)
+    dma("s", V("nei"), T.ne0[:], 3.8)
+    dma("s", V("Yb", 16, 2064), T.y0[:, 0:2048], 5.5)
     iota(col("pi", 0), [[0, 1]], 0, 1)
     iota(V("IO"), [[1, 176]], -16)
     iota(V("MG"), [[1, 8], [0, 16]])
@@ -212,8 +229,9 @@ def rank_program(g, core, T, topo):
     iota(V("codeX", 128, 640), [[-1, 512]], 256)
     iota(V("codeX", 640, 768), [[-2, 128]], -256)
     early[0] = EARLY
-    for n in range(4):
+    for n in range(2):
         ms(V("EWin", 1024 * n, 1024 * n + 1024), 0.0)
+        act(V("EWin", 2048 + 1024 * n, 3072 + 1024 * n), V("EWin", 0, 1024))
     early[0] = 0.0
     pi = col("pi", 0)
     ts(col("pq", 0), pi, 15, None, A.bitwise_and)
@@ -231,27 +249,37 @@ def rank_program(g, core, T, topo):
     early[0] = 2 * EARLY
     tt(V("cC"), V("cB"), bk(2), A.subtract)
     early[0] = 0.0
-    dma("s", V("EWin", 0, 4096, 1, 0, 128, 16), V("cC", 0, 256))
-    dma("s", V("EWin", 0, 4096, 1, 1, 128, 16), V("cC", 256, 512))
-    dma("s", Ywin, T.y0[:])
+    dma("s", V("EWin", 0, 4096, 1, 0, 128, 16), V("cC", 0, 256), 2.4)
+    dma("s", V("EWin", 0, 4096, 1, 1, 128, 16), V("cC", 256, 512), 2.4)
+    iota(V("M16"), [[1, 16], [0, 16]])
+    act(P["s16"], lf, scale=16.0)
+    act(V("HL", 0, 256), V("M16"), bias=P["s16"])
+    act(V("HL", 256, 512), V("ML"), bias=1.0)
+    dma("a", V("EWin", 0, 4096, 1, 2, 128, 16), V("HL", 0, 256), 2.4)
+    dma("a", V("EWin", 0, 4096, 1, 3, 128, 16), V("HL", 256, 512), 2.4)
+    dma("s", V("Yb", 2064, 4112), T.y0[:, 2048:4096], 4.2)
     cp(V("Ef"), V("eA"))
-    dma("a", V("EF", 0, 4096, 1, 0, 128, 16), V("Ef"))
+    dma("a", V("EF", 0, 4096, 1, 0, 128, 16), V("Ef"), 2.5)
     cp(V("neu"), V("nei"))
     ms(col("EWin", 4095), 768.0)
     early[0] = 60.0
     for n, x, sc, bi in (("m0", "m1", -1.0, 1.0), ("lo8", "hi8", -1.0, 1.0), ("hi8s", "hi8", 2.0 ** -13, 0.0), ("lo8s", "lo8", 2.0 ** -13, 0.0),
                          ("wpar", "par", 8191.0, 1.0), ("tc0", "lf", 1.0, "pff"), ("zc", "gf", 16.0, 15.0), ("l4", "lf", 4.0, 0.0),
                          ("a0", "m1", 256.0, 0.0), ("a1", "m0", 256.0, 0.0), ("c0", "l4", "m0", "a0"), ("c1", "l4", "m1", "a1"),
-                         ("kb", "lf", 1024.0, 512.0), ("l64", "lf", 64.0, 0.0), ("dA", "lf", 4.0, 255.0), ("dB", "lf", 4.0, 511.0)):
+                         ("kb", "lf", 1024.0, 512.0), ("l64", "lf", 64.0, 0.0)):
         act(P[n], P[x], bias=P.get(bi, bi), scale=P.get(sc, sc))
-    for t in range(RO):
-        act(P["dC%d" % t], lf, bias=3568.0 + 5 * t, scale=64.0)
-    for c in range(4):
-        act(P["du%d" % c], lf, bias=4096.0 + 16 * c)
+    k = names.index("dE0")
+    iota(V("pb", 0, 3), [[5, 3]])
+    iota(V("pb", 3, 9), [[512, 2], [5, 3]], 3568)
+    iota(V("pb", 9, 13), [[16, 4]], 4096)
+    act(V("pf", k, k + 9), V("pb", 0, 9), bias=P["l64"])
+    act(V("pf", k + 9, k + 13), V("pb", 9, 13), bias=lf)
     early[0] = 0.0
     ts(V("IW"), V("IO", 0, 160), P["pff"], None, A.is_equal)
     ts(V("BLK"), V("MG"), P["gf"], None, A.is_equal)
     ts(V("ZS"), V("IO", 16, 160), P["zc"], None, A.is_equal)
+    act(P["lt2"], P["hf"], AF.Relu, bias=1.0, scale=-1.0)
+    act(V("ZS2"), V("ZS"), scale=P["lt2"])
     for k, (d, m) in enumerate(((16, m0), (0, m0), (32, m1), (16, m1))):
         act(V("SH%d" % k), V("IW", d, d + 128), scale=m)
     for t in range(RO):
@@ -264,10 +292,11 @@ def rank_program(g, core, T, topo):
     early[0] = 0.0
     send([((rank + 1 + t) % N, V("off", 80 * t + 48, 80 * t + 80), V("off", 80 * t, 80 * t + 32), "qc%d" % t) for t in range(RO)], 4)
     for t in range(RO):
-        arrive(V("off", 80 * t, 80 * t + 32), "qc%d" % t, 4)
-    for t in range(RO):
         act(V("ZZ%d" % t, 0, 256), V("Yb", 16 + 5 * t, 4112, 16), bias=8.0)
-    act(col("ysave", 0), col("Yb", 4111))
+    gcopy(V("HL", 0, 256), V("Yb", 16, 4112, 16))
+    fill(V("M16"), 8)
+    fold((rank + 1) % N, [V("HL", 0, 256), V("M16")], V("ZZ0", 256, 512), "qz0", "lz", 1, 3.0)
+    gcopy(col("ysave", 0), col("Yb", 4111))
 
     for ch in range(12):
         o, x = V("FG", 1024 * ch, 1024 * ch + 1024), ind(V("EWin"), V("neu", 64 * ch, 64 * ch + 64))
@@ -277,11 +306,11 @@ def rank_program(g, core, T, topo):
             cp(o, x)
     for ch in range(12):
         msum(bk(ch // 8, 64 * (ch % 8), 64 * (ch % 8) + 64), [(Ib, V("codeX", 64 * ch, 64 * ch + 64))]
-             + [(V("ZS", 15 - k, 143 - k), V("FG", 1024 * ch + k, 1024 * ch + 1024, 16)) for k in range(16)])
+             + [(V("ZS2", 15 - k, 143 - k), V("FG", 1024 * ch + k, 1024 * ch + 1024, 16)) for k in range(16)])
 
     early[0] = 40.0
     ts(V("MK", 0, 8), V("IO", 16, 24), P["hf"], P["wpar"], A.is_equal, A.mult)
-    ts(V("MK", 8, 10), V("IO", 16, 18), lf, None, A.is_equal)
+    ts(V("MK", 8, 12), V("IO", 16, 20), lf, None, A.is_equal)
     for n in range(2):
         for pc in range(2):
             d = 16 + 16 * n - pc
@@ -291,90 +320,107 @@ def rank_program(g, core, T, topo):
     for j in range(2):
         act(V("BC%d" % j), V("BLK"), scale=col("MK", 8 + j))
     act(V("nI"), Ib, scale=-1.0)
-    for x, c in (("NB", 1.0), ("FC", 0.0)):
-        ms(V(x, 1, 256, 2), c)
-        ms(V(x, 769, 1024, 2), c)
+    act(P["a2"], col("MK", 11), scale=-1.0)
+    act(P["bd"], col("MK", 10), bias=P["a2"], scale=-16.0)
+    act(V("BD"), V("BLK"), scale=P["bd"])
+    act(V("B1n"), V("BC1"), scale=-8192.0)
+    fill(V("C4"), 4096)
+    for x, c in (("NB", 1), ("FC", 0)):
+        fill(V(x, 1, 256, 2), c)
+        fill(V(x, 769, 1024, 2), c)
     SEG = [(0, 128, 0, 256, 2), (128, 640, 256, 768, 1), (640, 768, 768, 1024, 2)]
     for (x0, x1, a0, a1, st) in SEG:
         ts(V("NB", a0, a1, st), V("nei", x0, x1), -1.0, 4095.0, A.mult, A.add)
-    for n, x, sc in (("BL256", "BLK", 256.0), ("BLn256", "BLK", -256.0), ("BL4096", "BLK", 4096.0), ("BL8k", "BLK", 8192.0), ("BLn8k", "BLK", -8192.0)):
-        act(V(n), V(x), scale=sc)
-    for n, sc in (("If", 1.0), ("Is", 2.0 ** -27), ("Ik", 1024.0), ("In8k", -8192.0)):
+    for n, sc in (("BLn256", -256.0), ("BL4096", 4096.0), ("BLn8k", -2.0 ** 18)):
+        act(V(n), V("BLK"), scale=sc)
+    for n, sc in (("If", 1.0), ("Is", 2.0 ** -27)):
         act(V(n), Ib, scale=sc)
-    ms(V("PC", 0, 128), -4096.0)
-    ms(V("PC", 128, 256), -3072.0)
-    ms(V("cm128"), -128.0)
-    ms(V("CW", 256, 272), float(1 << 24))
-    ms(V("Yb", 0, 16), 128.0)
+    iota(V("PC"), [[-3072, 2], [0, 128]], -4096)
+    fill(V("cm128"), -128)
+    fill(V("CW", 256, 272), (1 << 24) - 1)
+    fill(V("Yb", 0, 16), 128)
     ts(V("PEN16"), V("ML"), lf, PEN, A.not_equal, A.mult)
     act(V("RB16"), V("ML", 0, 192), bias=BIG / 2, scale=-BIG)
     early[0] = 0.0
-    ms(col("Yb", 4111), 128.0)
-    act(V("FC", 0, 256, 2), bk(0, 0, 128), AF.Relu, bias=1024.0, scale=-1.0)
-    act(V("FC", 256, 640), bk(0, 128, 512), AF.Relu, bias=1024.0, scale=-1.0)
-    act(V("FC", 640, 768), bk(1, 0, 128), AF.Relu, bias=1024.0, scale=-1.0)
-    act(V("FC", 768, 1024, 2), bk(1, 128, 256), AF.Relu, bias=1024.0, scale=-1.0)
-    send([((rank + 1 + t) % N, V("ZZ%d" % t, 0, 256), V("ZZ%d" % t, 256, 512), "qz%d" % t) for t in range(RO)], 4, [FCw])
-    for t in range(RO):
-        arrive(V("ZZ%d" % t, 256, 512), "qz%d" % t, 4)
-
-    def late_consts():
-        iota(V("M4"), [[0, 4], [1, 16], [0, 4]])
-        iota(V("icolK"), [[64, 4], [0, 16], [1, 4]])
-        iota(V("M64"), [[0, 4], [1, 64]])
-        iota(V("M32"), [[0, 4], [1, 32]])
-        iota(V("CE"), [[0, 4], [8192, 2], [0, 32]], -8704)
-        iota(V("icol2"), [[0, 2], [1, 256]])
-        iota(V("codeT"), [[1, 1024]], -512)
-        iota(V("numT", 0, 256), [[1, 128], [0, 2]])
-        iota(V("numT", 256, 768), [[1, 512]], 128)
-        iota(V("numT", 768, 1024), [[1, 128], [0, 2]], 640)
-        ts(V("PENK"), V("M4"), lf, PEN, A.not_equal, A.mult)
-        act(V("RB64"), V("M64"), bias=BIG / 2, scale=-BIG)
-        act(V("CAPS"), V("M32"), AF.Relu, bias=float(CAP), scale=-float(CAP))
-        pick(V("TRn"), V("BLn8k"), [[1, 128]], A.is_gt, 0.0, 0, -1)
-        act(V("T1"), V("TRn"), scale=2.0 ** -13)
-        pick(V("FST"), V("T1"), [[1, 128]], A.not_equal, 1.0, 0, -1)
-        act(V("FS4"), V("FST"), scale=4096.0)
-        ts(P["bT0"], col("thi", 0), -256.0, 30.0, A.mult, A.add)
-        act(P["th2"], P["bT0"], bias=65536.0)
-
-    late_consts()
+    fill(col("Yb", 4111), 128)
+    for o, x in ((V("FC", 0, 256, 2), bk(0, 0, 128)), (V("FC", 256, 640), bk(0, 128, 512)), (V("FC", 640, 768), bk(1, 0, 128)),
+                 (V("FC", 768, 1024, 2), bk(1, 128, 256))):
+        act(o, x, AF.Relu, bias=1024.0, scale=-1.0)
+    send([((rank + 1 + t) % N, V("ZZ%d" % t, 0, 256), V("ZZ%d" % t, 256, 512), "qz%d" % t) for t in range(1, RO)], 4, [FCw])
+    iota(V("M4"), [[0, 4], [1, 16], [0, 4]])
+    iota(V("icolK"), [[64, 4], [0, 16], [1, 4]])
+    iota(V("M64"), [[0, 4], [1, 64]])
+    iota(V("M32"), [[0, 4], [1, 32]])
+    iota(V("CE"), [[0, 4], [8192, 2], [0, 32]], -8704)
+    iota(V("codeT"), [[1, 1024]], -512)
+    iota(V("numT", 0, 256), [[1, 128], [0, 2]])
+    iota(V("numT", 256, 768), [[1, 512]], 128)
+    iota(V("numT", 768, 1024), [[1, 128], [0, 2]], 640)
+    ts(V("PENK"), V("M4"), lf, PEN, A.not_equal, A.mult)
+    act(V("RB64"), V("M64"), bias=BIG / 2, scale=-BIG)
+    act(V("CAPS"), V("M32"), AF.Relu, bias=float(CAP), scale=-float(CAP))
+    pick(V("TRn"), V("BLn8k"), [[1, 128]], A.is_gt, 0.0, 0, -1)
+    act(V("T1"), V("TRn"), scale=2.0 ** -18)
+    pick(V("FST"), V("T1"), [[1, 128]], A.not_equal, 1.0, 0, -1)
+    ts(P["bT0"], col("thi", 0), -256.0, 30.0, A.mult, A.add)
+    act(P["th2"], P["bT0"], bias=65536.0)
+    act(P["s16"], P["dC2"], bias=-2048.0)
 
     def spread_z(t):
         for k in range(16):
-            pick(V("zr%d" % (t % 2), k, None, 16), V("ZZ%d" % t, X0, X1), [[0, X1 - X0]], A.is_ge, 0.0, 0, 0)
+            gcopy(V("zr%d" % (t % 2), 16 * X0 + k, 8192, 16), V("ZZ%d" % t, X0, 512))
+
+    tip = {}
+
+    def chain(name):
+        if name in tip:
+            hints.append((tip[name], len(ops) - 1))
+        tip[name] = len(ops) - 1
 
     oC, oE, oD, oN, oQ, oA, oS = 0, 8, 12, 20, 36, 52, 56
     ou = lambda a, n, st=1: V("ou", a, a + n, st)
     si = lambda a: V("si", a, a + 4)
-    rot = [0]
+
+    def put_ends():
+        cp(ind(V("EF", 0, TAB), ou(oS + 16, 4)), V("en"))
+
     spread_z(0)
 
     for t in range(RO):
         last = t == RO - 1
         o0 = 80 * t
-        ZZ = "ZZ%d" % t
-        z = [V(ZZ, 256, 512), V(ZZ, 0, 256)]
+        ZZ, zr = "ZZ%d" % t, "zr%d" % (t % 2)
         sS, fV = V("FS", 256, 768), [V("FS", 0, 256), V("FS", 768, 1024)]
-        act(V("FS"), ind(FCw, V("off", o0, o0 + 64)), bias=8192.0 * 1024, scale=-8192.0)
+        if t == 0:
+            act(V("FS", 256, 768), ind(FCw, V("off", o0 + 16, o0 + 48)), bias=8192.0 * 1024, scale=-8192.0)
+            for a in (0, 48):
+                ts(V("FS", 16 * a, 16 * a + 256), ind(FCw, V("off", o0 + a, o0 + a + 16)), -8192.0, 8192.0 * 1024, A.mult, A.add)
+        else:
+            for a, b in ((16, 48), (0, 16), (48, 64)):
+                act(V("FS", 16 * a, 16 * b), ind(FCw, V("off", o0 + a, o0 + b)), bias=8192.0 * 1024, scale=-8192.0)
+                if a != 16:
+                    hints.append((len(ops) - 2, len(ops) - 1))
         ts(V("aU", 0, 64), ind(NBw, V("off", o0 + 16, o0 + 20)), -1.0, 4095.0, A.mult, A.add)
         for h in range(2):
             ts(V("bV", 256 * h, 256 * h + 256), ind(NBw, V("off", o0 + 48 * h, o0 + 48 * h + 16)), -2048.0, None, A.add)
+        if t > 0:
+            put_y()
+            hints.append((len(ops) - 2, len(ops) - 1))
         ts(V("aU", 64, 512), ind(NBw, V("off", o0 + 20, o0 + 48)), -1.0, 4095.0, A.mult, A.add)
 
         def ya_gather(c):
             act(V("ya", 16 * c, 16 * c + 1024), ind(Ywin, V("aU", c, c + 64)))
+            chain("a")
 
         def yc_gather(c):
             tt(V("mm", 16 * c, 16 * c + 1024), ind(V("Yb", 0, 4112), V("cU", c, c + 64)), V("ya", 16 * c, 16 * c + 1024), A.max)
 
-        ya_gather(0)
         for n in range(2):
-            mmul(bk(6 + n), V("RP%d" % (2 * n)), V("bV"), True, False)
+            mmul(bk(4 + n), V("RP%d" % (2 * n)), V("bV"), True, False)
             for h in range(2):
-                mmul(bk(6 + n, 256 * h, 256 * h + 256), V("RP%d" % (2 * n + 1)), fV[h], False, h == 1)
-            cp(V("PT", 512 * n, 512 * n + 512), bk(6 + n))
+                mmul(bk(4 + n, 256 * h, 256 * h + 256), V("RP%d" % (2 * n + 1)), fV[h], False, h == 1)
+            cp(V("PT", 512 * n, 512 * n + 512), bk(4 + n))
+            chain("v")
         for j in range(16):
             bn = (0, 1, 2, 3, 6, 7)[j % 6]
             b = bk(bn)
@@ -386,73 +432,71 @@ def rank_program(g, core, T, topo):
             else:
                 mmul(b, V("BT%d" % (j % 8)), V("PT", 512 * (j // 8), 512 * (j // 8) + 512), False, True)
             ac = V("acc" if j % 2 == 0 else "acd")
-            if j < 2:
-                act(ac, b, AF.Abs, bias=2048.0)
-            else:
-                act(b, b, AF.Abs, bias=2048.0)
+            act(ac if j < 2 else b, b, AF.Abs, bias=2048.0)
+            chain("a")
+            if j > 1:
                 tt(bk(4) if j == 15 else ac, b, ac, A.min)
+                chain("v")
+        ya_gather(0)
         for h in range(2):
             tt(V("acc", 256 * h, 256 * h + 256), bk(4, 256 * h, 256 * h + 256), V("acc", 256 * h, 256 * h + 256), A.min)
             ts(V("cU", 256 * h, 256 * h + 256), V("acc", 256 * h, 256 * h + 256), -1.0, 4111.0, A.mult, A.add)
-        for n in range(2):
-            mmul(bk(5, 256 * n, 256 * n + 256), V("BC%d" % (1 - n)), V("EWin", 5 * t, 4096, 16), True, True)
-        act(V("TT"), bk(5))
         mmul(bk(3, X0, 256), Ib, V(ZZ, X0, 256), True, True)
 
         def score(a, n, e, stop):
             c = 256 + a
             o = bk(5, a, a + n)
-            za = V(ZZ, a, a + n)
             if e == "v":
                 x = 16 * (a - X0)
                 tt(V("m15", a, a + n), bk(3, a, a + n), V("mm", 16 * c + 15, 16 * (c + n), 16), A.min)
                 ms(V("mm", 16 * c + 15, 16 * (c + n), 16), 0.0)
-                scan(V("mz", x, x + 16 * n), V("zr%d" % (t % 2), x, x + 16 * n), V("mm", 16 * c, 16 * (c + n)))
-                mmul(o, V("BL4096"), za, False, False)
+                scan(V("mz", x, x + 16 * n), V(zr, 16 * a, 16 * (a + n)), V("mm", 16 * c, 16 * (c + n)))
+                if t > 0 and stop:
+                    put_ends()
+                    hints.append((len(ops) - 2, len(ops) - 1))
+                mmul(o, V("BL4096"), V(ZZ, a, a + n), False, False)
                 mmul(o, V("BLn256"), V("m15", a, a + n), False, False)
                 for k in range(15):
                     mmul(o, V("BLn256"), V("mz", x + k, x + 16 * n, 16), False, stop and k == 14)
                 return
-            per = 512 // n
-            r0 = 16 * a
-            for k0 in range(0, 16, per):
-                bn = rot[0] % 3
-                rot[0] += 1
-                for k in range(per):
-                    msum(bk(bn, n * k, n * k + n), [(Ib, za), (V("nI"), V("mm", 16 * c + k0 + k, 16 * (c + n), 16))])
-                act(V("EQ", r0 + n * k0, r0 + n * k0 + 512), bk(bn), AF.Relu)
+            for x in range(16 * a, 16 * (a + n), 512):
+                bn = (0, 1, 2, 4, 7)[x // 512 % 5]
+                for k in range(8):
+                    msum(bk(bn, n * k, n * k + n), [(Ib, V(ZZ, a, a + n)), (V("nI"), V("mm", 16 * c + x // 64 % 16 + k, 16 * (c + n), 16))])
+                act(V("EQ", x, x + 512), bk(bn), AF.Relu, scale=256.0)
             for k in range(16):
-                mmul(o, V("BL256"), V("EQ", r0 + n * k, r0 + n * k + n), False, stop and k == 15)
+                mmul(o, V("BLK"), V("EQ", 16 * a + n * k, 16 * a + n * k + n), False, stop and k == 15)
 
-        for a, n in PART:
+        land = "FG" if t else "L0"
+        for u, (a, n) in enumerate(PART):
             for c in range(a, a + n, 64):
                 if c > 0:
                     ya_gather(c)
                 yc_gather(c)
-            x, y = 16 * (256 + a - X0), 4096 * t + 16 * a
-            fold_min((rank - 1 - t) % N, [V("zr%d" % (t % 2), x, x + 16 * n), V("mm", 16 * a, 16 * (a + n))], V("FG", y, y + 16 * n),
-                     ("qm", "qk")[a == 0] + str(t), ("lm", "lk")[a == 0] + str(t))
+            x, y = 4096 + 16 * a, 4096 * t + 16 * a
+            fold((rank - 1 - t) % N, [V(zr, x, x + 16 * n), V("mm", 16 * a, 16 * (a + n))], V(land, y, y + 16 * n),
+                     "q%d_%d" % (t, u), "l%d_%d" % (t, u))
         if not last:
             spread_z(t + 1)
         mmul(bk(5, 0, 256), Ib, V("icolK"), True, False)
         mmul(bk(5, 0, 256), Ib, V("PENK"), False, False)
         for c in range(256, 512, 64):
             ya_gather(c)
-        act(V("pc"), V("acc", 256, 512), AF.Relu, bias=4096.0, scale=-1.0)
-        msum(bk(7, 0, 256), [(Ib, V("FS", 512, 768)), (V("In8k"), V("TT", 0, 256))])
-        act(bk(7, 0, 256), bk(7, 0, 256), AF.Abs)
-        act(V("pv"), bk(7, 0, 256), AF.Relu, bias=4096.0, scale=-1.0)
+        act(V("pc"), V("acc", 256, 512), AF.Relu, bias=4096.0 * 1024, scale=-1024.0)
+        msum(bk(3, 256, 512), [(Ib, V("FS", 512, 768)), (V("B1n"), V("EWin", 5 * t, 4096, 16))])
+        act(bk(3, 256, 512), bk(3, 256, 512), AF.Abs)
+        act(V("pv"), bk(3, 256, 512), AF.Relu, bias=4096.0 * 1024, scale=-1024.0)
         mmul(bk(6, 0, 256), V("Is"), V("FS", 512, 768), True, False)
         for c in range(0, 256, 64):
             for k in range(16):
                 mmul(bk(6, c, c + 64), V("ZS", 15 - k, 143 - k), V("ya", 4096 + 16 * c + k, 5120 + 16 * c, 16), False, False)
-        mmul(bk(6, 0, 256), V("Ik"), V("pc"), False, False)
-        mmul(bk(6, 0, 256), V("Ik"), V("pv"), False, True)
+        mmul(bk(6, 0, 256), Ib, V("pc"), False, False)
+        mmul(bk(6, 0, 256), Ib, V("pv"), False, True)
         act(V("CW", 0, 256), bk(6, 0, 256), bias=P["kb"], scale=16384.0)
-        mmul(bk(5, 0, 256), V("BL4096"), z[1], False, False)
+        mmul(bk(5, 0, 256), V("BL4096"), V(ZZ, 0, 256), False, False)
         for a, n in PART:
             for k in range(16):
-                mmul(bk(5, a, a + n), V("BLn256"), V("FG", 4096 * t + 16 * a + k, 4096 * t + 16 * (a + n), 16), False, False)
+                mmul(bk(5, a, a + n), V("BLn256"), V(land, 4096 * t + 16 * a + k, 4096 * t + 16 * (a + n), 16), False, False)
         for m, (a, n, e) in enumerate(OWN):
             for c in range(a, a + n, 64):
                 yc_gather(256 + c)
@@ -460,94 +504,116 @@ def rank_program(g, core, T, topo):
         scan(V("ke"), V("RB64"), bk(5, 0, 256))
         act(V("KA"), bk(5, 0, 256), AF.Abs, bias=KTOP, scale=-1.0)
         act(V("sg"), bk(5, 0, 256), AF.Sign, bias=P["bT%d" % t])
-        le, ld, xi, sc, k1, e16, kk = si(4), si(12), si(16), si(20), si(24), si(28), si(32)
-        cp(si(0), V("ke", 63, 256, 64))
-        ts(le, si(0), 255, None, A.bitwise_and)
+        le, ld, sc, k1, e16, kk = si(4), si(12), si(20), si(24), si(28), si(32)
+
+        def whole(x, o):
+            if SINT:
+                return x
+            cp(o, x)
+            return o
+
+        ts(le, whole(V("ke", 63, 256, 64), si(0)), 255, None, A.bitwise_and)
         ts(ou(oC, 8, 2), le, m0, P["c0"], A.mult, A.add)
         ts(ou(oC + 1, 7, 2), le, m1, P["c1"], A.mult, A.add)
         act(V("G1"), ind(V("CW"), ou(oC, 8)))
-        ts(ou(oE, 4), le, P["l4"], None, A.add)
+        ts(ou(oE, 4), le, 16.0, P["dE%d" % t], A.mult, A.add)
         scan(V("kd"), V("RB64"), V("KA"))
-        cp(si(8), V("kd", 63, 256, 64))
-        ts(ld, si(8), 255, None, A.bitwise_and)
-        ts(ou(oD, 4), ld, -1.0, P["dA"], A.mult, A.add)
-        ts(ou(oD + 4, 4), ld, -1.0, P["dB"], A.mult, A.add)
-        ts(V("NM", 16, 20), ld, -16.0, P["dC%d" % t], A.mult, A.add)
-        act(V("Q3"), ind(V("TT"), ou(oE, 12)))
-        msum(bk(1, 0, 192), [(Ib, V("PEN16", 0, 192)), (Ib, V("Q3"))])
+        ts(ld, whole(V("kd", 63, 256, 64), si(8)), 255, None, A.bitwise_and)
+        ts(ou(oD, 4), ld, -16.0, P["dD%d" % t], A.mult, A.add)
+        if last:
+            ts(V("NM", 16, 18), V("si", 12, 14), -16.0, P["dC2"], A.mult, A.add)
+            ts(V("NM", 18, 20), V("si", 14, 16), -16.0, P["s16"], A.mult, A.add)
+        else:
+            ts(V("NM", 16, 20), ld, -16.0, P["dC%d" % t], A.mult, A.add)
+        act(V("Q3"), ind(V("EWin"), ou(oE, 8)))
+        act(V("zg"), ind(Ywin, ou(oE, 4)))
+        Qd = V("Q3", 64, 128)
+        mmul(bk(1, 0, 192), Ib, V("PEN16", 0, 192), True, False)
+        mmul(bk(1, 0, 128), V("BC1"), V("Q3"), False, False)
+        mmul(bk(1, 128, 192), V("BC0"), Qd, False, True)
         transpose(V("G2"), V("G1"))
         scan(V("G3"), V("CAPS"), V("G2"))
-        cp(xi, V("G3", 31, 128, 32))
+        xi = whole(V("G3", 31, 128, 32), si(16))
         ts(sc, xi, 1023, None, A.bitwise_and)
         scan(V("k3"), V("RB16"), bk(1, 0, 192))
-        for sl in range(3):
-            ts(ou(oQ + 1 + sl, 15 - sl, 4), V("k3", 64 * sl + 15, 64 * sl + 64, 16), 512.0, None, A.add)
-        cp(ou(oQ, 16, 4), sc)
-        act(V("Q"), ind(V("codeT"), ou(oQ, 16)))
         cp(ou(oN, 4), sc)
+        act(V("QS"), ind(V("codeT"), ou(oN, 4)))
+        for sl, l, x in ((1, V("BC1"), ("Q3", 0)), (2, V("BC1"), ("Q3", 64)), (3, V("BC0"), ("Q3", 64)), (0, Ib, ("QS", 0))):
+            for c in range(4):
+                mmul(bk(2, 256 + 64 * c + 16 * sl, 272 + 64 * c + 16 * sl), l, V(x[0], x[1] + 16 * c, x[1] + 16 * c + 16), True, True)
+        act(V("Q"), bk(2, 256, 512))
+        name = lambda sl, c: col("k3", 64 * sl + 16 * c - 49) if sl else col("NM", c)
         ts(ou(oN + 4, 12), V("k3", 15, 192, 16), 512.0, None, A.add)
         ts(V("NM", 0, 4), sc, -512.0, None, A.add)
         act(V("NM", 4, 16), V("k3", 15, 192, 16))
-        act(V("has", 0, 4), V("G3", 31, 128, 32), AF.Relu, bias=1009.0 * 16384, scale=-1.0)
-        if EQA:
-            act(V("has", 4, 8), V("has", 0, 4), AF.Sign)
-            act(col("has", 8), col("has", 7), scale=-1.0)
-            for sl in range(4):
-                act(V("EA", 64 * sl, 64 * sl + 64), V("Q", 192, 256), AF.Abs, bias=col("NM", 4 * sl + 3), scale=-1.0)
-            act(V("EQ", 0, 256), V("EA"), AF.Relu, bias=col("has", 7), scale=col("has", 8))
-        msum(bk(0, 0, 256), [(Ib, z[1]), (V("BLK"), V("sg"))])
+        if SINT:
+            ts(V("has"), xi, 1009.0 * 16384, None, A.is_lt)
+        else:
+            act(V("has"), V("G3", 31, 128, 32), AF.Relu, bias=1009.0 * 16384, scale=-1.0)
+        for sl in range(4):
+            act(V("EA", 64 * sl, 64 * sl + 64), V("Q", 192, 256), AF.Abs, bias=name(sl, 3), scale=-1.0)
+        act(V("EQ", 0, 256), V("EA"), AF.Relu, bias=col("has", 3), scale=-BIG)
+        msum(bk(0, 0, 256), [(Ib, V(ZZ, 0, 256)), (V("BLK"), V("sg"))])
         act(V("r1"), bk(0, 0, 256), AF.Relu, bias=86.0, scale=-1.0)
         act(V("Yb", 16 + 5 * t, 4112, 16), V("r1"), AF.Relu, bias=63.0, scale=-1.0)
         if last:
             act(col("Yb", 4111), col("ysave", 0))
         act(V("GN"), ind(NBw, ou(oN, 16)))
-        act(V("dd"), ind(V("icol2"), ou(oD, 8)), bias=4095.0 - 5 * t, scale=-16.0)
-        act(V("emp"), V("GN", 0, 128), AF.Relu, bias=1.0, scale=-1.0)
-        mmul(bk(2, 0, 128), V("FST"), V("emp"), True, True)
-        act(V("ins"), bk(2, 0, 128), AF.Relu)
-        for h in range(2):
-            mmul(bk(4, 128 * h, 128 * h + 128), V("If"), V("dd"), True, True)
+        act(V("emp"), V("GN", 0, 128), AF.Relu, bias=8192.0, scale=-8192.0)
+        mmul(bk(4, 0, 256), Ib, V("C4"), True, False)
+        for sl in range(4):
+            mmul(bk(4, 64 * sl, 64 * sl + 64), V("BD"), Qd, False, sl == 3)
         tt(V("rd"), V("GN"), bk(4, 0, 256), A.not_equal)
         w = 128 if last else 256
         mmul(bk(3, 0, w), Ib, V("PC", 0, w), True, False)
-        mmul(bk(3, 0, 128), V("If"), V("dd"), False, False)
-        mmul(bk(3, 0, 128), V("FS4"), V("emp"), False, last)
+        for sl in range(2):
+            mmul(bk(3, 64 * sl, 64 * sl + 64), V("BD"), Qd, False, False)
+        mmul(bk(3, 0, 128), V("FST"), V("emp"), False, last)
         if not last:
             act(V("GF"), ind(FCw, ou(oN, 16)))
-            mmul(bk(3, 128, 256), V("FS4"), V("emp"), False, False)
+            mmul(bk(3, 128, 256), V("FST"), V("emp"), False, False)
             for n in range(8):
                 sl, c = divmod(n, 4)
                 x = 64 * c + 16 * (1 - sl)
                 mmul(bk(3, 128 + 16 * n, 144 + 16 * n), V("nI"), V("Q", x, x + 16), False, n == 7)
-            tt(V("MX", 128, 256), bk(3, 128, 256), V("GF", 0, 128), A.max)
-        tt(V("MX", 0, 128), bk(3, 0, 128), V("GN", 0, 128), A.max)
-        mmul(bk(7, 0, 256), Ib, V("PEN16"), True, False)
-        mmul(bk(7, 0, 256), Ib, V("CE"), False, False)
-        n = 0
+        act(V("KA", 0, w), bk(3, 0, w), AF.Relu)
+        mmul(bk(1, 256, 256 + w), V("If"), V("KA", 0, w), True, False)
+        if not last:
+            mmul(bk(1, 384, 512), V("If"), V("GF", 0, 128), False, False)
+        mmul(bk(1, 256, 384), V("If"), V("GN", 0, 128), False, True)
+        act(V("MX", 0, w), bk(1, 256, 256 + w))
+        parts = ((7, 0, 128), (5, 128, 256))
+
+        def clash(l, e0, a, b, stop=False):
+            for bn, p0, p1 in parts:
+                if max(a, p0) < min(b, p1):
+                    mmul(bk(bn, max(a, p0), min(b, p1)), l, V(e0[0], e0[1] + max(a, p0) - a, e0[1] + min(b, p1) - a), False, stop)
+
+        for bn, p0, p1 in parts:
+            mmul(bk(bn, p0, p1), Ib, V("PEN16", p0, p1), True, False)
+        clash(Ib, ("CE", 0), 0, 256)
         for m in range(8):
-            s2, c2 = divmod(m, 4)
-            mmul(bk(7, 64 * c2 + 16 * s2, 64 * c2 + 16 * s2 + 16), V("BL8k"), V("ins", 16 * m, 16 * m + 16), False, False)
-        for sl in range(4 * EQA):
-            mmul(bk(7, 192, 256), V("TRn"), V("EQ", 64 * sl, 64 * sl + 64), False, False)
-        for c in range(4 - EQA):
+            sl, c = divmod(m, 4)
+            clash(V("BLK"), ("emp", 16 * m), 64 * c + 16 * sl, 64 * c + 16 * sl + 16)
+        for sl in range(4):
+            clash(V("TRn"), ("EQ", 64 * sl), 192, 256)
+        for c in range(3):
             for sl in range(4):
-                n += 1
-                e0 = 256 * n - (0 if EQA else 256)
-                ts(V("EQ", e0 + 64 * c, e0 + 256), V("Q", 64 * c, 256), col("NM", 4 * sl + c), col("has", c), A.is_equal, A.min)
-                if c < 3:
-                    mmul(bk(7, 64 * c + 64, 256), V("BLn8k"), V("EQ", e0 + 64 * c + 64, e0 + 256), False, False)
-                mmul(bk(7, 64 * c, 64 * c + 64), V("TRn"), V("EQ", e0 + 64 * c, e0 + 64 * c + 64), False, c == 3 - EQA and sl == 3)
-        scan(V("kv"), V("RB64"), bk(7, 0, 256))
+                e0 = 256 * (1 + 4 * c + sl) + 64 * c
+                ts(V("EQ", e0, e0 + 256 - 64 * c), V("Q", 64 * c, 256), name(sl, c), col("has", c), A.is_equal, A.min)
+                clash(V("BLn8k"), ("EQ", e0 + 64), 64 * c + 64, 256)
+                clash(V("TRn"), ("EQ", e0), 64 * c, 64 * c + 64, sl == 3 and c > 0)
+        for bn, p0, p1 in parts:
+            scan(V("kv", p0, p1), V("RB64", p0, p1), bk(bn, p0, p1))
         for c in range(4):
             ts(ou(oS + c, 20 - c, 4), V("NM", c, 20, 4), col("kv", 64 * c + 63), P["du%d" % c], A.subtract, A.min)
         ts(k1, xi, 10, 15, A.logical_shift_right, A.bitwise_and)
         ts(e16, le, 16.0, P["l64"], A.mult, A.add)
         tt(kk, k1, e16, A.add)
         cp(ou(oA, 4), kk)
-        act(V("zg"), ind(z[1], ou(oE, 4)))
         act(V("yh"), ind(V("ya", 4096, 8192), ou(oA, 4)))
         msum(bk(0, 256, 320), [(Ib, V("zg")), (Ib, V("yh"))])
-        act(V("ys"), bk(0, 256, 320), bias=123.75, scale=0.5)
+        act(V("ys"), bk(0, 256, 320), bias=127.75, scale=0.5)
 
         def put_y():
             tt(ind(V("Yb", 16, 4176), ou(oS + 16, 4)), V("ys"), V("cm128"), A.add)
@@ -555,19 +621,16 @@ def rank_program(g, core, T, topo):
         def put(tab, old, new):
             for sl in (2, 3, 0, 1):
                 x = V(old, 64 * sl, 64 * sl + 64) if sl > 1 else V("MX", new + 64 * sl, new + 64 * sl + 64)
-                tt(ind(V(tab), ou(oS + 4 * sl, 4)), x, V("rd", 64 * sl, 64 * sl + 64), A.mult)
+                tt(ind(V(tab, 0, TAB), ou(oS + 4 * sl, 4)), x, V("rd", 64 * sl, 64 * sl + 64), A.mult)
 
         if last:
-            early[0] = 5.0
-            put_y()
-            early[0] = 0.0
-            dma("s", T.y1[:, 0:2048], V("Yb", 16, 2064))
-            dma("a", T.y1[:, 2048:4096], V("Yb", 2064, 4112))
+            for h in range(2):
+                tt(ind(V("Yb", 16 + 2048 * h, 4176 + 2048 * h), ou(oS + 16 + 2 * h, 2)), V("ys", 32 * h, 32 * h + 32), V("cm128", 0, 32), A.add)
+                dma("s", T.y1[:, 2048 * h:2048 * h + 2048], V("Yb", 16 + 2048 * h, 2064 + 2048 * h), 5.1 - 1.05 * h)
         else:
             put("FC", "GF", 128)
         put("NB", "GN", 0)
         if not last:
-            put_y()
             act(V("GB", 4 * t, 4 * t + 4), V("kv", 63, 256, 64), AF.Relu, bias=513.0)
             msum(bk(6, 64, 65), [(V("BLK"), col("GB", c)) for c in range(4 * t + 4)])
             cnt = bk(6, 64, 65)
@@ -587,12 +650,16 @@ def rank_program(g, core, T, topo):
         act(V("mn"), bk(6, 128, 192), AF.Relu, scale=1023.0)
         msum(bk(6, 0, 64), [(V("If"), V("nsv", 128, 192)), (V("If"), V("nsv", 64, 128)), (V("If"), V("mn"))])
         act(V("en"), bk(6, 0, 64), scale=-1.0)
-        cp(ind(V("EF"), ou(oS + 16, 4)), V("en"))
 
+    for h in range(2):
+        cp(ind(V("EF", 2048 * h, 2048 * h + TAB), ou(oS + 16 + 2 * h, 2)), V("en", 32 * h, 32 * h + 32))
     for (x0, x1, a0, a1, st) in SEG:
-        act(V("neo", x0, x1), V("NB", a0, a1, st), bias=4095.0, scale=-1.0)
-    dma("s", T.ne1[:], V("neo"))
-    dma("a", T.ends1[:], V("EF", 0, 4096, 1, 0, 128, 16))
+        if st == 1:
+            ts(V("neo", x0, x1), V("NB", a0, a1, st), -1.0, 4095.0, A.mult, A.add)
+        else:
+            act(V("neo", x0, x1), V("NB", a0, a1, st), bias=4095.0, scale=-1.0)
+    dma("a", T.ends1[:], V("EF", 0, 4096, 1, 0, 128, 16), 3.1)
+    dma("s", T.ne1[:], V("neo"), 2.8)
 
     def meet(x, y, wide):
         if x[0] != y[0]:
@@ -617,7 +684,7 @@ def rank_program(g, core, T, topo):
     for n, op in enumerate(ops):
         q = op["q"]
         asy = op["dma"] or q is None or op["left"] is not None
-        sync, after = set(), set()
+        sync, after = set(), set(a for a, b in hints if b == n)
         for w, v in [(False, v) for v in op["rd"]] + [(True, v) for v in op["wr"]]:
             psum = SCRATCH[v[0]][0] == "psum"
             for (m, w2, v2) in touch.get(v[0], []):
@@ -725,7 +792,6 @@ def rank_program(g, core, T, topo):
             at = {n: k for k, n in enumerate(back)}
             order = sorted(back, key=lambda n: (-end[n], -at[n]))
         PLAN["order"] = best[1]
-        PLAN["span"] = best[0]
     order = PLAN["order"]
     known = {q: {} for q in eng}
     seq = {q: 0 for q in eng}

import numpy as np
from concourse.bass import DstId, RemoteDMATransfer, IndirectOffsetOnAxis
from concourse.mybir import AluOpType, ActivationFunctionType

F, B, I, U, H = "float32", "bfloat16", "int32", "uint16", "float16"
RO = 3
CAP = 1009 * 16384 + 1023
PEN, BIG = 2.0 ** 50, 2.0 ** 25
KTOP = 256.0 * 35216 + 255
CY, PECY, WAKE, LOOK, EARLY, FLAT = 1.0e-3, 0.5e-3, 0.13, 0.3, 12.0, 5.0
PLAN = {}
ROUNDS, JIT, SEED = 8, 0.3, 2
FE = "avavavavavav"
PART = ((0, 128), (128, 64), (192, 64))
OWN = ((0, 64, "a"), (64, 64, "a"), (128, 64, "v"), (192, 64, "v"))
X0 = min(a for a, n, e in OWN if e == "v")
TAB = 4160
SINT = True

SB = {
    "Yb": (6224, B), "EWin": (4096, B), "FG": (12288, B), "ya": (8192, B), "mm": (8192, B), "m15": (256, B), "mz": (16 * (256 - X0), B),
    "zr0": (8192 - 16 * X0, B), "zr1": (8192 - 16 * X0, B), "L0": (4096, B),
    "FC": (TAB, F), "NB": (TAB, F), "EF": (2048 + TAB, F), "nei": (768, I), "neu": (768, U),
    "eA": (256, I), "Ef": (256, F), "UV": (512, I), "cB": (512, F), "cC": (512, B), "TR": (96, B), "HL": (512, B),
    "ZZ0": (512, B), "ZZ1": (512, B), "ZZ2": (512, B), "off": (240, U),
    "pi": (4, I), "pq": (8, I), "pf": (48, F), "thi": (4, I), "pb": (16, F), "ysave": (8, B), "MK": (12, F),
    "IO": (176, F), "ML": (256, B), "MG": (128, B), "M4": (256, B), "M16": (256, B), "M64": (256, B), "M32": (128, B),
    "RB16": (192, F), "RB64": (256, F), "CAPS": (128, F), "CE": (256, B), "PC": (256, B), "C4": (256, B), "PENK": (256, B), "PEN16": (256, B),
    "icolK": (256, B), "codeT": (1024, B), "codeX": (768, B), "numT": (1024, F),
    "If": (128, F), "ZS": (144, B), "ZS2": (144, B), "IW": (160, B), "PT": (1024, H), "cm128": (64, B),
    "aU": (512, U), "cU": (512, U), "bV": (512, H), "FS": (1024, B), "acc": (512, F), "acd": (512, F),
    "pc": (256, B), "pv": (256, B), "CW": (272, F), "sg": (256, B), "r1": (256, B), "KA": (256, F),
    "ke": (256, I if SINT else F), "kd": (256, I if SINT else F), "k3": (192, F), "kv": (256, F), "si": (40, I), "ou": (96, U), "NM": (20, F),
    "has": (4, F), "EA": (256, B), "G1": (128, F), "G2": (128, F), "G3": (128, I if SINT else F), "Q3": (128, B), "Q": (256, B), "QS": (64, B),
    "GN": (256, F), "GF": (256, F), "emp": (128, B), "MX": (256, F), "rd": (256, F),
    "zg": (64, B), "yh": (64, B), "ys": (64, B), "GB": (8, B), "nsv": (192, F), "mn": (64, F), "en": (64, F),
}
MATS = (["nI", "Is", "BD", "B1n", "BLK", "BLn256", "BL4096", "BLn8k", "TRn", "T1", "FST", "BC0", "BC1"]
        + ["RP%d" % k for k in range(4)] + ["BT%d" % k for k in range(8)] + ["SH%d" % k for k in range(4)])
SCRATCH = {k: ("sbuf", [128, v[0]], v[1]) for k, v in SB.items()}
SCRATCH["MT"] = ("sbuf", [128, 128 * len(MATS)], B)
for _b in range(8):
    SCRATCH["bank%d" % _b] = ("psum", [128, 512], F)
NDMA = 16
SEMAPHORES = (["sv", "sa", "sp", "sg", "lsem", "lz"] + ["dm%d" % k for k in range(NDMA)] + ["%s%d" % (a, t) for a in ("qc", "qz") for t in range(RO)]
              + ["%s%d_%d" % (a, t, u) for a in "ql" for t in range(RO) for u in range(len(PART))])
SIZE = {F: 4, B: 2, I: 4, U: 2, H: 2}
QSEM = {"v": "sv", "a": "sa", "p": "sp", "g": "sg"}


def rank_program(g, core, T, topo):
    rank = T.rank_of(core)
    if rank is None:
        return
    N = len(T.cores)
    A = AluOpType
    AF = ActivationFunctionType
    ops = []
    group = {}
    hints = []
    early = [0.0]
    eng = {"v": g.vector, "a": g.scalar, "p": g.tensor, "g": g, "s": g.sync}

    def V(name, lo=0, hi=None, st=1, p0=0, p1=128, ps=1):
        if name in MATS:
            return ("MT", 128 * MATS.index(name), 128 * MATS.index(name) + 128, 1, 0, 128, 1)
        if name == "neo":
            return ("FC", 2048 + lo, 2048 + (768 if hi is None else hi), st, p0, p1, ps)
        if name[:2] == "zr":
            return (name, lo - 16 * X0, hi - 16 * X0, st, p0, p1, ps)
        if name == "EQ":
            return ("FG", lo, hi, st, p0, p1, ps)
        return (name, lo, SCRATCH[name][1][1] if hi is None else hi, st, p0, p1, ps)

    def col(name, c):
        return V(name, c, c + 1)

    def ind(w, o):
        return ("ind", w, o)

    def ap(v):
        if not isinstance(v, tuple):
            return v
        if v[0] == "ind":
            return ap(v[1]).indirect(ap(v[2]))
        pp = slice(v[4], v[5], v[6]) if v[6] != 1 else slice(v[4], v[5])
        cc = slice(v[1], v[2], v[3]) if v[3] != 1 else slice(v[1], v[2])
        return T[v[0]][pp, cc]

    def add(q, fn, outs, ins, dma=False, ext=None, two=False, way=3.0, left=None):
        rd, wr = [], []
        for v in ins:
            if isinstance(v, tuple):
                rd.extend([v[1], v[2]] if v[0] == "ind" else [v])
        for v in outs:
            if isinstance(v, tuple):
                if v[0] == "ind":
                    wr.append(v[1])
                    rd.append(v[2])
                else:
                    wr.append(v)
        full = [v for v in list(outs) + list(ins) if isinstance(v, tuple)]
        flat = [v for v in full if v[0] != "ind"]
        n = max([len(range(v[1], v[2], v[3])) for v in flat] + [1])
        dts = [SCRATCH[v[0]][2] for v in flat if v[2] - v[1] > 1]
        lat = 0.0
        fix = 0.06
        if q is None:
            cost, lat = 0.0, way
        elif ext == "send":
            cost, lat = 0.5, (way if left else 0.0)
        elif dma:
            cost, lat = (1.7 if q == "g" else 0.1), way
        elif q == "p":
            cost, lat = PECY * max(64, len(range(*outs[0][1:4]))) * (4 if SCRATCH[ins[0][0]][2] == F else 1), 0.2
        elif q == "g":
            cost = 1.3 * (0.17 + 2 * CY * n)
        elif outs[0][0] == "ind":
            cost = fix + 3.8 * CY * n
        elif ins and ins[0][0] == "ind":
            cost = fix + 1.56 * CY * n
        elif two and all(SCRATCH[v[0]][0] == "sbuf" for v in ins):
            cost = fix + CY * max(64, 2 * n)
        elif q == "v" and not two and all(SIZE[d] == 2 for d in dts):
            cost = fix + CY * max(64, n / 2)
        else:
            cost = fix + CY * max(64, n)
        ops.append({"q": q, "fn": fn, "rd": rd, "wr": wr, "dma": dma, "ext": ext, "cost": cost, "lat": lat, "early": early[0], "left": left})

    def ts(o, x, s1, s2, op0, op1=None):
        if op1 is None:
            add("v", lambda: g.vector.tensor_scalar(ap(o), ap(x), ap(s1), None, op0), [o], [x, s1])
        else:
            add("v", lambda: g.vector.tensor_scalar(ap(o), ap(x), ap(s1), ap(s2), op0, op1), [o], [x, s1, s2])

    def tt(o, x, y, op):
        add("v", lambda: g.vector.tensor_tensor(ap(o), ap(x), ap(y), op), [o], [x, y], two=True)

    def cp(o, x):
        add("v", lambda: g.vector.tensor_copy(ap(o), ap(x)), [o], [x])

    def ms(o, c):
        add("v", lambda: g.vector.memset(ap(o), c), [o], [])

    def scan(o, x, y):
        add("v", lambda: g.vector.tensor_tensor_scan(ap(o), ap(x), ap(y), 0.0, A.max, A.min), [o], [x, y])

    def transpose(o, x):
        add("v", lambda: g.vector.transpose(ap(o), ap(x)), [o], [x])

    def act(o, x, func=AF.Identity, bias=0.0, scale=1.0):
        add("a", lambda: g.scalar.activation(ap(o), ap(x), func, bias=ap(bias), scale=ap(scale)), [o], [x, bias, scale])

    def mmul(o, l, r, start, stop):
        add("p", lambda: g.tensor.matmul(ap(o), ap(l), ap(r), start, stop), [o], [l, r])
        group[o[0]] = group.get(o[0], 0) + start
        if not start and not stop:
            ops[-1]["inner"] = group[o[0]]

    def msum(o, terms):
        for n, (l, r) in enumerate(terms):
            mmul(o, l, r, n == 0, n == len(terms) - 1)

    def iota(o, pat, base=0, cm=0):
        if SCRATCH[o[0]][2] == I:
            add("g", lambda: g.iota(ap(o), pat, base, cm), [o], [])
        else:
            add("g", lambda: g.iota(ap(o), pat, base, cm, allow_small_or_imprecise_dtypes=True), [o], [])

    def fill(o, c):
        iota(o, [[0, len(range(*o[1:4]))]], c)

    def pick(o, x, pat, op, other, base, cm):
        add("g", lambda: g.affine_select(ap(o), ap(x), pat, op, other, base, cm), [o], [x])

    def gcopy(o, x):
        pick(o, x, [[0, len(range(*o[1:4]))]], A.is_ge, 0.0, 0, 0)

    def dma(q, o, x, way):
        add(q, lambda: eng[q].dma_start(ap(o), ap(x)), [o], [x], dma=True, way=way)

    sent = [0]

    def send(items, nq, behind=()):
        trs = []
        for k, (r, s, d, sem) in enumerate(items):
            dst = T.cores[r]
            m = 0
            for e in topo.engines(core, dst)[k * nq:(k + 1) * nq]:
                m += 1 << e
            rid, pid = topo.addr(dst)[:2]
            trs.append(RemoteDMATransfer(dst_ids=[DstId(rid=rid, pnc=pid)], dma_engine_mask=m, remote_sem=T.sem[sem], src=ap(s), dst=ap(d)))
        sent[0] += nq * len(items)
        add("g", lambda: g.remote_dma_fused(trs, local_sem=T.sem.lsem), [], [it[1] for it in items] + list(behind), ext="send")
        for r, s, d, sem in items:
            arrive(d, sem, nq)

    def fold(r, srcs, d, sem, left, how=3, way=FLAT):
        dst = T.cores[r]
        rid, pid = topo.addr(dst)[:2]
        tr = RemoteDMATransfer(dst_ids=[DstId(rid=rid, pnc=pid)], dma_engine_mask=topo.mask(core, dst), remote_sem=T.sem[sem],
                               srcs=[ap(s) for s in srcs], dsts=[ap(d)], alu_op=how)
        n = len(topo.engines(core, dst))
        add("g", lambda: g.remote_dma_fused([tr], local_sem=T.sem[left]), [], srcs, ext="send", way=way, left=(left, n))
        arrive(d, sem, n, 0.0)

    def arrive(v, sem, n, way=3.0):
        add(None, None, [v], [], ext=(sem, n), way=way)

    def bk(n, lo=0, hi=512, st=1):
        return V("bank%d" % n, lo, hi, st)

    Ywin = V("Yb", 16, 4112)
    Ib = V("IW", 16, 144)
    NBw, FCw = V("NB", 0, 1024), V("FC", 0, 1024)
    names = ("lf gf pff m1 hf par hi8 m0 lo8 hi8s lo8s wpar tc0 c0 c1 kb zc lt2 s16 bd l64 l4 dE0 dE1 dE2 dC0 dC1 dC2 dD0 dD1 dD2 "
             "du0 du1 du2 du3 bT0 bT1 bT2 th2 a0 a1 a2 a3").split()
    P = {n: col("pf", k) for k, n in enumerate(names)}
    lf, m0, m1 = P["lf"], P["m0"], P["m1"]

    dma("s", V("eA"), T.ends0[:], 2.5)
    dma("s", V("nei"), T.ne0[:], 3.8)
    dma("s", V("Yb", 16, 2064), T.y0[:, 0:2048], 5.5)
    iota(col("pi", 0), [[0, 1]], 0, 1)
    iota(V("IO"), [[1, 176]], -16)
    iota(V("MG"), [[1, 8], [0, 16]])
    iota(V("ML"), [[0, 16], [1, 16]])
    iota(V("codeX", 0, 128), [[-2, 128]], 512)
    iota(V("codeX", 128, 640), [[-1, 512]], 256)
    iota(V("codeX", 640, 768), [[-2, 128]], -256)
    early[0] = EARLY
    for n in range(2):
        ms(V("EWin", 1024 * n, 1024 * n + 1024), 0.0)
        act(V("EWin", 2048 + 1024 * n, 3072 + 1024 * n), V("EWin", 0, 1024))
    early[0] = 0.0
    pi = col("pi", 0)
    ts(col("pq", 0), pi, 15, None, A.bitwise_and)
    ts(col("pq", 1), pi, 4, None, A.logical_shift_right)
    cp(col("pq", 2), pi)
    for c, (sh, m) in enumerate(((4, 1), (1, 7), (0, 1), (3, 1))):
        ts(col("pq", 3 + c), pi, sh, m, A.logical_shift_right, A.bitwise_and)
    cp(V("pf", 0, 7), V("pq", 0, 7))
    add("g", lambda: g.indirect_dma_start(ap(col("thi", 0)), None, T.th[:], IndirectOffsetOnAxis(ap=ap(col("pq", 1)), axis=0), bounds_check=7),
        [col("thi", 0)], [col("pq", 1)], dma=True)
    ts(V("UV", 0, 256), V("eA"), 10, None, A.logical_shift_right)
    ts(V("UV", 256, 512), V("eA"), 1023, None, A.bitwise_and)
    ts(bk(2), V("UV"), 128.0, 640.0, A.max, A.min)
    ts(V("cB"), V("UV"), 2.0, -384.0, A.mult, A.add)
    early[0] = 2 * EARLY
    tt(V("cC"), V("cB"), bk(2), A.subtract)
    early[0] = 0.0
    dma("s", V("EWin", 0, 4096, 1, 0, 128, 16), V("cC", 0, 256), 2.4)
    dma("s", V("EWin", 0, 4096, 1, 1, 128, 16), V("cC", 256, 512), 2.4)
    iota(V("M16"), [[1, 16], [0, 16]])
    act(P["s16"], lf, scale=16.0)
    act(V("HL", 0, 256), V("M16"), bias=P["s16"])
    act(V("HL", 256, 512), V("ML"), bias=1.0)
    dma("a", V("EWin", 0, 4096, 1, 2, 128, 16), V("HL", 0, 256), 2.4)
    dma("a", V("EWin", 0, 4096, 1, 3, 128, 16), V("HL", 256, 512), 2.4)
    dma("s", V("Yb", 2064, 4112), T.y0[:, 2048:4096], 4.2)
    cp(V("Ef"), V("eA"))
    dma("a", V("EF", 0, 4096, 1, 0, 128, 16), V("Ef"), 2.5)
    cp(V("neu"), V("nei"))
    ms(col("EWin", 4095), 768.0)
    early[0] = 60.0
    for n, x, sc, bi in (("m0", "m1", -1.0, 1.0), ("lo8", "hi8", -1.0, 1.0), ("hi8s", "hi8", 2.0 ** -13, 0.0), ("lo8s", "lo8", 2.0 ** -13, 0.0),
                         ("wpar", "par", 8191.0, 1.0), ("tc0", "lf", 1.0, "pff"), ("zc", "gf", 16.0, 15.0), ("l4", "lf", 4.0, 0.0),
                         ("a0", "m1", 256.0, 0.0), ("a1", "m0", 256.0, 0.0), ("c0", "l4", "m0", "a0"), ("c1", "l4", "m1", "a1"),
                         ("kb", "lf", 1024.0, 512.0), ("l64", "lf", 64.0, 0.0)):
        act(P[n], P[x], bias=P.get(bi, bi), scale=P.get(sc, sc))
    k = names.index("dE0")
    iota(V("pb", 0, 3), [[5, 3]])
    iota(V("pb", 3, 9), [[512, 2], [5, 3]], 3568)
    iota(V("pb", 9, 13), [[16, 4]], 4096)
    act(V("pf", k, k + 9), V("pb", 0, 9), bias=P["l64"])
    act(V("pf", k + 9, k + 13), V("pb", 9, 13), bias=lf)
    early[0] = 0.0
    ts(V("IW"), V("IO", 0, 160), P["pff"], None, A.is_equal)
    ts(V("BLK"), V("MG"), P["gf"], None, A.is_equal)
    ts(V("ZS"), V("IO", 16, 160), P["zc"], None, A.is_equal)
    act(P["lt2"], P["hf"], AF.Relu, bias=1.0, scale=-1.0)
    act(V("ZS2"), V("ZS"), scale=P["lt2"])
    for k, (d, m) in enumerate(((16, m0), (0, m0), (32, m1), (16, m1))):
        act(V("SH%d" % k), V("IW", d, d + 128), scale=m)
    for t in range(RO):
        transpose(V("TR", 32 * t, 32 * t + 32), V("cC", 5 * t, 512, 16))
        for n, k in enumerate((0, 2, 0)):
            msum(bk(3, 48 * t + 16 * n, 48 * t + 16 * n + 16), [(V("SH%d" % (k + h)), V("TR", 32 * t + 16 * h, 32 * t + 16 * h + 16)) for h in range(2)])
    early[0] = 1.5 * EARLY
    for t in range(RO):
        ts(V("off", 80 * t + 32, 80 * t + 80), bk(3, 48 * t, 48 * t + 48), 512.0, None, A.add)
    early[0] = 0.0
    send([((rank + 1 + t) % N, V("off", 80 * t + 48, 80 * t + 80), V("off", 80 * t, 80 * t + 32), "qc%d" % t) for t in range(RO)], 4)
    for t in range(RO):
        act(V("ZZ%d" % t, 0, 256), V("Yb", 16 + 5 * t, 4112, 16), bias=8.0)
    gcopy(V("HL", 0, 256), V("Yb", 16, 4112, 16))
    fill(V("M16"), 8)
    fold((rank + 1) % N, [V("HL", 0, 256), V("M16")], V("ZZ0", 256, 512), "qz0", "lz", 1, 3.0)
    gcopy(col("ysave", 0), col("Yb", 4111))

    for ch in range(12):
        o, x = V("FG", 1024 * ch, 1024 * ch + 1024), ind(V("EWin"), V("neu", 64 * ch, 64 * ch + 64))
        if FE[ch] == "a":
            act(o, x)
        else:
            cp(o, x)
    for ch in range(12):
        msum(bk(ch // 8, 64 * (ch % 8), 64 * (ch % 8) + 64), [(Ib, V("codeX", 64 * ch, 64 * ch + 64))]
             + [(V("ZS2", 15 - k, 143 - k), V("FG", 1024 * ch + k, 1024 * ch + 1024, 16)) for k in range(16)])

    early[0] = 40.0
    ts(V("MK", 0, 8), V("IO", 16, 24), P["hf"], P["wpar"], A.is_equal, A.mult)
    ts(V("MK", 8, 12), V("IO", 16, 20), lf, None, A.is_equal)
    for n in range(2):
        for pc in range(2):
            d = 16 + 16 * n - pc
            ts(V("RP%d" % (2 * n + pc)), V("IO", d, d + 128), P["tc0"], P[("lo8", "hi8")[n] + ("", "s")[pc]], A.is_equal, A.mult)
    for jj in range(8):
        act(V("BT%d" % jj), V("BLK"), scale=col("MK", jj))
    for j in range(2):
        act(V("BC%d" % j), V("BLK"), scale=col("MK", 8 + j))
    act(V("nI"), Ib, scale=-1.0)
    act(P["a2"], col("MK", 11), scale=-1.0)
    act(P["bd"], col("MK", 10), bias=P["a2"], scale=-16.0)
    act(V("BD"), V("BLK"), scale=P["bd"])
    act(V("B1n"), V("BC1"), scale=-8192.0)
    fill(V("C4"), 4096)
    for x, c in (("NB", 1), ("FC", 0)):
        fill(V(x, 1, 256, 2), c)
        fill(V(x, 769, 1024, 2), c)
    SEG = [(0, 128, 0, 256, 2), (128, 640, 256, 768, 1), (640, 768, 768, 1024, 2)]
    for (x0, x1, a0, a1, st) in SEG:
        ts(V("NB", a0, a1, st), V("nei", x0, x1), -1.0, 4095.0, A.mult, A.add)
    for n, sc in (("BLn256", -256.0), ("BL4096", 4096.0), ("BLn8k", -2.0 ** 18)):
        act(V(n), V("BLK"), scale=sc)
    for n, sc in (("If", 1.0), ("Is", 2.0 ** -27)):
        act(V(n), Ib, scale=sc)
    iota(V("PC"), [[-3072, 2], [0, 128]], -4096)
    fill(V("cm128"), -128)
    fill(V("CW", 256, 272), (1 << 24) - 1)
    fill(V("Yb", 0, 16), 128)
    ts(V("PEN16"), V("ML"), lf, PEN, A.not_equal, A.mult)
    act(V("RB16"), V("ML", 0, 192), bias=BIG / 2, scale=-BIG)
    early[0] = 0.0
    fill(col("Yb", 4111), 128)
    for o, x in ((V("FC", 0, 256, 2), bk(0, 0, 128)), (V("FC", 256, 640), bk(0, 128, 512)), (V("FC", 640, 768), bk(1, 0, 128)),
                 (V("FC", 768, 1024, 2), bk(1, 128, 256))):
        act(o, x, AF.Relu, bias=1024.0, scale=-1.0)
    send([((rank + 1 + t) % N, V("ZZ%d" % t, 0, 256), V("ZZ%d" % t, 256, 512), "qz%d" % t) for t in range(1, RO)], 4, [FCw])
    iota(V("M4"), [[0, 4], [1, 16], [0, 4]])
    iota(V("icolK"), [[64, 4], [0, 16], [1, 4]])
    iota(V("M64"), [[0, 4], [1, 64]])
    iota(V("M32"), [[0, 4], [1, 32]])
    iota(V("CE"), [[0, 4], [8192, 2], [0, 32]], -8704)
    iota(V("codeT"), [[1, 1024]], -512)
    iota(V("numT", 0, 256), [[1, 128], [0, 2]])
    iota(V("numT", 256, 768), [[1, 512]], 128)
    iota(V("numT", 768, 1024), [[1, 128], [0, 2]], 640)
    ts(V("PENK"), V("M4"), lf, PEN, A.not_equal, A.mult)
    act(V("RB64"), V("M64"), bias=BIG / 2, scale=-BIG)
    act(V("CAPS"), V("M32"), AF.Relu, bias=float(CAP), scale=-float(CAP))
    pick(V("TRn"), V("BLn8k"), [[1, 128]], A.is_gt, 0.0, 0, -1)
    act(V("T1"), V("TRn"), scale=2.0 ** -18)
    pick(V("FST"), V("T1"), [[1, 128]], A.not_equal, 1.0, 0, -1)
    ts(P["bT0"], col("thi", 0), -256.0, 30.0, A.mult, A.add)
    act(P["th2"], P["bT0"], bias=65536.0)
    act(P["s16"], P["dC2"], bias=-2048.0)

    def spread_z(t):
        for k in range(16):
            gcopy(V("zr%d" % (t % 2), 16 * X0 + k, 8192, 16), V("ZZ%d" % t, X0, 512))

    tip = {}

    def chain(name):
        if name in tip:
            hints.append((tip[name], len(ops) - 1))
        tip[name] = len(ops) - 1

    oC, oE, oD, oN, oQ, oA, oS = 0, 8, 12, 20, 36, 52, 56
    ou = lambda a, n, st=1: V("ou", a, a + n, st)
    si = lambda a: V("si", a, a + 4)

    def put_ends():
        cp(ind(V("EF", 0, TAB), ou(oS + 16, 4)), V("en"))

    spread_z(0)

    for t in range(RO):
        last = t == RO - 1
        o0 = 80 * t
        ZZ, zr = "ZZ%d" % t, "zr%d" % (t % 2)
        sS, fV = V("FS", 256, 768), [V("FS", 0, 256), V("FS", 768, 1024)]
        if t == 0:
            act(V("FS", 256, 768), ind(FCw, V("off", o0 + 16, o0 + 48)), bias=8192.0 * 1024, scale=-8192.0)
            for a in (0, 48):
                ts(V("FS", 16 * a, 16 * a + 256), ind(FCw, V("off", o0 + a, o0 + a + 16)), -8192.0, 8192.0 * 1024, A.mult, A.add)
        else:
            for a, b in ((16, 48), (0, 16), (48, 64)):
                act(V("FS", 16 * a, 16 * b), ind(FCw, V("off", o0 + a, o0 + b)), bias=8192.0 * 1024, scale=-8192.0)
                if a != 16:
                    hints.append((len(ops) - 2, len(ops) - 1))
        ts(V("aU", 0, 64), ind(NBw, V("off", o0 + 16, o0 + 20)), -1.0, 4095.0, A.mult, A.add)
        for h in range(2):
            ts(V("bV", 256 * h, 256 * h + 256), ind(NBw, V("off", o0 + 48 * h, o0 + 48 * h + 16)), -2048.0, None, A.add)
        if t > 0:
            put_y()
            hints.append((len(ops) - 2, len(ops) - 1))
        ts(V("aU", 64, 512), ind(NBw, V("off", o0 + 20, o0 + 48)), -1.0, 4095.0, A.mult, A.add)

        def ya_gather(c):
            act(V("ya", 16 * c, 16 * c + 1024), ind(Ywin, V("aU", c, c + 64)))
            chain("a")

        def yc_gather(c):
            tt(V("mm", 16 * c, 16 * c + 1024), ind(V("Yb", 0, 4112), V("cU", c, c + 64)), V("ya", 16 * c, 16 * c + 1024), A.max)

        for n in range(2):
            mmul(bk(4 + n), V("RP%d" % (2 * n)), V("bV"), True, False)
            for h in range(2):
                mmul(bk(4 + n, 256 * h, 256 * h + 256), V("RP%d" % (2 * n + 1)), fV[h], False, h == 1)
            cp(V("PT", 512 * n, 512 * n + 512), bk(4 + n))
            chain("v")
        for j in range(16):
            bn = (0, 1, 2, 3, 6, 7)[j % 6]
            b = bk(bn)
            mmul(b, V("nI"), sS, True, False)
            if j < 2:
                mmul(b, V("BC%d" % j), V("bV"), False, False)
                for h in range(2):
                    mmul(bk(bn, 256 * h, 256 * h + 256), V("BC%d" % j), fV[h], False, h == 1)
            else:
                mmul(b, V("BT%d" % (j % 8)), V("PT", 512 * (j // 8), 512 * (j // 8) + 512), False, True)
            ac = V("acc" if j % 2 == 0 else "acd")
            act(ac if j < 2 else b, b, AF.Abs, bias=2048.0)
            chain("a")
            if j > 1:
                tt(bk(4) if j == 15 else ac, b, ac, A.min)
                chain("v")
        ya_gather(0)
        for h in range(2):
            tt(V("acc", 256 * h, 256 * h + 256), bk(4, 256 * h, 256 * h + 256), V("acc", 256 * h, 256 * h + 256), A.min)
            ts(V("cU", 256 * h, 256 * h + 256), V("acc", 256 * h, 256 * h + 256), -1.0, 4111.0, A.mult, A.add)
        mmul(bk(3, X0, 256), Ib, V(ZZ, X0, 256), True, True)

        def score(a, n, e, stop):
            c = 256 + a
            o = bk(5, a, a + n)
            if e == "v":
                x = 16 * (a - X0)
                tt(V("m15", a, a + n), bk(3, a, a + n), V("mm", 16 * c + 15, 16 * (c + n), 16), A.min)
                ms(V("mm", 16 * c + 15, 16 * (c + n), 16), 0.0)
                scan(V("mz", x, x + 16 * n), V(zr, 16 * a, 16 * (a + n)), V("mm", 16 * c, 16 * (c + n)))
                if t > 0 and stop:
                    put_ends()
                    hints.append((len(ops) - 2, len(ops) - 1))
                mmul(o, V("BL4096"), V(ZZ, a, a + n), False, False)
                mmul(o, V("BLn256"), V("m15", a, a + n), False, False)
                for k in range(15):
                    mmul(o, V("BLn256"), V("mz", x + k, x + 16 * n, 16), False, stop and k == 14)
                return
            for x in range(16 * a, 16 * (a + n), 512):
                bn = (0, 1, 2, 4, 7)[x // 512 % 5]
                for k in range(8):
                    msum(bk(bn, n * k, n * k + n), [(Ib, V(ZZ, a, a + n)), (V("nI"), V("mm", 16 * c + x // 64 % 16 + k, 16 * (c + n), 16))])
                act(V("EQ", x, x + 512), bk(bn), AF.Relu, scale=256.0)
            for k in range(16):
                mmul(o, V("BLK"), V("EQ", 16 * a + n * k, 16 * a + n * k + n), False, stop and k == 15)

        land = "FG" if t else "L0"
        for u, (a, n) in enumerate(PART):
            for c in range(a, a + n, 64):
                if c > 0:
                    ya_gather(c)
                yc_gather(c)
            x, y = 4096 + 16 * a, 4096 * t + 16 * a
            fold((rank - 1 - t) % N, [V(zr, x, x + 16 * n), V("mm", 16 * a, 16 * (a + n))], V(land, y, y + 16 * n),
                     "q%d_%d" % (t, u), "l%d_%d" % (t, u))
        if not last:
            spread_z(t + 1)
        mmul(bk(5, 0, 256), Ib, V("icolK"), True, False)
        mmul(bk(5, 0, 256), Ib, V("PENK"), False, False)
        for c in range(256, 512, 64):
            ya_gather(c)
        act(V("pc"), V("acc", 256, 512), AF.Relu, bias=4096.0 * 1024, scale=-1024.0)
        msum(bk(3, 256, 512), [(Ib, V("FS", 512, 768)), (V("B1n"), V("EWin", 5 * t, 4096, 16))])
        act(bk(3, 256, 512), bk(3, 256, 512), AF.Abs)
        act(V("pv"), bk(3, 256, 512), AF.Relu, bias=4096.0 * 1024, scale=-1024.0)
        mmul(bk(6, 0, 256), V("Is"), V("FS", 512, 768), True, False)
        for c in range(0, 256, 64):
            for k in range(16):
                mmul(bk(6, c, c + 64), V("ZS", 15 - k, 143 - k), V("ya", 4096 + 16 * c + k, 5120 + 16 * c, 16), False, False)
        mmul(bk(6, 0, 256), Ib, V("pc"), False, False)
        mmul(bk(6, 0, 256), Ib, V("pv"), False, True)
        act(V("CW", 0, 256), bk(6, 0, 256), bias=P["kb"], scale=16384.0)
        mmul(bk(5, 0, 256), V("BL4096"), V(ZZ, 0, 256), False, False)
        for a, n in PART:
            for k in range(16):
                mmul(bk(5, a, a + n), V("BLn256"), V(land, 4096 * t + 16 * a + k, 4096 * t + 16 * (a + n), 16), False, False)
        for m, (a, n, e) in enumerate(OWN):
            for c in range(a, a + n, 64):
                yc_gather(256 + c)
            score(a, n, e, m == len(OWN) - 1)
        scan(V("ke"), V("RB64"), bk(5, 0, 256))
        act(V("KA"), bk(5, 0, 256), AF.Abs, bias=KTOP, scale=-1.0)
        act(V("sg"), bk(5, 0, 256), AF.Sign, bias=P["bT%d" % t])
        le, ld, sc, k1, e16, kk = si(4), si(12), si(20), si(24), si(28), si(32)

        def whole(x, o):
            if SINT:
                return x
            cp(o, x)
            return o

        ts(le, whole(V("ke", 63, 256, 64), si(0)), 255, None, A.bitwise_and)
        ts(ou(oC, 8, 2), le, m0, P["c0"], A.mult, A.add)
        ts(ou(oC + 1, 7, 2), le, m1, P["c1"], A.mult, A.add)
        act(V("G1"), ind(V("CW"), ou(oC, 8)))
        ts(ou(oE, 4), le, 16.0, P["dE%d" % t], A.mult, A.add)
        scan(V("kd"), V("RB64"), V("KA"))
        ts(ld, whole(V("kd", 63, 256, 64), si(8)), 255, None, A.bitwise_and)
        ts(ou(oD, 4), ld, -16.0, P["dD%d" % t], A.mult, A.add)
        if last:
            ts(V("NM", 16, 18), V("si", 12, 14), -16.0, P["dC2"], A.mult, A.add)
            ts(V("NM", 18, 20), V("si", 14, 16), -16.0, P["s16"], A.mult, A.add)
        else:
            ts(V("NM", 16, 20), ld, -16.0, P["dC%d" % t], A.mult, A.add)
        act(V("Q3"), ind(V("EWin"), ou(oE, 8)))
        act(V("zg"), ind(Ywin, ou(oE, 4)))
        Qd = V("Q3", 64, 128)
        mmul(bk(1, 0, 192), Ib, V("PEN16", 0, 192), True, False)
        mmul(bk(1, 0, 128), V("BC1"), V("Q3"), False, False)
        mmul(bk(1, 128, 192), V("BC0"), Qd, False, True)
        transpose(V("G2"), V("G1"))
        scan(V("G3"), V("CAPS"), V("G2"))
        xi = whole(V("G3", 31, 128, 32), si(16))
        ts(sc, xi, 1023, None, A.bitwise_and)
        scan(V("k3"), V("RB16"), bk(1, 0, 192))
        cp(ou(oN, 4), sc)
        act(V("QS"), ind(V("codeT"), ou(oN, 4)))
        for sl, l, x in ((1, V("BC1"), ("Q3", 0)), (2, V("BC1"), ("Q3", 64)), (3, V("BC0"), ("Q3", 64)), (0, Ib, ("QS", 0))):
            for c in range(4):
                mmul(bk(2, 256 + 64 * c + 16 * sl, 272 + 64 * c + 16 * sl), l, V(x[0], x[1] + 16 * c, x[1] + 16 * c + 16), True, True)
        act(V("Q"), bk(2, 256, 512))
        name = lambda sl, c: col("k3", 64 * sl + 16 * c - 49) if sl else col("NM", c)
        ts(ou(oN + 4, 12), V("k3", 15, 192, 16), 512.0, None, A.add)
        ts(V("NM", 0, 4), sc, -512.0, None, A.add)
        act(V("NM", 4, 16), V("k3", 15, 192, 16))
        if SINT:
            ts(V("has"), xi, 1009.0 * 16384, None, A.is_lt)
        else:
            act(V("has"), V("G3", 31, 128, 32), AF.Relu, bias=1009.0 * 16384, scale=-1.0)
        for sl in range(4):
            act(V("EA", 64 * sl, 64 * sl + 64), V("Q", 192, 256), AF.Abs, bias=name(sl, 3), scale=-1.0)
        act(V("EQ", 0, 256), V("EA"), AF.Relu, bias=col("has", 3), scale=-BIG)
        msum(bk(0, 0, 256), [(Ib, V(ZZ, 0, 256)), (V("BLK"), V("sg"))])
        act(V("r1"), bk(0, 0, 256), AF.Relu, bias=86.0, scale=-1.0)
        act(V("Yb", 16 + 5 * t, 4112, 16), V("r1"), AF.Relu, bias=63.0, scale=-1.0)
        if last:
            act(col("Yb", 4111), col("ysave", 0))
        act(V("GN"), ind(NBw, ou(oN, 16)))
        act(V("emp"), V("GN", 0, 128), AF.Relu, bias=8192.0, scale=-8192.0)
        mmul(bk(4, 0, 256), Ib, V("C4"), True, False)
        for sl in range(4):
            mmul(bk(4, 64 * sl, 64 * sl + 64), V("BD"), Qd, False, sl == 3)
        tt(V("rd"), V("GN"), bk(4, 0, 256), A.not_equal)
        w = 128 if last else 256
        mmul(bk(3, 0, w), Ib, V("PC", 0, w), True, False)
        for sl in range(2):
            mmul(bk(3, 64 * sl, 64 * sl + 64), V("BD"), Qd, False, False)
        mmul(bk(3, 0, 128), V("FST"), V("emp"), False, last)
        if not last:
            act(V("GF"), ind(FCw, ou(oN, 16)))
            mmul(bk(3, 128, 256), V("FST"), V("emp"), False, False)
            for n in range(8):
                sl, c = divmod(n, 4)
                x = 64 * c + 16 * (1 - sl)
                mmul(bk(3, 128 + 16 * n, 144 + 16 * n), V("nI"), V("Q", x, x + 16), False, n == 7)
        act(V("KA", 0, w), bk(3, 0, w), AF.Relu)
        mmul(bk(1, 256, 256 + w), V("If"), V("KA", 0, w), True, False)
        if not last:
            mmul(bk(1, 384, 512), V("If"), V("GF", 0, 128), False, False)
        mmul(bk(1, 256, 384), V("If"), V("GN", 0, 128), False, True)
        act(V("MX", 0, w), bk(1, 256, 256 + w))
        parts = ((7, 0, 128), (5, 128, 256))

        def clash(l, e0, a, b, stop=False):
            for bn, p0, p1 in parts:
                if max(a, p0) < min(b, p1):
                    mmul(bk(bn, max(a, p0), min(b, p1)), l, V(e0[0], e0[1] + max(a, p0) - a, e0[1] + min(b, p1) - a), False, stop)

        for bn, p0, p1 in parts:
            mmul(bk(bn, p0, p1), Ib, V("PEN16", p0, p1), True, False)
        clash(Ib, ("CE", 0), 0, 256)
        for m in range(8):
            sl, c = divmod(m, 4)
            clash(V("BLK"), ("emp", 16 * m), 64 * c + 16 * sl, 64 * c + 16 * sl + 16)
        for sl in range(4):
            clash(V("TRn"), ("EQ", 64 * sl), 192, 256)
        for c in range(3):
            for sl in range(4):
                e0 = 256 * (1 + 4 * c + sl) + 64 * c
                ts(V("EQ", e0, e0 + 256 - 64 * c), V("Q", 64 * c, 256), name(sl, c), col("has", c), A.is_equal, A.min)
                clash(V("BLn8k"), ("EQ", e0 + 64), 64 * c + 64, 256)
                clash(V("TRn"), ("EQ", e0), 64 * c, 64 * c + 64, sl == 3 and c > 0)
        for bn, p0, p1 in parts:
            scan(V("kv", p0, p1), V("RB64", p0, p1), bk(bn, p0, p1))
        for c in range(4):
            ts(ou(oS + c, 20 - c, 4), V("NM", c, 20, 4), col("kv", 64 * c + 63), P["du%d" % c], A.subtract, A.min)
        ts(k1, xi, 10, 15, A.logical_shift_right, A.bitwise_and)
        ts(e16, le, 16.0, P["l64"], A.mult, A.add)
        tt(kk, k1, e16, A.add)
        cp(ou(oA, 4), kk)
        act(V("yh"), ind(V("ya", 4096, 8192), ou(oA, 4)))
        msum(bk(0, 256, 320), [(Ib, V("zg")), (Ib, V("yh"))])
        act(V("ys"), bk(0, 256, 320), bias=127.75, scale=0.5)

        def put_y():
            tt(ind(V("Yb", 16, 4176), ou(oS + 16, 4)), V("ys"), V("cm128"), A.add)

        def put(tab, old, new):
            for sl in (2, 3, 0, 1):
                x = V(old, 64 * sl, 64 * sl + 64) if sl > 1 else V("MX", new + 64 * sl, new + 64 * sl + 64)
                tt(ind(V(tab, 0, TAB), ou(oS + 4 * sl, 4)), x, V("rd", 64 * sl, 64 * sl + 64), A.mult)

        if last:
            for h in range(2):
                tt(ind(V("Yb", 16 + 2048 * h, 4176 + 2048 * h), ou(oS + 16 + 2 * h, 2)), V("ys", 32 * h, 32 * h + 32), V("cm128", 0, 32), A.add)
                dma("s", T.y1[:, 2048 * h:2048 * h + 2048], V("Yb", 16 + 2048 * h, 2064 + 2048 * h), 5.1 - 1.05 * h)
        else:
            put("FC", "GF", 128)
        put("NB", "GN", 0)
        if not last:
            act(V("GB", 4 * t, 4 * t + 4), V("kv", 63, 256, 64), AF.Relu, bias=513.0)
            msum(bk(6, 64, 65), [(V("BLK"), col("GB", c)) for c in range(4 * t + 4)])
            cnt = bk(6, 64, 65)
            if t == 0:
                act(P["a0"], cnt, AF.Relu, bias=-63.0)
                act(P["a1"], cnt, bias=P["bT0"], scale=-2048.0)
                act(P["bT1"], P["a0"], bias=P["a1"], scale=131072.0)
            else:
                act(P["a0"], cnt, AF.Sign, bias=-63.5)
                act(P["a1"], cnt, bias=P["th2"], scale=-2048.0)
                act(P["a2"], cnt, AF.Relu, bias=-127.0)
                act(P["a3"], P["a0"], bias=P["a1"], scale=65536.0)
                act(P["bT2"], P["a2"], bias=P["a3"], scale=131072.0)
        for n, (o, f) in enumerate(((oN, 1.0), (oN + 4, -1.0), (oN, -1024.0))):
            act(V("nsv", 64 * n, 64 * n + 64), ind(V("numT"), ou(o, 4)), scale=f)
        msum(bk(6, 128, 192), [(V("If"), V("nsv", 0, 64)), (V("If"), V("nsv", 64, 128))])
        act(V("mn"), bk(6, 128, 192), AF.Relu, scale=1023.0)
        msum(bk(6, 0, 64), [(V("If"), V("nsv", 128, 192)), (V("If"), V("nsv", 64, 128)), (V("If"), V("mn"))])
        act(V("en"), bk(6, 0, 64), scale=-1.0)

    for h in range(2):
        cp(ind(V("EF", 2048 * h, 2048 * h + TAB), ou(oS + 16 + 2 * h, 2)), V("en", 32 * h, 32 * h + 32))
    for (x0, x1, a0, a1, st) in SEG:
        if st == 1:
            ts(V("neo", x0, x1), V("NB", a0, a1, st), -1.0, 4095.0, A.mult, A.add)
        else:
            act(V("neo", x0, x1), V("NB", a0, a1, st), bias=4095.0, scale=-1.0)
    dma("a", T.ends1[:], V("EF", 0, 4096, 1, 0, 128, 16), 3.1)
    dma("s", T.ne1[:], V("neo"), 2.8)

    def meet(x, y, wide):
        if x[0] != y[0]:
            return False
        if x[5] <= y[4] or y[5] <= x[4]:
            return False
        if x[6] == y[6] and x[6] > 1 and x[4] % x[6] != y[4] % y[6]:
            return False
        s = SIZE[SCRATCH[x[0]][2]]
        a0, a1, b0, b1 = x[1] * s, x[2] * s, y[1] * s, y[2] * s
        if wide:
            a0, b0, a1, b1 = a0 // 16 * 16, b0 // 16 * 16, -(-a1 // 16) * 16, -(-b1 // 16) * 16
        if not (a0 < b1 and b0 < a1):
            return False
        if wide or (x[3] == 1 and y[3] == 1):
            return True
        return len(set(range(x[1], x[2], x[3])) & set(range(y[1], y[2], y[3]))) > 0

    touch = {}
    lastdma = {}
    lastsend = [None]
    for n, op in enumerate(ops):
        q = op["q"]
        asy = op["dma"] or q is None or op["left"] is not None
        sync, after = set(), set(a for a, b in hints if b == n)
        for w, v in [(False, v) for v in op["rd"]] + [(True, v) for v in op["wr"]]:
            psum = SCRATCH[v[0]][0] == "psum"
            for (m, w2, v2) in touch.get(v[0], []):
                o2 = ops[m]
                asy2 = o2["dma"] or o2["q"] is None or o2["left"] is not None
                same = o2["q"] == q and not asy and not asy2
                if psum and not same:
                    sync.add(m)
                elif psum and q == "p":
                    if op.get("inner", -1) != o2.get("inner", -2):
                        after.add(m)
                elif (w or w2) and meet(v, v2, asy or asy2):
                    sync.add(m)
        if (op["dma"] and q != "g") or op["ext"] == "send":
            if q in lastdma:
                after.add(lastdma[q])
            lastdma[q] = n
        if op["ext"] == "send":
            lastsend[0] = n
        if q is None:
            after.add(lastsend[0])
        op["sync"], op["after"] = sync, after - sync
        for v in op["rd"]:
            touch.setdefault(v[0], []).append((n, False, v))
        for v in op["wr"]:
            touch.setdefault(v[0], []).append((n, True, v))
    succ = [[] for op in ops]
    for n, op in enumerate(ops):
        for m in op["sync"]:
            succ[m].append((n, True))
        for m in op["after"]:
            succ[m].append((n, False))
    prio = [0.0] * len(ops)
    for n in range(len(ops) - 1, -1, -1):
        op = ops[n]
        prio[n] = op["early"] + op["cost"] + max([0.0] + [prio[m] + (op["lat"] + WAKE if sy or ops[m]["q"] is None else 0.0) for m, sy in succ[n]] + [op["lat"]])
    left = [len(op["sync"]) + len(op["after"]) for op in ops]
    rdy = [0.0] * len(ops)
    free = {q: 0.0 for q in eng}
    cand = [n for n in range(len(ops)) if left[n] == 0]
    order = []
    while cand:
        st = {n: max(rdy[n], free.get(ops[n]["q"], 0.0)) for n in cand}
        n0 = min(cand, key=lambda n: (st[n], -prio[n], n))
        q = ops[n0]["q"]
        n = max([m for m in cand if ops[m]["q"] == q and st[m] <= st[n0] + LOOK * min(1.0, ops[n0]["cost"])], key=lambda m: (prio[m], -m))
        op = ops[n]
        cand.remove(n)
        order.append(n)
        end = st[n] + op["cost"]
        if q is not None:
            free[q] = end
        for m, sy in succ[n]:
            rdy[m] = max(rdy[m], end + (op["lat"] + WAKE if sy or ops[m]["q"] is None else 0.0))
            left[m] -= 1
            if left[m] == 0:
                cand.append(m)
    fw = [[] for op in ops]
    bw = [[] for op in ops]
    for n, op in enumerate(ops):
        for m, sy in succ[n]:
            lag = op["lat"] + WAKE if sy or ops[m]["q"] is None else 0.0
            fw[m].append((n, lag))
            bw[n].append((m, lag))

    def place(seqn, pre, back):
        end = [0.0] * len(ops)
        busy = {q: [] for q in eng}
        for n in seqn:
            op = ops[n]
            r = max([op["lat"] if back else 0.0] + [end[m] + lag for m, lag in pre[n]])
            if op["q"] is not None:
                iv = busy[op["q"]]
                k = len(iv)
                while k > 0 and iv[k - 1][1] > r:
                    k -= 1
                while k < len(iv) and iv[k][0] < r + op["cost"] - 1e-9:
                    r = max(r, iv[k][1])
                    k += 1
                iv.insert(k, (r, r + op["cost"]))
            end[n] = r + op["cost"]
        return end

    if "order" not in PLAN:
        best = None
        rng = np.random.default_rng(SEED)
        for it in range(ROUNDS + 1):
            at = {n: k for k, n in enumerate(order)}
            end = place(order, fw, False)
            order = sorted(order, key=lambda n: (end[n] - ops[n]["cost"], at[n]))
            span = max(end[n] + ops[n]["lat"] for n in order)
            PLAN.setdefault("spans", []).append(span)
            if best is None or span < best[0]:
                best = (span, order, end)
            order, end = best[1], best[2]
            at = {n: k for k, n in enumerate(order)}
            back = sorted(order, key=lambda n: (-end[n], -at[n]))
            keep = [op["cost"] for op in ops]
            if it > 0:
                for op, x in zip(ops, rng.random(len(ops)).tolist()):
                    op["cost"] = op["cost"] * (1.0 + JIT * (2 * x - 1))
            end = place(back, bw, True)
            for op, x in zip(ops, keep):
                op["cost"] = x
            at = {n: k for k, n in enumerate(back)}
            order = sorted(back, key=lambda n: (-end[n], -at[n]))
        PLAN["order"] = best[1]
    order = PLAN["order"]
    known = {q: {} for q in eng}
    seq = {q: 0 for q in eng}
    ndma = [0]
    for pos, n in enumerate(order):
        op = ops[n]
        q = op["q"]
        op["pos"] = pos
        if op["dma"]:
            op["key"] = "dm%d" % ndma[0]
            op["idx"] = 16
            ndma[0] += 1
        elif q is None:
            op["key"], op["idx"] = op["ext"]
        elif op["left"]:
            op["key"], op["idx"] = op["left"]
        else:
            seq[q] += 1
            op["key"], op["idx"] = q, seq[q]
        op["waits"] = []
        if q is not None:
            for m in sorted(op["sync"], key=lambda m: -ops[m]["pos"]):
                o2 = ops[m]
                if known[q].get(o2["key"], 0) < o2["idx"]:
                    op["waits"].append(m)
                    o2["need"] = True
                    known[q][o2["key"]] = o2["idx"]
                    for k2, v2 in o2["clock"].items():
                        if known[q].get(k2, 0) < v2:
                            known[q][k2] = v2
            op["clock"] = dict(known[q])
        else:
            op["clock"] = {}
    cnt = {q: 0 for q in QSEM}
    tail = []
    for n in order:
        op = ops[n]
        q = op["q"]
        if q is None:
            op["sem"], op["val"] = op["ext"]
            continue
        for m in op["waits"]:
            eng[q].wait_ge(T.sem[ops[m]["sem"]], ops[m]["val"])
        ins = op["fn"]()
        if op["left"]:
            op["sem"], op["val"] = op["left"]
            if not op.get("need"):
                tail.append(op)
        elif op["dma"]:
            op["sem"], op["val"] = op["key"], 16
            ins.then_inc(T.sem[op["sem"]], 16)
            if not op.get("need"):
                tail.append(op)
        elif op.get("need"):
            cnt[q] += 1
            op["sem"], op["val"] = QSEM[q], cnt[q]
            ins.then_inc(T.sem[op["sem"]], 1)
    g.wait_ge(T.sem.lsem, sent[0])
    for op in tail:
        eng[op["q"]].wait_ge(T.sem[op["sem"]], op["val"])
